import numpy as np
import ml_dtypes


def mxq(x, axis, fmt="e4m3"):
    dtype, down = {"e4m3": (ml_dtypes.float8_e4m3fn, 7), "e5m2": (ml_dtypes.float8_e5m2, 14)}[fmt]
    v = np.moveaxis(np.asarray(x, np.float32).astype(ml_dtypes.bfloat16).astype(np.float64), axis, -1)
    blocks = v.reshape(v.shape[:-1] + (-1, 32))
    amax = np.abs(blocks).max(-1, keepdims=True)
    byte = np.maximum(np.where(amax > 0, np.frexp(amax)[1] - 1 + 127, 0) - down, 1)
    scale = np.exp2(byte - 127.0)
    codes = (blocks / scale).astype(np.float32).astype(dtype).astype(np.float64)
    return np.moveaxis((codes * scale).reshape(v.shape), -1, axis)


WIDE = False


def mx_kscale(k):
    if not WIDE:
        return np.ones(k)
    levels = np.array([10, -10, 5, -5, 0])
    if k % 512:
        return np.exp2(np.random.permutation(np.resize(levels, k // 32))).repeat(32)
    a = np.empty((k // 512, 16))
    for p in range(k // 512):
        a[p, :8] = np.random.permutation(np.resize(levels, 8))
        for g in range(8):
            far = levels[np.abs(levels - a[p, g]) >= 10]
            a[p, g + 8] = far[np.random.randint(len(far))]
    return np.exp2(a.ravel()).repeat(32)


def f64(x):
    return np.asarray(x).astype(np.float64)


def striped(idx):
    return np.tile(idx.reshape(-1, 16).T, (8, 1)).astype(np.uint16)


def unstriped(offs):
    return offs[:16].T.reshape(-1).astype(np.int64)


E2M1 = np.array([0.0, 0.5, 1.0, 1.5, 2.0, 3.0, 4.0, 6.0, -0.0, -0.5, -1.0, -1.5, -2.0, -3.0, -4.0, -6.0])


def pack_weight(w, fmt):
    k, n = w.shape
    w = f64(np.asarray(w, np.float32).astype(ml_dtypes.bfloat16)).reshape(k // 32, 32, n)
    amax = np.abs(w).max(1)
    if fmt == "e4m3":
        byte = np.frexp(amax)[1] - 1 + 127 - 7
    else:
        mant, ex = np.frexp(amax / 6.0)
        byte = np.where(mant > 0.5, ex, ex - 1) + 127
    byte = np.clip(np.where(amax > 0, byte, 1), 1, 254)
    scaled = (w * np.exp2(127.0 - byte)[:, None, :]).reshape(k, n).astype(np.float32)
    by_word = np.ascontiguousarray(scaled.reshape(k // 512, 128, 4, n).transpose(0, 1, 3, 2))
    if fmt == "e4m3":
        words = by_word.astype(ml_dtypes.float8_e4m3fn).view(np.uint8)
    else:
        c = by_word.astype(ml_dtypes.float4_e2m1fn).view(np.uint8) & 0xF
        words = (c[..., 0::2] | (c[..., 1::2] << 4)).reshape(k // 512, 128, 2 * n)
    return np.ascontiguousarray(words), np.ascontiguousarray(byte.astype(np.uint8).reshape(k // 512, 16, n))


def unpack_weight(words, scales, fmt):
    g, _, n = scales.shape
    words = np.ascontiguousarray(words).reshape(g, 128, n, -1)
    if fmt == "e4m3":
        vals = words.view(ml_dtypes.float8_e4m3fn).astype(np.float64)
    else:
        nib = np.empty((g, 128, n, 4), np.uint8)
        nib[..., 0::2] = words & 0xF
        nib[..., 1::2] = words >> 4
        vals = E2M1[nib]
    vals = vals * np.repeat(np.exp2(scales.astype(np.float64) - 127.0), 8, axis=1)[..., None]
    return vals.transpose(0, 1, 3, 2).reshape(g * 512, n)


def gelu(v):
    return 0.5 * v * (1.0 + np.tanh(np.sqrt(2.0 / np.pi) * (v + 0.044715 * v**3)))


K, T, H, N, S, T2, P = 1024, 4096, 512, 384, 1024, 2048, 1024

def setup_inputs():
    n = np.random.standard_normal
    s = mx_kscale(K)[:, None]
    u = mx_kscale(H)[:, None]
    tab_words, tab_scales = pack_weight(n((K, T)) * s, "e4m3")
    w2_words, w2_scales = pack_weight(1.5 * n((H, N)) / np.sqrt(H) / u, "e2m1")
    return {
        "tab_words": tab_words, "tab_scales": tab_scales,
        "offs": striped(np.random.permutation(T)[:S]),
        "w1": (n((K, H)) / np.sqrt(K) / s).astype(np.float32),
        "gain": (np.exp(0.3 * n(H)) * u[:, 0]).astype(np.float32),
        "wgs": np.exp(0.3 * n((128, S))).astype(np.float32),
        "offs2": striped(np.random.permutation(T2)[:S]),
        "limit": ((0.5 + n((H, T2))) * u).astype(np.float32),
        "w2_words": w2_words, "w2_scales": w2_scales,
        "w3": (1.5 * n((H, N)) / np.sqrt(H) / u).astype(np.float32),
        "offs3": striped(np.random.permutation(T2)[:P]),
        "bias": (0.5 * n(N)).astype(np.float32),
        "wgo": np.exp(0.3 * n((128, P))).astype(np.float32),
        "offs4": striped(np.random.permutation(T2)[:P]),
    }

def reference(tab_words, tab_scales, offs, w1, gain, wgs, offs2, limit, w2_words, w2_scales, w3, offs3, bias, wgo, offs4):
    v = unpack_weight(tab_words, tab_scales, "e4m3")[:, unstriped(offs)]
    a = mxq(f64(w1), 0, "e4m3").T @ v
    h = f64(gain)[:, None] / (1 + a * a)
    page = np.zeros((H, T2))
    page[:, unstriped(offs2)] = np.tile(f64(wgs), (H // 128, 1)) * h
    z = mxq(np.minimum(page, f64(limit)), 0, "e4m3")
    y2 = unpack_weight(w2_words, w2_scales, "e2m1").T @ z
    y3 = mxq(f64(w3), 0, "e4m3").T @ z
    y = np.maximum(y2, y3)
    x = y[:, unstriped(offs3)] - f64(bias)[:, None]
    out = np.zeros((N, T2))
    out[:, unstriped(offs4)] = np.tile(f64(wgo), (N // 128, 1)) * x
    return out

@@ -1,0 +1,245 @@
+from contextlib import ExitStack
+
+import concourse.mybir as mybir
+
+K, T, H, N, S, T2 = 1024, 4096, 512, 384, 1024, 2048
+FLOPS = 2 * K * H * S + 2 * 2 * H * N * T2
+
+F32 = mybir.dt.float32
+BF16 = mybir.dt.bfloat16
+I32 = mybir.dt.int32
+U32 = mybir.dt.uint32
+U16 = mybir.dt.uint16
+U8 = mybir.dt.uint8
+FP8X4 = mybir.dt.float8_e4m3fn_x4
+FP4X4 = mybir.dt.float4_e2m1fn_x4
+ALU = mybir.AluOpType
+ACT = mybir.ActivationFunctionType
+
+P = 128
+PACK = 4
+BANK = 512
+PASSES = K // (P * PACK)
+HALVES = S // BANK
+CHUNKS = T2 // BANK
+BLOCKS = N // P
+QUADS = 4
+LIST_COLS = S // 16
+
+
+def tile_list_propellant_gauge_fusion_kernel(
+    tc, tab_words, tab_scales, offs, w1, gain, wgs, offs2, limit, w2_words, w2_scales, w3, offs3, bias, wgo, offs4, out
+):
+    nc = tc.nc
+    with ExitStack() as ctx:
+        lists = ctx.enter_context(tc.tile_pool(name="lists", bufs=1))
+        sb = ctx.enter_context(tc.tile_pool(name="sb", bufs=1))
+        psum = ctx.enter_context(tc.psum_pool(name="psum", bufs=8))
+
+        def tile(shape, dtype, name, tag=None):
+            return sb.tile(shape, dtype, name=name, tag=tag or name, align_bytes=64)
+
+        def load_list(src, name):
+            held = lists.tile([P, LIST_COLS], U16, name=name)
+            nc.sync.dma_start(held[:], src)
+            return held
+
+        tab_sc = tile([P, T], U8, "tab_sc")
+        nc.vector.memset(tab_sc[:].bitcast(I32), 0)
+        idx1 = load_list(offs, "idx1")
+        tab = [tile([P, T], U32, "tab%d" % a) for a in range(PASSES)]
+        w1_raw = [tile([P, PACK, H], F32, "w1_raw%d" % a) for a in range(PASSES)]
+
+        def load_tab(a):
+            nc.sync.dma_start(tab[a][:].bitcast(I32), tab_words[a].rearrange("p t i -> p (t i)").bitcast(I32))
+
+        load_tab(0)
+        for q in range(QUADS):
+            nc.sync.dma_start(
+                tab_sc[32 * q : 32 * q + 4 * PASSES, :].bitcast(I32),
+                tab_scales[:, 4 * q : 4 * q + 4, :].bitcast(I32),
+            )
+        for a in range(PASSES):
+            nc.sync.dma_start(w1_raw[a][:], w1[512 * a : 512 * (a + 1), :].rearrange("(p j) c -> p j c", j=PACK))
+        load_tab(1)
+        idx2 = load_list(offs2, "idx2")
+        wgs_rows = wgs.rearrange("(q t) j -> q t j", t=PACK)
+        wgs_sb = tile([P, PACK, S], F32, "wgs_sb")
+        for t0, t1 in ((0, 1), (1, PACK)):
+            for q in range(QUADS):
+                nc.sync.dma_start(wgs_sb[32 * q : 32 * (q + 1), t0:t1, :], wgs_rows[:, t0:t1, :])
+        gain_sb = tile([P, PACK], F32, "gain_sb")
+        nc.sync.dma_start(gain_sb[:], gain.rearrange("(p t) -> p t", t=PACK))
+        limit_rows = limit.rearrange("(p t) c -> t p c", t=PACK)
+        lim = [tile([P, T2], F32, "lim%d" % t) for t in range(PACK)]
+        for t in range(PACK):
+            nc.sync.dma_start(lim[t][:], limit_rows[t])
+
+        pages = [tile([P, T2], F32, "page%d" % t) for t in range(PACK)]
+        for t in range(PACK):
+            nc.vector.memset(pages[t][:], 0.0)
+        w2_sc = tile([P, N], U8, "w2_sc")
+        nc.gpsimd.memset(w2_sc[:].bitcast(I32), 0)
+        budget = [tile([P, T2], F32, "budget%d" % b) for b in range(BLOCKS)]
+        for b in range(BLOCKS):
+            nc.gpsimd.memset(budget[b][:], 0.0)
+
+        got_sc = tile([P, S], U8, "got_sc")
+        got = [tile([P, S], U32, "got%d" % a) for a in range(PASSES)]
+        nc.vector.tensor_copy(got[0][:], tab[0][:].indirect(idx1[:]))
+        nc.vector.tensor_copy(got_sc[:], tab_sc[:].indirect(idx1[:]))
+        w1_codes = []
+        w1_sc = []
+        for a in range(PASSES):
+            grouped = tile([P, PACK, P, PACK], BF16, "w1_grouped%d" % a)
+            dst = grouped[:].rearrange("p t m j -> p m j t")
+            src = w1_raw[a][:].rearrange("p j (m t) -> p m j t", t=PACK)
+            if a == 0:
+                nc.scalar.copy(dst, src)
+            else:
+                nc.vector.tensor_copy(dst, src)
+            codes = tile([P, H], U32, "w1_codes%d" % a)
+            sc = tile([P, H], U8, "w1_sc%d" % a)
+            nc.vector.quantize_mx(codes[:].bitcast(FP8X4), sc[:], grouped[:].rearrange("p t m j -> p (t m j)"))
+            w1_codes.append(codes)
+            w1_sc.append(sc)
+        half_cols = LIST_COLS // HALVES
+        for u in range(HALVES):
+            nc.vector.tensor_copy(
+                got[1][:, u * BANK : (u + 1) * BANK], tab[1][:].indirect(idx1[:, u * half_cols : (u + 1) * half_cols])
+            )
+
+        w3_raw = tile([P, PACK, N], F32, "w3_raw", tag="w1_raw0")
+        nc.sync.dma_start(w3_raw[:], w3.rearrange("(p j) c -> p j c", j=PACK))
+        w2_codes = tile([P, 2 * N], U8, "w2_codes")
+        nc.sync.dma_start(w2_codes[:].bitcast(I32), w2_words[0].bitcast(I32))
+        for q in range(QUADS):
+            nc.sync.dma_start(w2_sc[32 * q : 32 * q + 4, :].bitcast(I32), w2_scales[0, 4 * q : 4 * q + 4, :].bitcast(I32))
+        bias_sb = tile([P, BLOCKS], F32, "bias_sb")
+        with nc.allow_non_contiguous_dma(reason="one bias value for each partition and block"):
+            nc.sync.dma_start(bias_sb[:], bias.rearrange("(b p) -> p b", p=P))
+        idx3 = load_list(offs3, "idx3")
+        idx4 = load_list(offs4, "idx4")
+        wgo_sb = tile([P, S], F32, "wgo_sb")
+        nc.sync.dma_start(wgo_sb[:], wgo)
+
+        bell = [tile([P, S], F32, "bell%d" % t) for t in range(PACK)]
+        for t in range(PACK):
+            for u in range(HALVES):
+                cols = slice(u * BANK, (u + 1) * BANK)
+                acc = psum.tile([P, BANK], F32, name="acc", tag="bank")
+                for a in range(PASSES):
+                    nc.tensor.matmul_mx(
+                        acc[:],
+                        lhsT=w1_codes[a][:, t * P : (t + 1) * P].bitcast(FP8X4),
+                        lhsT_scale=w1_sc[a][:, t * P : (t + 1) * P],
+                        rhs=got[a][:, cols].bitcast(FP8X4),
+                        rhs_scale=got_sc[4 * a : P, cols],
+                        start=(a == 0),
+                        stop=(a == PASSES - 1),
+                    )
+                nc.scalar.activation(bell[t][:, cols], acc[:], ACT.Square)
+                nc.scalar.activation(bell[t][:, cols], bell[t][:, cols], ACT.Abs_reciprocal_sqrt, bias=1.0)
+                nc.scalar.activation(bell[t][:, cols], bell[t][:, cols], ACT.Square)
+                if t == 0:
+                    nc.vector.tensor_tensor(
+                        pages[t][:].indirect(idx2[:, u * half_cols : (u + 1) * half_cols]),
+                        bell[t][:, cols], wgs_sb[:, t, cols], ALU.mult,
+                    )
+            if t > 0:
+                nc.vector.tensor_tensor(pages[t][:].indirect(idx2[:]), bell[t][:], wgs_sb[:, t, :], ALU.mult)
+
+        early = PACK - 1
+        planes = [tile([P, PACK, BANK], BF16, "planes%d" % c) for c in range(CHUNKS)]
+        lim16 = [
+            tile([P, early, BANK], BF16, "lim16_%d" % c, tag=("w1_grouped%d" % c if c < PASSES else None))
+            for c in range(CHUNKS)
+        ]
+
+        def round_page(t):
+            for c in range(CHUNKS):
+                nc.scalar.activation(
+                    planes[c][:, t, :], pages[t][:, c * BANK : (c + 1) * BANK], ACT.Copy, scale=gain_sb[:, t : t + 1]
+                )
+
+        def round_limit(t):
+            for c in range(CHUNKS):
+                nc.scalar.copy(lim16[c][:, t, :], lim[t][:, c * BANK : (c + 1) * BANK])
+
+        round_page(0)
+        round_limit(0)
+        round_limit(1)
+        round_page(1)
+        round_limit(2)
+        w3_grouped = tile([P, N, PACK], BF16, "w3_grouped")
+        nc.scalar.copy(
+            w3_grouped[:].rearrange("p (c i) j -> p c j i", i=4), w3_raw[:].rearrange("p j (c i) -> p c j i", i=4)
+        )
+        round_page(2)
+        w3_codes = tile([P, N], U32, "w3_codes")
+        w3_sc = tile([P, N], U8, "w3_sc")
+        w3_flat = w3_grouped[:].rearrange("p c j -> p (c j)")
+        for c0, c1 in ((0, 256), (256, N)):
+            nc.vector.quantize_mx(w3_codes[:, c0:c1].bitcast(FP8X4), w3_sc[:, c0:c1], w3_flat[:, PACK * c0 : PACK * c1])
+        neg_bias = tile([P, BLOCKS], F32, "neg_bias")
+        nc.vector.tensor_scalar(neg_bias[:], bias_sb[:], -1.0, None, ALU.mult)
+
+        z_grouped = tile([P, CHUNKS, BANK, PACK], BF16, "z_grouped", tag="wgs_sb")
+        z_codes = tile([P, T2], U32, "z_codes", tag="w1_raw1")
+        z_sc = [tile([P, BANK], U8, "z_sc%d" % c) for c in range(CHUNKS)]
+        score = [tile([P, T2], F32, "score%d" % b, tag="lim%d" % b) for b in range(BLOCKS)]
+
+        def clip(c):
+            cols = slice(c * BANK, (c + 1) * BANK)
+            nc.vector.tensor_tensor(planes[c][:, 0:early, :], planes[c][:, 0:early, :], lim16[c][:], ALU.min)
+            nc.vector.scalar_tensor_tensor(
+                planes[c][:, early, :], pages[early][:, cols], gain_sb[:, early : early + 1], lim[early][:, cols],
+                ALU.mult, ALU.min,
+            )
+
+        def group(c):
+            dst = z_grouped[:, c].rearrange("p (c i) t -> p c t i", i=4)
+            src = planes[c][:].rearrange("p t (c i) -> p c t i", i=4)
+            if c < CHUNKS - 1:
+                nc.scalar.copy(dst, src)
+            else:
+                nc.vector.tensor_copy(dst, src)
+
+        def quantize(c):
+            nc.vector.quantize_mx(
+                z_codes[:, c * BANK : (c + 1) * BANK].bitcast(FP8X4), z_sc[c][:],
+                z_grouped[:, c].rearrange("p c t -> p (c t)"),
+            )
+
+        def scores(b, c):
+            cols = slice(c * BANK, (c + 1) * BANK)
+            y2 = psum.tile([P, BANK], F32, name="y2", tag="bank")
+            nc.tensor.matmul_mx(
+                y2[:], lhsT=w2_codes[:, 2 * P * b : 2 * P * (b + 1)].bitcast(FP4X4), lhsT_scale=w2_sc[:, P * b : P * (b + 1)],
+                rhs=z_codes[:, cols].bitcast(FP8X4), rhs_scale=z_sc[c][:], start=True, stop=True,
+            )
+            y3 = psum.tile([P, BANK], F32, name="y3", tag="bank")
+            nc.tensor.matmul_mx(
+                y3[:], lhsT=w3_codes[:, P * b : P * (b + 1)].bitcast(FP8X4), lhsT_scale=w3_sc[:, P * b : P * (b + 1)],
+                rhs=z_codes[:, cols].bitcast(FP8X4), rhs_scale=z_sc[c][:], start=True, stop=True,
+            )
+            nc.scalar.activation(score[b][:, cols], y2[:], ACT.Identity, bias=neg_bias[:, b : b + 1])
+            nc.vector.scalar_tensor_tensor(
+                score[b][:, cols], y3[:], bias_sb[:, b : b + 1], score[b][:, cols], ALU.subtract, ALU.max
+            )
+
+        for c in range(CHUNKS):
+            clip(c)
+            group(c)
+        for c in (0, CHUNKS - 1, 1, 2):
+            quantize(c)
+            scores(0, c)
+
+        for b in range(BLOCKS):
+            if b > 0:
+                for c in range(CHUNKS):
+                    scores(b, c)
+            picked = tile([P, S], F32, "picked%d" % b, tag="bell%d" % b)
+            nc.vector.tensor_copy(picked[:], score[b][:].indirect(idx3[:]))
+            nc.vector.tensor_tensor(budget[b][:].indirect(idx4[:]), picked[:], wgo_sb[:], ALU.mult)
+            nc.sync.dma_start(out[b * P : (b + 1) * P, :], budget[b][:])

@@ -46,6 +46,9 @@ def tile_list_propellant_gauge_fusion_kernel(
 
         tab_sc = tile([P, T], U8, "tab_sc")
         nc.vector.memset(tab_sc[:].bitcast(I32), 0)
+        warm = tile([P, 2], F32, "warm")
+        nc.vector.memset(warm[:, 0:1], 1.0)
+        nc.scalar.activation(warm[:, 1:2], warm[:, 0:1], ACT.Abs_reciprocal_sqrt)
         idx1 = load_list(offs, "idx1")
         tab = [tile([P, T], U32, "tab%d" % a) for a in range(PASSES)]
         w1_raw = [tile([P, PACK, H], F32, "w1_raw%d" % a) for a in range(PASSES)]
@@ -55,7 +58,7 @@ def tile_list_propellant_gauge_fusion_kernel(
 
         load_tab(0)
         for q in range(QUADS):
-            nc.sync.dma_start(
+            nc.gpsimd.dma_start(
                 tab_sc[32 * q : 32 * q + 4 * PASSES, :].bitcast(I32),
                 tab_scales[:, 4 * q : 4 * q + 4, :].bitcast(I32),
             )
@@ -77,12 +80,9 @@ def tile_list_propellant_gauge_fusion_kernel(
 
         pages = [tile([P, T2], F32, "page%d" % t) for t in range(PACK)]
         for t in range(PACK):
-            nc.vector.memset(pages[t][:], 0.0)
+            (nc.vector if t < 2 else nc.gpsimd).memset(pages[t][:], 0.0)
         w2_sc = tile([P, N], U8, "w2_sc")
-        nc.gpsimd.memset(w2_sc[:].bitcast(I32), 0)
-        budget = [tile([P, T2], F32, "budget%d" % b) for b in range(BLOCKS)]
-        for b in range(BLOCKS):
-            nc.gpsimd.memset(budget[b][:], 0.0)
+        nc.vector.memset(w2_sc[:].bitcast(I32), 0)
 
         got_sc = tile([P, S], U8, "got_sc")
         got = [tile([P, S], U32, "got%d" % a) for a in range(PASSES)]
@@ -94,10 +94,7 @@ def tile_list_propellant_gauge_fusion_kernel(
             grouped = tile([P, PACK, P, PACK], BF16, "w1_grouped%d" % a)
             dst = grouped[:].rearrange("p t m j -> p m j t")
             src = w1_raw[a][:].rearrange("p j (m t) -> p m j t", t=PACK)
-            if a == 0:
-                nc.scalar.copy(dst, src)
-            else:
-                nc.vector.tensor_copy(dst, src)
+            nc.scalar.copy(dst, src)
             codes = tile([P, H], U32, "w1_codes%d" % a)
             sc = tile([P, H], U8, "w1_sc%d" % a)
             nc.vector.quantize_mx(codes[:].bitcast(FP8X4), sc[:], grouped[:].rearrange("p t m j -> p (t m j)"))
@@ -109,7 +106,11 @@ def tile_list_propellant_gauge_fusion_kernel(
                 got[1][:, u * BANK : (u + 1) * BANK], tab[1][:].indirect(idx1[:, u * half_cols : (u + 1) * half_cols])
             )
 
-        w3_raw = tile([P, PACK, N], F32, "w3_raw", tag="w1_raw0")
+        budget = [tile([P, T2], F32, "budget%d" % b, tag=tag) for b, tag in enumerate(("tab0", "w1_raw0", "tab1"))]
+        for b in range(BLOCKS):
+            nc.gpsimd.memset(budget[b][:], 0.0)
+
+        w3_raw = tile([P, PACK, N], F32, "w3_raw", tag="w1_raw1")
         nc.sync.dma_start(w3_raw[:], w3.rearrange("(p j) c -> p j c", j=PACK))
         w2_codes = tile([P, 2 * N], U8, "w2_codes")
         nc.sync.dma_start(w2_codes[:].bitcast(I32), w2_words[0].bitcast(I32))
@@ -138,23 +139,33 @@ def tile_list_propellant_gauge_fusion_kernel(
                         start=(a == 0),
                         stop=(a == PASSES - 1),
                     )
-                nc.scalar.activation(bell[t][:, cols], acc[:], ACT.Square)
-                nc.scalar.activation(bell[t][:, cols], bell[t][:, cols], ACT.Abs_reciprocal_sqrt, bias=1.0)
-                nc.scalar.activation(bell[t][:, cols], bell[t][:, cols], ACT.Square)
-                if t == 0:
-                    nc.vector.tensor_tensor(
-                        pages[t][:].indirect(idx2[:, u * half_cols : (u + 1) * half_cols]),
-                        bell[t][:, cols], wgs_sb[:, t, cols], ALU.mult,
-                    )
+                if t >= 2:
+                    stem = "lim16_%d" if t == 2 else "planes%d"
+                    square = tile([P, BANK], F32, "square%d_%d" % (t, u), tag=stem % (2 * u))
+                    root = tile([P, BANK], F32, "root%d_%d" % (t, u), tag=stem % (2 * u + 1))
+                    nc.scalar.activation(square[:], acc[:], ACT.Square)
+                    nc.scalar.activation(root[:], square[:], ACT.Abs_reciprocal_sqrt, bias=1.0)
+                    nc.scalar.activation(bell[t][:, cols], root[:], ACT.Square)
+                    continue
+                pieces = 2 if (t, u) == (0, 0) else 1
+                width = BANK // pieces
+                for v in range(pieces):
+                    j0 = u * BANK + v * width
+                    part = bell[t][:, j0 : j0 + width]
+                    nc.scalar.activation(part, acc[:, v * width : (v + 1) * width], ACT.Square)
+                    nc.scalar.activation(part, part, ACT.Abs_reciprocal_sqrt, bias=1.0)
+                    nc.scalar.activation(part, part, ACT.Square)
+                    if t == 0:
+                        nc.vector.tensor_tensor(
+                            pages[t][:].indirect(idx2[:, j0 // 16 : (j0 + width) // 16]),
+                            part, wgs_sb[:, t, j0 : j0 + width], ALU.mult,
+                        )
             if t > 0:
                 nc.vector.tensor_tensor(pages[t][:].indirect(idx2[:]), bell[t][:], wgs_sb[:, t, :], ALU.mult)
 
         early = PACK - 1
         planes = [tile([P, PACK, BANK], BF16, "planes%d" % c) for c in range(CHUNKS)]
-        lim16 = [
-            tile([P, early, BANK], BF16, "lim16_%d" % c, tag=("w1_grouped%d" % c if c < PASSES else None))
-            for c in range(CHUNKS)
-        ]
+        lim16 = [tile([P, early, BANK], BF16, "lim16_%d" % c) for c in range(CHUNKS)]
 
         def round_page(t):
             for c in range(CHUNKS):
@@ -171,7 +182,7 @@ def tile_list_propellant_gauge_fusion_kernel(
         round_limit(1)
         round_page(1)
         round_limit(2)
-        w3_grouped = tile([P, N, PACK], BF16, "w3_grouped")
+        w3_grouped = tile([P, N, PACK], BF16, "w3_grouped", tag="w1_grouped0")
         nc.scalar.copy(
             w3_grouped[:].rearrange("p (c i) j -> p c j i", i=4), w3_raw[:].rearrange("p j (c i) -> p c j i", i=4)
         )
@@ -182,10 +193,10 @@ def tile_list_propellant_gauge_fusion_kernel(
         for c0, c1 in ((0, 256), (256, N)):
             nc.vector.quantize_mx(w3_codes[:, c0:c1].bitcast(FP8X4), w3_sc[:, c0:c1], w3_flat[:, PACK * c0 : PACK * c1])
         neg_bias = tile([P, BLOCKS], F32, "neg_bias")
-        nc.vector.tensor_scalar(neg_bias[:], bias_sb[:], -1.0, None, ALU.mult)
+        nc.gpsimd.tensor_scalar(neg_bias[:], bias_sb[:], -1.0, None, ALU.mult)
 
         z_grouped = tile([P, CHUNKS, BANK, PACK], BF16, "z_grouped", tag="wgs_sb")
-        z_codes = tile([P, T2], U32, "z_codes", tag="w1_raw1")
+        z_codes = tile([P, T2], U32, "z_codes")
         z_sc = [tile([P, BANK], U8, "z_sc%d" % c) for c in range(CHUNKS)]
         score = [tile([P, T2], F32, "score%d" % b, tag="lim%d" % b) for b in range(BLOCKS)]
 

@@ -34,7 +34,7 @@ def tile_list_propellant_gauge_fusion_kernel(
     with ExitStack() as ctx:
         lists = ctx.enter_context(tc.tile_pool(name="lists", bufs=1))
         sb = ctx.enter_context(tc.tile_pool(name="sb", bufs=1))
-        psum = ctx.enter_context(tc.psum_pool(name="psum", bufs=8))
+        psum = ctx.enter_context(tc.psum_pool(name="psum", bufs=1))
 
         def tile(shape, dtype, name, tag=None):
             return sb.tile(shape, dtype, name=name, tag=tag or name, align_bytes=64)
@@ -52,66 +52,44 @@ def tile_list_propellant_gauge_fusion_kernel(
         idx1 = load_list(offs, "idx1")
         tab = [tile([P, T], U32, "tab%d" % a) for a in range(PASSES)]
         w1_raw = [tile([P, PACK, H], F32, "w1_raw%d" % a) for a in range(PASSES)]
-
-        def load_tab(a):
-            nc.sync.dma_start(tab[a][:].bitcast(I32), tab_words[a].rearrange("p t i -> p (t i)").bitcast(I32))
-
-        load_tab(0)
+        for a in range(PASSES):
+            nc.sync.dma_start(w1_raw[a][:], w1[512 * a : 512 * (a + 1), :].rearrange("(p j) c -> p j c", j=PACK))
         for q in range(QUADS):
             nc.gpsimd.dma_start(
                 tab_sc[32 * q : 32 * q + 4 * PASSES, :].bitcast(I32),
                 tab_scales[:, 4 * q : 4 * q + 4, :].bitcast(I32),
             )
         for a in range(PASSES):
-            nc.sync.dma_start(w1_raw[a][:], w1[512 * a : 512 * (a + 1), :].rearrange("(p j) c -> p j c", j=PACK))
-        load_tab(1)
+            nc.sync.dma_start(tab[a][:].bitcast(I32), tab_words[a].rearrange("p t i -> p (t i)").bitcast(I32))
         idx2 = load_list(offs2, "idx2")
-        wgs_rows = wgs.rearrange("(q t) j -> q t j", t=PACK)
-        wgs_sb = tile([P, PACK, S], F32, "wgs_sb")
-        for t0, t1 in ((0, 1), (1, PACK)):
-            for q in range(QUADS):
-                nc.sync.dma_start(wgs_sb[32 * q : 32 * (q + 1), t0:t1, :], wgs_rows[:, t0:t1, :])
+        wgs_rows = wgs.rearrange("(q t) j -> t q j", t=PACK)
+        wgs_sb = [tile([P, S], F32, "wgs%d" % t) for t in range(PACK)]
+        limit_rows = limit.rearrange("(p t) c -> p t c", t=PACK)
+        lim = [tile([P, PACK, BANK], F32, "lim%d" % c) for c in range(CHUNKS)]
+
+        def load_wgs(t):
+            for q in (0, 2, 1, 3):
+                nc.sync.dma_start(wgs_sb[t][32 * q : 32 * (q + 1), :], wgs_rows[t])
+
+        def load_limit(c):
+            nc.sync.dma_start(lim[c][:], limit_rows[:, :, c * BANK : (c + 1) * BANK])
+
+        load_wgs(0)
         gain_sb = tile([P, PACK], F32, "gain_sb")
         nc.sync.dma_start(gain_sb[:], gain.rearrange("(p t) -> p t", t=PACK))
-        limit_rows = limit.rearrange("(p t) c -> t p c", t=PACK)
-        lim = [tile([P, T2], F32, "lim%d" % t) for t in range(PACK)]
-        for t in range(PACK):
-            nc.sync.dma_start(lim[t][:], limit_rows[t])
+        for t in range(1, PACK):
+            load_wgs(t)
+            load_limit(t - 1)
+        w3_raw = tile([P, PACK, N], F32, "w3_raw")
+        nc.sync.dma_start(w3_raw[:], w3.rearrange("(p j) c -> p j c", j=PACK))
+        load_limit(CHUNKS - 1)
 
         pages = [tile([P, T2], F32, "page%d" % t) for t in range(PACK)]
         for t in range(PACK):
-            (nc.vector if t < 2 else nc.gpsimd).memset(pages[t][:], 0.0)
+            nc.vector.memset(pages[t][:], 0.0)
         w2_sc = tile([P, N], U8, "w2_sc")
         nc.vector.memset(w2_sc[:].bitcast(I32), 0)
 
-        got_sc = tile([P, S], U8, "got_sc")
-        got = [tile([P, S], U32, "got%d" % a) for a in range(PASSES)]
-        nc.vector.tensor_copy(got[0][:], tab[0][:].indirect(idx1[:]))
-        nc.vector.tensor_copy(got_sc[:], tab_sc[:].indirect(idx1[:]))
-        w1_codes = []
-        w1_sc = []
-        for a in range(PASSES):
-            grouped = tile([P, PACK, P, PACK], BF16, "w1_grouped%d" % a)
-            dst = grouped[:].rearrange("p t m j -> p m j t")
-            src = w1_raw[a][:].rearrange("p j (m t) -> p m j t", t=PACK)
-            nc.scalar.copy(dst, src)
-            codes = tile([P, H], U32, "w1_codes%d" % a)
-            sc = tile([P, H], U8, "w1_sc%d" % a)
-            nc.vector.quantize_mx(codes[:].bitcast(FP8X4), sc[:], grouped[:].rearrange("p t m j -> p (t m j)"))
-            w1_codes.append(codes)
-            w1_sc.append(sc)
-        half_cols = LIST_COLS // HALVES
-        for u in range(HALVES):
-            nc.vector.tensor_copy(
-                got[1][:, u * BANK : (u + 1) * BANK], tab[1][:].indirect(idx1[:, u * half_cols : (u + 1) * half_cols])
-            )
-
-        budget = [tile([P, T2], F32, "budget%d" % b, tag=tag) for b, tag in enumerate(("tab0", "w1_raw0", "tab1"))]
-        for b in range(BLOCKS):
-            nc.gpsimd.memset(budget[b][:], 0.0)
-
-        w3_raw = tile([P, PACK, N], F32, "w3_raw", tag="w1_raw1")
-        nc.sync.dma_start(w3_raw[:], w3.rearrange("(p j) c -> p j c", j=PACK))
         w2_codes = tile([P, 2 * N], U8, "w2_codes")
         nc.sync.dma_start(w2_codes[:].bitcast(I32), w2_words[0].bitcast(I32))
         for q in range(QUADS):
@@ -124,11 +102,40 @@ def tile_list_propellant_gauge_fusion_kernel(
         wgo_sb = tile([P, S], F32, "wgo_sb")
         nc.sync.dma_start(wgo_sb[:], wgo)
 
+        w1_codes = []
+        w1_sc = []
+        for a in range(PASSES):
+            grouped = tile([P, PACK, P, PACK], BF16, "w1_grouped%d" % a)
+            dst = grouped[:].rearrange("p t m j -> p m j t")
+            src = w1_raw[a][:].rearrange("p j (m t) -> p m j t", t=PACK)
+            nc.scalar.copy(dst, src)
+            codes = tile([P, H], U32, "w1_codes%d" % a)
+            sc = tile([P, H], U8, "w1_sc%d" % a)
+            nc.vector.quantize_mx(codes[:].bitcast(FP8X4), sc[:], grouped[:].rearrange("p t m j -> p (t m j)"))
+            w1_codes.append(codes)
+            w1_sc.append(sc)
+        got_sc = tile([P, S], U8, "got_sc")
+        nc.vector.tensor_copy(got_sc[:], tab_sc[:].indirect(idx1[:]))
+        got = [tile([P, S], U32, "got0", tag="tab_sc"), tile([P, S], U32, "got1", tag="tab0")]
+        nc.vector.tensor_copy(got[0][:], tab[0][:].indirect(idx1[:]))
+        half_cols = LIST_COLS // HALVES
+        for u in range(HALVES):
+            nc.vector.tensor_copy(
+                got[1][:, u * BANK : (u + 1) * BANK], tab[1][:].indirect(idx1[:, u * half_cols : (u + 1) * half_cols])
+            )
+
         bell = [tile([P, S], F32, "bell%d" % t) for t in range(PACK)]
+
+        def place(t, j0, j1):
+            (nc.vector if (t, j0) == (0, 0) else nc.gpsimd).tensor_tensor(
+                bell[t][:, j0:j1], bell[t][:, j0:j1], wgs_sb[t][:, j0:j1], ALU.mult
+            )
+            nc.vector.tensor_copy(pages[t][:].indirect(idx2[:, j0 // 16 : j1 // 16]), bell[t][:, j0:j1])
+
         for t in range(PACK):
             for u in range(HALVES):
                 cols = slice(u * BANK, (u + 1) * BANK)
-                acc = psum.tile([P, BANK], F32, name="acc", tag="bank")
+                acc = psum.tile([P, BANK], F32, name="acc", tag="bank%d" % ((HALVES * t + u) % 4))
                 for a in range(PASSES):
                     nc.tensor.matmul_mx(
                         acc[:],
@@ -140,7 +147,7 @@ def tile_list_propellant_gauge_fusion_kernel(
                         stop=(a == PASSES - 1),
                     )
                 if t >= 2:
-                    stem = "lim16_%d" if t == 2 else "planes%d"
+                    stem = "lim_pairs%d" if t == 2 else "pairs%d"
                     square = tile([P, BANK], F32, "square%d_%d" % (t, u), tag=stem % (2 * u))
                     root = tile([P, BANK], F32, "root%d_%d" % (t, u), tag=stem % (2 * u + 1))
                     nc.scalar.activation(square[:], acc[:], ACT.Square)
@@ -156,80 +163,70 @@ def tile_list_propellant_gauge_fusion_kernel(
                     nc.scalar.activation(part, part, ACT.Abs_reciprocal_sqrt, bias=1.0)
                     nc.scalar.activation(part, part, ACT.Square)
                     if t == 0:
-                        nc.vector.tensor_tensor(
-                            pages[t][:].indirect(idx2[:, j0 // 16 : (j0 + width) // 16]),
-                            part, wgs_sb[:, t, j0 : j0 + width], ALU.mult,
-                        )
+                        place(t, j0, j0 + width)
             if t > 0:
-                nc.vector.tensor_tensor(pages[t][:].indirect(idx2[:]), bell[t][:], wgs_sb[:, t, :], ALU.mult)
+                place(t, 0, S)
 
-        early = PACK - 1
-        planes = [tile([P, PACK, BANK], BF16, "planes%d" % c) for c in range(CHUNKS)]
-        lim16 = [tile([P, early, BANK], BF16, "lim16_%d" % c) for c in range(CHUNKS)]
+        pairs = [tile([P, 2, BANK, 2], BF16, "pairs%d" % c) for c in range(CHUNKS)]
+        lim_pairs = [tile([P, 2, BANK, 2], BF16, "lim_pairs%d" % c) for c in range(CHUNKS)]
 
-        def round_page(t):
+        def round_page(t, c):
+            nc.scalar.activation(
+                pairs[c][:, t // 2, :, t % 2], pages[t][:, c * BANK : (c + 1) * BANK], ACT.Copy, scale=gain_sb[:, t : t + 1]
+            )
+
+        def round_limit(c):
+            src = lim[c][:].rearrange("p (u e) c -> p u c e", e=2)
+            nc.gpsimd.tensor_scalar(lim_pairs[c][:], src, 1.0, 0.0, ALU.mult, ALU.add)
+
+        for t in range(PACK - 1):
             for c in range(CHUNKS):
-                nc.scalar.activation(
-                    planes[c][:, t, :], pages[t][:, c * BANK : (c + 1) * BANK], ACT.Copy, scale=gain_sb[:, t : t + 1]
-                )
-
-        def round_limit(t):
-            for c in range(CHUNKS):
-                nc.scalar.copy(lim16[c][:, t, :], lim[t][:, c * BANK : (c + 1) * BANK])
-
-        round_page(0)
-        round_limit(0)
-        round_limit(1)
-        round_page(1)
-        round_limit(2)
+                round_page(t, c)
+            round_limit(t)
         w3_grouped = tile([P, N, PACK], BF16, "w3_grouped", tag="w1_grouped0")
         nc.scalar.copy(
             w3_grouped[:].rearrange("p (c i) j -> p c j i", i=4), w3_raw[:].rearrange("p j (c i) -> p c j i", i=4)
         )
-        round_page(2)
+        round_limit(CHUNKS - 1)
+        budget = [tile([P, T2], F32, "budget%d" % b, tag=tag) for b, tag in enumerate(("wgs3", "lim2", "lim3"))]
+        for b in range(BLOCKS):
+            nc.gpsimd.memset(budget[b][:], 0.0)
         w3_codes = tile([P, N], U32, "w3_codes")
         w3_sc = tile([P, N], U8, "w3_sc")
         w3_flat = w3_grouped[:].rearrange("p c j -> p (c j)")
         for c0, c1 in ((0, 256), (256, N)):
             nc.vector.quantize_mx(w3_codes[:, c0:c1].bitcast(FP8X4), w3_sc[:, c0:c1], w3_flat[:, PACK * c0 : PACK * c1])
         neg_bias = tile([P, BLOCKS], F32, "neg_bias")
-        nc.gpsimd.tensor_scalar(neg_bias[:], bias_sb[:], -1.0, None, ALU.mult)
+        nc.vector.tensor_scalar(neg_bias[:], bias_sb[:], -1.0, None, ALU.mult)
 
-        z_grouped = tile([P, CHUNKS, BANK, PACK], BF16, "z_grouped", tag="wgs_sb")
+        z_tags = ("tab0", "w1_raw0", "w1_raw1", "w1_grouped1")
+        z_grouped = [tile([P, BANK, PACK], BF16, "z_grouped%d" % c, tag=z_tags[c]) for c in range(CHUNKS)]
         z_codes = tile([P, T2], U32, "z_codes")
         z_sc = [tile([P, BANK], U8, "z_sc%d" % c) for c in range(CHUNKS)]
-        score = [tile([P, T2], F32, "score%d" % b, tag="lim%d" % b) for b in range(BLOCKS)]
+        score = [tile([P, T2], F32, "score%d" % b, tag="page%d" % b) for b in range(BLOCKS)]
 
         def clip(c):
-            cols = slice(c * BANK, (c + 1) * BANK)
-            nc.vector.tensor_tensor(planes[c][:, 0:early, :], planes[c][:, 0:early, :], lim16[c][:], ALU.min)
-            nc.vector.scalar_tensor_tensor(
-                planes[c][:, early, :], pages[early][:, cols], gain_sb[:, early : early + 1], lim[early][:, cols],
-                ALU.mult, ALU.min,
+            nc.vector.tensor_tensor(
+                z_grouped[c][:].rearrange("p c (u e) -> p c u e", e=2),
+                pairs[c][:].rearrange("p u c e -> p c u e"),
+                lim_pairs[c][:].rearrange("p u c e -> p c u e"),
+                ALU.min,
             )
-
-        def group(c):
-            dst = z_grouped[:, c].rearrange("p (c i) t -> p c t i", i=4)
-            src = planes[c][:].rearrange("p t (c i) -> p c t i", i=4)
-            if c < CHUNKS - 1:
-                nc.scalar.copy(dst, src)
-            else:
-                nc.vector.tensor_copy(dst, src)
 
         def quantize(c):
             nc.vector.quantize_mx(
                 z_codes[:, c * BANK : (c + 1) * BANK].bitcast(FP8X4), z_sc[c][:],
-                z_grouped[:, c].rearrange("p c t -> p (c t)"),
+                z_grouped[c][:].rearrange("p c t -> p (c t)"),
             )
 
         def scores(b, c):
             cols = slice(c * BANK, (c + 1) * BANK)
-            y2 = psum.tile([P, BANK], F32, name="y2", tag="bank")
+            y2 = psum.tile([P, BANK], F32, name="y2", tag="bank%d" % c)
             nc.tensor.matmul_mx(
                 y2[:], lhsT=w2_codes[:, 2 * P * b : 2 * P * (b + 1)].bitcast(FP4X4), lhsT_scale=w2_sc[:, P * b : P * (b + 1)],
                 rhs=z_codes[:, cols].bitcast(FP8X4), rhs_scale=z_sc[c][:], start=True, stop=True,
             )
-            y3 = psum.tile([P, BANK], F32, name="y3", tag="bank")
+            y3 = psum.tile([P, BANK], F32, name="y3", tag="bank%d" % (CHUNKS + c))
             nc.tensor.matmul_mx(
                 y3[:], lhsT=w3_codes[:, P * b : P * (b + 1)].bitcast(FP8X4), lhsT_scale=w3_sc[:, P * b : P * (b + 1)],
                 rhs=z_codes[:, cols].bitcast(FP8X4), rhs_scale=z_sc[c][:], start=True, stop=True,
@@ -240,17 +237,20 @@ def tile_list_propellant_gauge_fusion_kernel(
             )
 
         for c in range(CHUNKS):
-            clip(c)
-            group(c)
-        for c in (0, CHUNKS - 1, 1, 2):
+            round_page(PACK - 1, c)
+        clip(0)
+        for c in range(CHUNKS):
+            if c + 1 < CHUNKS:
+                clip(c + 1)
             quantize(c)
+        for c in range(CHUNKS):
             scores(0, c)
 
         for b in range(BLOCKS):
-            if b > 0:
-                for c in range(CHUNKS):
-                    scores(b, c)
             picked = tile([P, S], F32, "picked%d" % b, tag="bell%d" % b)
             nc.vector.tensor_copy(picked[:], score[b][:].indirect(idx3[:]))
+            if b + 1 < BLOCKS:
+                for c in range(CHUNKS):
+                    scores(b + 1, c)
             nc.vector.tensor_tensor(budget[b][:].indirect(idx4[:]), picked[:], wgo_sb[:], ALU.mult)
             nc.sync.dma_start(out[b * P : (b + 1) * P, :], budget[b][:])

@@ -25,6 +25,7 @@ CHUNKS = T2 // BANK
 BLOCKS = N // P
 QUADS = 4
 LIST_COLS = S // 16
+ON_SCALAR = 2
 
 
 def tile_list_propellant_gauge_fusion_kernel(
@@ -55,7 +56,7 @@ def tile_list_propellant_gauge_fusion_kernel(
         for a in range(PASSES):
             nc.sync.dma_start(w1_raw[a][:], w1[512 * a : 512 * (a + 1), :].rearrange("(p j) c -> p j c", j=PACK))
         for q in range(QUADS):
-            nc.gpsimd.dma_start(
+            nc.sync.dma_start(
                 tab_sc[32 * q : 32 * q + 4 * PASSES, :].bitcast(I32),
                 tab_scales[:, 4 * q : 4 * q + 4, :].bitcast(I32),
             )
@@ -63,21 +64,29 @@ def tile_list_propellant_gauge_fusion_kernel(
             nc.sync.dma_start(tab[a][:].bitcast(I32), tab_words[a].rearrange("p t i -> p (t i)").bitcast(I32))
         idx2 = load_list(offs2, "idx2")
         wgs_rows = wgs.rearrange("(q t) j -> t q j", t=PACK)
-        wgs_sb = [tile([P, S], F32, "wgs%d" % t) for t in range(PACK)]
+        wgs_sb = tile([P, PACK, S], F32, "wgs_sb")
         limit_rows = limit.rearrange("(p t) c -> p t c", t=PACK)
         lim = [tile([P, PACK, BANK], F32, "lim%d" % c) for c in range(CHUNKS)]
 
-        def load_wgs(t):
+        def load_wgs(t, j0=0, j1=S):
             for q in (0, 2, 1, 3):
-                nc.sync.dma_start(wgs_sb[t][32 * q : 32 * (q + 1), :], wgs_rows[t])
+                nc.sync.dma_start(wgs_sb[32 * q : 32 * (q + 1), t, j0:j1], wgs_rows[t, :, j0:j1])
 
         def load_limit(c):
             nc.sync.dma_start(lim[c][:], limit_rows[:, :, c * BANK : (c + 1) * BANK])
 
-        load_wgs(0)
+        load_wgs(0, 0, BANK // 2)
+        load_wgs(0, BANK // 2, S)
+        load_wgs(1)
         gain_sb = tile([P, PACK], F32, "gain_sb")
         nc.sync.dma_start(gain_sb[:], gain.rearrange("(p t) -> p t", t=PACK))
-        for t in range(1, PACK):
+        bias_sb = tile([P, BLOCKS], F32, "bias_sb")
+        with nc.allow_non_contiguous_dma(reason="one bias value for each partition and block"):
+            nc.sync.dma_start(bias_sb[:], bias.rearrange("(b p) -> p b", p=P))
+        neg_bias = tile([P, BLOCKS], F32, "neg_bias")
+        nc.gpsimd.tensor_scalar(neg_bias[:], bias_sb[:], -1.0, None, ALU.mult)
+        load_limit(0)
+        for t in range(2, PACK):
             load_wgs(t)
             load_limit(t - 1)
         w3_raw = tile([P, PACK, N], F32, "w3_raw")
@@ -87,6 +96,9 @@ def tile_list_propellant_gauge_fusion_kernel(
         pages = [tile([P, T2], F32, "page%d" % t) for t in range(PACK)]
         for t in range(PACK):
             nc.vector.memset(pages[t][:], 0.0)
+        budget = [tile([P, T2], F32, "budget%d" % b) for b in range(BLOCKS)]
+        for b in range(BLOCKS):
+            nc.gpsimd.memset(budget[b][:], 0.0)
         w2_sc = tile([P, N], U8, "w2_sc")
         nc.vector.memset(w2_sc[:].bitcast(I32), 0)
 
@@ -94,9 +106,6 @@ def tile_list_propellant_gauge_fusion_kernel(
         nc.sync.dma_start(w2_codes[:].bitcast(I32), w2_words[0].bitcast(I32))
         for q in range(QUADS):
             nc.sync.dma_start(w2_sc[32 * q : 32 * q + 4, :].bitcast(I32), w2_scales[0, 4 * q : 4 * q + 4, :].bitcast(I32))
-        bias_sb = tile([P, BLOCKS], F32, "bias_sb")
-        with nc.allow_non_contiguous_dma(reason="one bias value for each partition and block"):
-            nc.sync.dma_start(bias_sb[:], bias.rearrange("(b p) -> p b", p=P))
         idx3 = load_list(offs3, "idx3")
         idx4 = load_list(offs4, "idx4")
         wgo_sb = tile([P, S], F32, "wgo_sb")
@@ -126,14 +135,43 @@ def tile_list_propellant_gauge_fusion_kernel(
 
         bell = [tile([P, S], F32, "bell%d" % t) for t in range(PACK)]
 
-        def place(t, j0, j1):
+        def weigh(t, j0, j1):
             (nc.vector if (t, j0) == (0, 0) else nc.gpsimd).tensor_tensor(
-                bell[t][:, j0:j1], bell[t][:, j0:j1], wgs_sb[t][:, j0:j1], ALU.mult
+                bell[t][:, j0:j1], bell[t][:, j0:j1], wgs_sb[:, t, j0:j1], ALU.mult
             )
+
+        def place(t, j0, j1):
             nc.vector.tensor_copy(pages[t][:].indirect(idx2[:, j0 // 16 : j1 // 16]), bell[t][:, j0:j1])
+
+        FIRST = BANK // 2
+        for v in range(2):
+            cols = slice(v * FIRST, (v + 1) * FIRST)
+            acc = psum.tile([P, FIRST], F32, name="acc", tag="bank%d" % (4 * v))
+            for a in range(PASSES):
+                nc.tensor.matmul_mx(
+                    acc[:],
+                    lhsT=w1_codes[a][:, 0:P].bitcast(FP8X4),
+                    lhsT_scale=w1_sc[a][:, 0:P],
+                    rhs=got[a][:, cols].bitcast(FP8X4),
+                    rhs_scale=got_sc[4 * a : P, cols],
+                    start=(a == 0),
+                    stop=(a == PASSES - 1),
+                )
+            width = FIRST // (2 - v)
+            parts = [(bell[0][:, v * FIRST + j : v * FIRST + j + width], acc[:, j : j + width]) for j in range(0, FIRST, width)]
+            for part, sums in parts:
+                nc.scalar.activation(part, sums, ACT.Square)
+            for part, sums in parts:
+                nc.scalar.activation(part, part, ACT.Abs_reciprocal_sqrt, bias=1.0)
+            for part, sums in parts:
+                nc.scalar.activation(part, part, ACT.Square)
+            weigh(0, v * FIRST, (v + 1) * FIRST)
+            place(0, v * FIRST, (v + 1) * FIRST)
 
         for t in range(PACK):
             for u in range(HALVES):
+                if (t, u) == (0, 0):
+                    continue
                 cols = slice(u * BANK, (u + 1) * BANK)
                 acc = psum.tile([P, BANK], F32, name="acc", tag="bank%d" % ((HALVES * t + u) % 4))
                 for a in range(PASSES):
@@ -147,37 +185,41 @@ def tile_list_propellant_gauge_fusion_kernel(
                         stop=(a == PASSES - 1),
                     )
                 if t >= 2:
-                    stem = "lim_pairs%d" if t == 2 else "pairs%d"
+                    stem = "early%d" if t == 2 else "pairs%d"
                     square = tile([P, BANK], F32, "square%d_%d" % (t, u), tag=stem % (2 * u))
                     root = tile([P, BANK], F32, "root%d_%d" % (t, u), tag=stem % (2 * u + 1))
                     nc.scalar.activation(square[:], acc[:], ACT.Square)
                     nc.scalar.activation(root[:], square[:], ACT.Abs_reciprocal_sqrt, bias=1.0)
                     nc.scalar.activation(bell[t][:, cols], root[:], ACT.Square)
+                    weigh(t, u * BANK, (u + 1) * BANK)
                     continue
-                pieces = 2 if (t, u) == (0, 0) else 1
-                width = BANK // pieces
-                for v in range(pieces):
-                    j0 = u * BANK + v * width
-                    part = bell[t][:, j0 : j0 + width]
-                    nc.scalar.activation(part, acc[:, v * width : (v + 1) * width], ACT.Square)
-                    nc.scalar.activation(part, part, ACT.Abs_reciprocal_sqrt, bias=1.0)
-                    nc.scalar.activation(part, part, ACT.Square)
-                    if t == 0:
-                        place(t, j0, j0 + width)
+                part = bell[t][:, cols]
+                nc.scalar.activation(part, acc[:], ACT.Square)
+                nc.scalar.activation(part, part, ACT.Abs_reciprocal_sqrt, bias=1.0)
+                nc.scalar.activation(part, part, ACT.Square)
+                weigh(t, u * BANK, (u + 1) * BANK)
+                if t == 0:
+                    place(t, u * BANK, (u + 1) * BANK)
             if t > 0:
                 place(t, 0, S)
 
         pairs = [tile([P, 2, BANK, 2], BF16, "pairs%d" % c) for c in range(CHUNKS)]
-        lim_pairs = [tile([P, 2, BANK, 2], BF16, "lim_pairs%d" % c) for c in range(CHUNKS)]
+        lim_late = tile([P, CHUNKS - ON_SCALAR, 2, BANK, 2], BF16, "lim_late", tag="wgs_sb")
+        lim_pairs = [tile([P, 2, BANK, 2], BF16, "lim_pairs%d" % c, tag="early%d" % c)[:] for c in range(ON_SCALAR)]
+        lim_pairs.extend(lim_late[:, c] for c in range(CHUNKS - ON_SCALAR))
 
-        def round_page(t, c):
+        def round_page(t, c, j0=0, j1=BANK):
             nc.scalar.activation(
-                pairs[c][:, t // 2, :, t % 2], pages[t][:, c * BANK : (c + 1) * BANK], ACT.Copy, scale=gain_sb[:, t : t + 1]
+                pairs[c][:, t // 2, j0:j1, t % 2], pages[t][:, c * BANK + j0 : c * BANK + j1], ACT.Copy,
+                scale=gain_sb[:, t : t + 1],
             )
 
         def round_limit(c):
             src = lim[c][:].rearrange("p (u e) c -> p u c e", e=2)
-            nc.gpsimd.tensor_scalar(lim_pairs[c][:], src, 1.0, 0.0, ALU.mult, ALU.add)
+            if c < ON_SCALAR:
+                nc.scalar.copy(lim_pairs[c], src)
+            else:
+                nc.gpsimd.tensor_scalar(lim_pairs[c], src, 1.0, 0.0, ALU.mult, ALU.add)
 
         for t in range(PACK - 1):
             for c in range(CHUNKS):
@@ -188,28 +230,23 @@ def tile_list_propellant_gauge_fusion_kernel(
             w3_grouped[:].rearrange("p (c i) j -> p c j i", i=4), w3_raw[:].rearrange("p j (c i) -> p c j i", i=4)
         )
         round_limit(CHUNKS - 1)
-        budget = [tile([P, T2], F32, "budget%d" % b, tag=tag) for b, tag in enumerate(("wgs3", "lim2", "lim3"))]
-        for b in range(BLOCKS):
-            nc.gpsimd.memset(budget[b][:], 0.0)
         w3_codes = tile([P, N], U32, "w3_codes")
         w3_sc = tile([P, N], U8, "w3_sc")
         w3_flat = w3_grouped[:].rearrange("p c j -> p (c j)")
         for c0, c1 in ((0, 256), (256, N)):
             nc.vector.quantize_mx(w3_codes[:, c0:c1].bitcast(FP8X4), w3_sc[:, c0:c1], w3_flat[:, PACK * c0 : PACK * c1])
-        neg_bias = tile([P, BLOCKS], F32, "neg_bias")
-        nc.vector.tensor_scalar(neg_bias[:], bias_sb[:], -1.0, None, ALU.mult)
 
-        z_tags = ("tab0", "w1_raw0", "w1_raw1", "w1_grouped1")
+        z_tags = ("tab0", "w1_raw0", "w1_grouped1", "w1_raw1")
         z_grouped = [tile([P, BANK, PACK], BF16, "z_grouped%d" % c, tag=z_tags[c]) for c in range(CHUNKS)]
         z_codes = tile([P, T2], U32, "z_codes")
         z_sc = [tile([P, BANK], U8, "z_sc%d" % c) for c in range(CHUNKS)]
-        score = [tile([P, T2], F32, "score%d" % b, tag="page%d" % b) for b in range(BLOCKS)]
+        score = [tile([P, T2], F32, "score%d" % b, tag="page%d" % ((b - 1) % PACK)) for b in range(BLOCKS)]
 
-        def clip(c):
+        def clip(c, j0=0, j1=BANK):
             nc.vector.tensor_tensor(
-                z_grouped[c][:].rearrange("p c (u e) -> p c u e", e=2),
-                pairs[c][:].rearrange("p u c e -> p c u e"),
-                lim_pairs[c][:].rearrange("p u c e -> p c u e"),
+                z_grouped[c][:, j0:j1, :].rearrange("p c (u e) -> p c u e", e=2),
+                pairs[c][:, :, j0:j1, :].rearrange("p u c e -> p c u e"),
+                lim_pairs[c][:, :, j0:j1, :].rearrange("p u c e -> p c u e"),
                 ALU.min,
             )
 
@@ -236,9 +273,11 @@ def tile_list_propellant_gauge_fusion_kernel(
                 score[b][:, cols], y3[:], bias_sb[:, b : b + 1], score[b][:, cols], ALU.subtract, ALU.max
             )
 
-        for c in range(CHUNKS):
+        for j0, j1 in ((0, P), (P, BANK)):
+            round_page(PACK - 1, 0, j0, j1)
+            clip(0, j0, j1)
+        for c in range(1, CHUNKS):
             round_page(PACK - 1, c)
-        clip(0)
         for c in range(CHUNKS):
             if c + 1 < CHUNKS:
                 clip(c + 1)

@@ -19,12 +19,17 @@ ACT = mybir.ActivationFunctionType
 P = 128
 PACK = 4
 BANK = 512
-PASSES = K // (P * PACK)
+QUAD = 32
+QUADS = P // QUAD
+SCALE_ROWS = 4
+PER_COLUMN = 16
+K_PASS = P * PACK
+PASSES = K // K_PASS
 HALVES = S // BANK
 CHUNKS = T2 // BANK
 BLOCKS = N // P
-QUADS = 4
-LIST_COLS = S // 16
+LEAD = BANK // 2
+FIRST_BANKS = 4
 ON_SCALAR = 2
 
 
@@ -41,9 +46,12 @@ def tile_list_propellant_gauge_fusion_kernel(
             return sb.tile(shape, dtype, name=name, tag=tag or name, align_bytes=64)
 
         def load_list(src, name):
-            held = lists.tile([P, LIST_COLS], U16, name=name)
+            held = lists.tile([P, S // PER_COLUMN], U16, name=name)
             nc.sync.dma_start(held[:], src)
             return held
+
+        def entries(held, j0, j1):
+            return held[:, j0 // PER_COLUMN : j1 // PER_COLUMN]
 
         tab_sc = tile([P, T], U8, "tab_sc")
         nc.vector.memset(tab_sc[:].bitcast(I32), 0)
@@ -54,29 +62,29 @@ def tile_list_propellant_gauge_fusion_kernel(
         tab = [tile([P, T], U32, "tab%d" % a) for a in range(PASSES)]
         w1_raw = [tile([P, PACK, H], F32, "w1_raw%d" % a) for a in range(PASSES)]
         for a in range(PASSES):
-            nc.sync.dma_start(w1_raw[a][:], w1[512 * a : 512 * (a + 1), :].rearrange("(p j) c -> p j c", j=PACK))
+            nc.sync.dma_start(w1_raw[a][:], w1[K_PASS * a : K_PASS * (a + 1), :].rearrange("(p j) c -> p j c", j=PACK))
         for q in range(QUADS):
             nc.sync.dma_start(
-                tab_sc[32 * q : 32 * q + 4 * PASSES, :].bitcast(I32),
-                tab_scales[:, 4 * q : 4 * q + 4, :].bitcast(I32),
+                tab_sc[QUAD * q : QUAD * q + SCALE_ROWS * PASSES, :].bitcast(I32),
+                tab_scales[:, SCALE_ROWS * q : SCALE_ROWS * (q + 1), :].bitcast(I32),
             )
         for a in range(PASSES):
             nc.sync.dma_start(tab[a][:].bitcast(I32), tab_words[a].rearrange("p t i -> p (t i)").bitcast(I32))
         idx2 = load_list(offs2, "idx2")
-        wgs_rows = wgs.rearrange("(q t) j -> t q j", t=PACK)
+        wgs_rows = wgs.rearrange("(i t) j -> t i j", t=PACK)
         wgs_sb = tile([P, PACK, S], F32, "wgs_sb")
         limit_rows = limit.rearrange("(p t) c -> p t c", t=PACK)
         lim = [tile([P, PACK, BANK], F32, "lim%d" % c) for c in range(CHUNKS)]
 
         def load_wgs(t, j0=0, j1=S):
             for q in (0, 2, 1, 3):
-                nc.sync.dma_start(wgs_sb[32 * q : 32 * (q + 1), t, j0:j1], wgs_rows[t, :, j0:j1])
+                nc.sync.dma_start(wgs_sb[QUAD * q : QUAD * (q + 1), t, j0:j1], wgs_rows[t, :, j0:j1])
 
         def load_limit(c):
             nc.sync.dma_start(lim[c][:], limit_rows[:, :, c * BANK : (c + 1) * BANK])
 
-        load_wgs(0, 0, BANK // 2)
-        load_wgs(0, BANK // 2, S)
+        load_wgs(0, 0, LEAD)
+        load_wgs(0, LEAD, S)
         load_wgs(1)
         gain_sb = tile([P, PACK], F32, "gain_sb")
         nc.sync.dma_start(gain_sb[:], gain.rearrange("(p t) -> p t", t=PACK))
@@ -86,11 +94,11 @@ def tile_list_propellant_gauge_fusion_kernel(
         neg_bias = tile([P, BLOCKS], F32, "neg_bias")
         nc.gpsimd.tensor_scalar(neg_bias[:], bias_sb[:], -1.0, None, ALU.mult)
         load_limit(0)
+        w3_raw = tile([P, PACK, N], F32, "w3_raw")
+        nc.sync.dma_start(w3_raw[:], w3.rearrange("(p j) c -> p j c", j=PACK))
         for t in range(2, PACK):
             load_wgs(t)
             load_limit(t - 1)
-        w3_raw = tile([P, PACK, N], F32, "w3_raw")
-        nc.sync.dma_start(w3_raw[:], w3.rearrange("(p j) c -> p j c", j=PACK))
         load_limit(CHUNKS - 1)
 
         pages = [tile([P, T2], F32, "page%d" % t) for t in range(PACK)]
@@ -105,7 +113,10 @@ def tile_list_propellant_gauge_fusion_kernel(
         w2_codes = tile([P, 2 * N], U8, "w2_codes")
         nc.sync.dma_start(w2_codes[:].bitcast(I32), w2_words[0].bitcast(I32))
         for q in range(QUADS):
-            nc.sync.dma_start(w2_sc[32 * q : 32 * q + 4, :].bitcast(I32), w2_scales[0, 4 * q : 4 * q + 4, :].bitcast(I32))
+            nc.sync.dma_start(
+                w2_sc[QUAD * q : QUAD * q + SCALE_ROWS, :].bitcast(I32),
+                w2_scales[0, SCALE_ROWS * q : SCALE_ROWS * (q + 1), :].bitcast(I32),
+            )
         idx3 = load_list(offs3, "idx3")
         idx4 = load_list(offs4, "idx4")
         wgo_sb = tile([P, S], F32, "wgo_sb")
@@ -115,9 +126,9 @@ def tile_list_propellant_gauge_fusion_kernel(
         w1_sc = []
         for a in range(PASSES):
             grouped = tile([P, PACK, P, PACK], BF16, "w1_grouped%d" % a)
-            dst = grouped[:].rearrange("p t m j -> p m j t")
-            src = w1_raw[a][:].rearrange("p j (m t) -> p m j t", t=PACK)
-            nc.scalar.copy(dst, src)
+            nc.scalar.copy(
+                grouped[:].rearrange("p t m j -> p m j t"), w1_raw[a][:].rearrange("p j (m t) -> p m j t", t=PACK)
+            )
             codes = tile([P, H], U32, "w1_codes%d" % a)
             sc = tile([P, H], U8, "w1_sc%d" % a)
             nc.vector.quantize_mx(codes[:].bitcast(FP8X4), sc[:], grouped[:].rearrange("p t m j -> p (t m j)"))
@@ -127,92 +138,77 @@ def tile_list_propellant_gauge_fusion_kernel(
         nc.vector.tensor_copy(got_sc[:], tab_sc[:].indirect(idx1[:]))
         got = [tile([P, S], U32, "got0", tag="tab_sc"), tile([P, S], U32, "got1", tag="tab0")]
         nc.vector.tensor_copy(got[0][:], tab[0][:].indirect(idx1[:]))
-        half_cols = LIST_COLS // HALVES
         for u in range(HALVES):
-            nc.vector.tensor_copy(
-                got[1][:, u * BANK : (u + 1) * BANK], tab[1][:].indirect(idx1[:, u * half_cols : (u + 1) * half_cols])
-            )
+            j0, j1 = u * BANK, (u + 1) * BANK
+            nc.vector.tensor_copy(got[1][:, j0:j1], tab[1][:].indirect(entries(idx1, j0, j1)))
 
         bell = [tile([P, S], F32, "bell%d" % t) for t in range(PACK)]
 
-        def weigh(t, j0, j1):
-            (nc.vector if (t, j0) == (0, 0) else nc.gpsimd).tensor_tensor(
-                bell[t][:, j0:j1], bell[t][:, j0:j1], wgs_sb[:, t, j0:j1], ALU.mult
-            )
-
-        def place(t, j0, j1):
-            nc.vector.tensor_copy(pages[t][:].indirect(idx2[:, j0 // 16 : j1 // 16]), bell[t][:, j0:j1])
-
-        FIRST = BANK // 2
-        for v in range(2):
-            cols = slice(v * FIRST, (v + 1) * FIRST)
-            acc = psum.tile([P, FIRST], F32, name="acc", tag="bank%d" % (4 * v))
+        def first_product(t, j0, j1, bank):
+            acc = psum.tile([P, j1 - j0], F32, name="acc", tag="bank%d" % bank)
             for a in range(PASSES):
                 nc.tensor.matmul_mx(
                     acc[:],
-                    lhsT=w1_codes[a][:, 0:P].bitcast(FP8X4),
-                    lhsT_scale=w1_sc[a][:, 0:P],
-                    rhs=got[a][:, cols].bitcast(FP8X4),
-                    rhs_scale=got_sc[4 * a : P, cols],
+                    lhsT=w1_codes[a][:, t * P : (t + 1) * P].bitcast(FP8X4),
+                    lhsT_scale=w1_sc[a][:, t * P : (t + 1) * P],
+                    rhs=got[a][:, j0:j1].bitcast(FP8X4),
+                    rhs_scale=got_sc[SCALE_ROWS * a : P, j0:j1],
                     start=(a == 0),
                     stop=(a == PASSES - 1),
                 )
-            width = FIRST // (2 - v)
-            parts = [(bell[0][:, v * FIRST + j : v * FIRST + j + width], acc[:, j : j + width]) for j in range(0, FIRST, width)]
-            for part, sums in parts:
-                nc.scalar.activation(part, sums, ACT.Square)
-            for part, sums in parts:
-                nc.scalar.activation(part, part, ACT.Abs_reciprocal_sqrt, bias=1.0)
-            for part, sums in parts:
-                nc.scalar.activation(part, part, ACT.Square)
-            weigh(0, v * FIRST, (v + 1) * FIRST)
-            place(0, v * FIRST, (v + 1) * FIRST)
+            return acc
 
+        def respond(steps):
+            for sums, square, root, result in steps:
+                nc.scalar.activation(square, sums, ACT.Square)
+            for sums, square, root, result in steps:
+                nc.scalar.activation(root, square, ACT.Abs_reciprocal_sqrt, bias=1.0)
+            for sums, square, root, result in steps:
+                nc.scalar.activation(result, root, ACT.Square)
+
+        def weigh(engine, t, j0, j1):
+            engine.tensor_tensor(bell[t][:, j0:j1], bell[t][:, j0:j1], wgs_sb[:, t, j0:j1], ALU.mult)
+
+        def place(t, j0, j1):
+            nc.vector.tensor_copy(pages[t][:].indirect(entries(idx2, j0, j1)), bell[t][:, j0:j1])
+
+        acc = first_product(0, 0, LEAD, 0)
+        respond([(acc[:, j : j + P],) + (bell[0][:, j : j + P],) * 3 for j in range(0, LEAD, P)])
+        weigh(nc.vector, 0, 0, LEAD)
+        place(0, 0, LEAD)
+        acc = first_product(0, LEAD, BANK, FIRST_BANKS)
+        respond([(acc[:],) + (bell[0][:, LEAD:BANK],) * 3])
+        weigh(nc.gpsimd, 0, LEAD, BANK)
+        place(0, LEAD, BANK)
+
+        held_tags = {2: "after_plane2_%d", 3: "after_plane3_%d"}
         for t in range(PACK):
-            for u in range(HALVES):
-                if (t, u) == (0, 0):
-                    continue
-                cols = slice(u * BANK, (u + 1) * BANK)
-                acc = psum.tile([P, BANK], F32, name="acc", tag="bank%d" % ((HALVES * t + u) % 4))
-                for a in range(PASSES):
-                    nc.tensor.matmul_mx(
-                        acc[:],
-                        lhsT=w1_codes[a][:, t * P : (t + 1) * P].bitcast(FP8X4),
-                        lhsT_scale=w1_sc[a][:, t * P : (t + 1) * P],
-                        rhs=got[a][:, cols].bitcast(FP8X4),
-                        rhs_scale=got_sc[4 * a : P, cols],
-                        start=(a == 0),
-                        stop=(a == PASSES - 1),
-                    )
-                if t >= 2:
-                    stem = "early%d" if t == 2 else "pairs%d"
-                    square = tile([P, BANK], F32, "square%d_%d" % (t, u), tag=stem % (2 * u))
-                    root = tile([P, BANK], F32, "root%d_%d" % (t, u), tag=stem % (2 * u + 1))
-                    nc.scalar.activation(square[:], acc[:], ACT.Square)
-                    nc.scalar.activation(root[:], square[:], ACT.Abs_reciprocal_sqrt, bias=1.0)
-                    nc.scalar.activation(bell[t][:, cols], root[:], ACT.Square)
-                    weigh(t, u * BANK, (u + 1) * BANK)
-                    continue
-                part = bell[t][:, cols]
-                nc.scalar.activation(part, acc[:], ACT.Square)
-                nc.scalar.activation(part, part, ACT.Abs_reciprocal_sqrt, bias=1.0)
-                nc.scalar.activation(part, part, ACT.Square)
-                weigh(t, u * BANK, (u + 1) * BANK)
-                if t == 0:
-                    place(t, u * BANK, (u + 1) * BANK)
-            if t > 0:
-                place(t, 0, S)
+            for u in range(1 if t == 0 else 0, HALVES):
+                j0, j1 = u * BANK, (u + 1) * BANK
+                acc = first_product(t, j0, j1, (HALVES * t + u) % FIRST_BANKS)
+                result = bell[t][:, j0:j1]
+                if t in held_tags:
+                    square = tile([P, BANK], F32, "square%d_%d" % (t, u), tag=held_tags[t] % (2 * u))[:]
+                    root = tile([P, BANK], F32, "root%d_%d" % (t, u), tag=held_tags[t] % (2 * u + 1))[:]
+                else:
+                    square, root = result, result
+                respond([(acc[:], square, root, result)])
+                weigh(nc.gpsimd, t, j0, j1)
+            place(t, BANK if t == 0 else 0, S)
 
-        pairs = [tile([P, 2, BANK, 2], BF16, "pairs%d" % c) for c in range(CHUNKS)]
+        edges = [0, P] + [BANK * (c + 1) for c in range(CHUNKS)]
+        pieces = list(zip(edges[:-1], edges[1:]))
+        pair_tags = ["after_plane3_0", "after_plane2_2"] + ["after_plane3_%d" % c for c in range(1, CHUNKS)]
+        pairs = [tile([P, 2, j1 - j0, 2], BF16, "pairs_at%d" % j0, tag=tag) for (j0, j1), tag in zip(pieces, pair_tags)]
         lim_late = tile([P, CHUNKS - ON_SCALAR, 2, BANK, 2], BF16, "lim_late", tag="wgs_sb")
-        lim_pairs = [tile([P, 2, BANK, 2], BF16, "lim_pairs%d" % c, tag="early%d" % c)[:] for c in range(ON_SCALAR)]
+        lim_pairs = [
+            tile([P, 2, BANK, 2], BF16, "lim_pairs%d" % c, tag="after_plane2_%d" % c)[:] for c in range(ON_SCALAR)
+        ]
         lim_pairs.extend(lim_late[:, c] for c in range(CHUNKS - ON_SCALAR))
 
-        def round_page(t, c, j0=0, j1=BANK):
-            nc.scalar.activation(
-                pairs[c][:, t // 2, j0:j1, t % 2], pages[t][:, c * BANK + j0 : c * BANK + j1], ACT.Copy,
-                scale=gain_sb[:, t : t + 1],
-            )
+        def round_page(t, i):
+            j0, j1 = pieces[i]
+            nc.scalar.activation(pairs[i][:, t // 2, :, t % 2], pages[t][:, j0:j1], ACT.Copy, scale=gain_sb[:, t : t + 1])
 
         def round_limit(c):
             src = lim[c][:].rearrange("p (u e) c -> p u c e", e=2)
@@ -222,74 +218,125 @@ def tile_list_propellant_gauge_fusion_kernel(
                 nc.gpsimd.tensor_scalar(lim_pairs[c], src, 1.0, 0.0, ALU.mult, ALU.add)
 
         for t in range(PACK - 1):
-            for c in range(CHUNKS):
-                round_page(t, c)
+            for i in range(len(pieces)):
+                round_page(t, i)
             round_limit(t)
-        w3_grouped = tile([P, N, PACK], BF16, "w3_grouped", tag="w1_grouped0")
+        w3_grouped = tile([P, N, PACK], BF16, "w3_grouped", tag="after_plane2_3")
         nc.scalar.copy(
             w3_grouped[:].rearrange("p (c i) j -> p c j i", i=4), w3_raw[:].rearrange("p j (c i) -> p c j i", i=4)
         )
         round_limit(CHUNKS - 1)
-        w3_codes = tile([P, N], U32, "w3_codes")
+        w3_codes = tile([P, N], U32, "w3_codes", tag="bell%d" % (PACK - 1))
         w3_sc = tile([P, N], U8, "w3_sc")
         w3_flat = w3_grouped[:].rearrange("p c j -> p (c j)")
-        for c0, c1 in ((0, 256), (256, N)):
+        for c0, c1 in ((0, 2 * P), (2 * P, N)):
             nc.vector.quantize_mx(w3_codes[:, c0:c1].bitcast(FP8X4), w3_sc[:, c0:c1], w3_flat[:, PACK * c0 : PACK * c1])
 
         z_tags = ("tab0", "w1_raw0", "w1_grouped1", "w1_raw1")
         z_grouped = [tile([P, BANK, PACK], BF16, "z_grouped%d" % c, tag=z_tags[c]) for c in range(CHUNKS)]
         z_codes = tile([P, T2], U32, "z_codes")
         z_sc = [tile([P, BANK], U8, "z_sc%d" % c) for c in range(CHUNKS)]
-        score = [tile([P, T2], F32, "score%d" % b, tag="page%d" % ((b - 1) % PACK)) for b in range(BLOCKS)]
+        chunks = [slice(c * BANK, (c + 1) * BANK) for c in range(CHUNKS)]
 
-        def clip(c, j0=0, j1=BANK):
+        def clip(i):
+            c = pieces[i][0] // BANK
+            j0, j1 = pieces[i][0] - c * BANK, pieces[i][1] - c * BANK
             nc.vector.tensor_tensor(
                 z_grouped[c][:, j0:j1, :].rearrange("p c (u e) -> p c u e", e=2),
-                pairs[c][:, :, j0:j1, :].rearrange("p u c e -> p c u e"),
+                pairs[i][:].rearrange("p u c e -> p c u e"),
                 lim_pairs[c][:, :, j0:j1, :].rearrange("p u c e -> p c u e"),
                 ALU.min,
             )
 
         def quantize(c):
             nc.vector.quantize_mx(
-                z_codes[:, c * BANK : (c + 1) * BANK].bitcast(FP8X4), z_sc[c][:],
-                z_grouped[c][:].rearrange("p c t -> p (c t)"),
+                z_codes[:, chunks[c]].bitcast(FP8X4), z_sc[c][:], z_grouped[c][:].rearrange("p c t -> p (c t)")
             )
 
-        def scores(b, c):
-            cols = slice(c * BANK, (c + 1) * BANK)
+        def second_products(b, c):
             y2 = psum.tile([P, BANK], F32, name="y2", tag="bank%d" % c)
             nc.tensor.matmul_mx(
                 y2[:], lhsT=w2_codes[:, 2 * P * b : 2 * P * (b + 1)].bitcast(FP4X4), lhsT_scale=w2_sc[:, P * b : P * (b + 1)],
-                rhs=z_codes[:, cols].bitcast(FP8X4), rhs_scale=z_sc[c][:], start=True, stop=True,
+                rhs=z_codes[:, chunks[c]].bitcast(FP8X4), rhs_scale=z_sc[c][:], start=True, stop=True,
             )
             y3 = psum.tile([P, BANK], F32, name="y3", tag="bank%d" % (CHUNKS + c))
             nc.tensor.matmul_mx(
                 y3[:], lhsT=w3_codes[:, P * b : P * (b + 1)].bitcast(FP8X4), lhsT_scale=w3_sc[:, P * b : P * (b + 1)],
-                rhs=z_codes[:, cols].bitcast(FP8X4), rhs_scale=z_sc[c][:], start=True, stop=True,
+                rhs=z_codes[:, chunks[c]].bitcast(FP8X4), rhs_scale=z_sc[c][:], start=True, stop=True,
             )
-            nc.scalar.activation(score[b][:, cols], y2[:], ACT.Identity, bias=neg_bias[:, b : b + 1])
+            return y2, y3
+
+        def less_bias(dst, sums, b):
+            nc.scalar.activation(dst, sums[:], ACT.Identity, bias=neg_bias[:, b : b + 1])
+
+        score = [tile([P, T2], F32, "score0", tag="page3"), tile([P, T2], F32, "score1", tag="page0")]
+
+        def scores(b, c):
+            y2, y3 = second_products(b, c)
+            less_bias(score[b][:, chunks[c]], y2, b)
             nc.vector.scalar_tensor_tensor(
-                score[b][:, cols], y3[:], bias_sb[:, b : b + 1], score[b][:, cols], ALU.subtract, ALU.max
+                score[b][:, chunks[c]], y3[:], bias_sb[:, b : b + 1], score[b][:, chunks[c]], ALU.subtract, ALU.max
             )
 
-        for j0, j1 in ((0, P), (P, BANK)):
-            round_page(PACK - 1, 0, j0, j1)
-            clip(0, j0, j1)
-        for c in range(1, CHUNKS):
-            round_page(PACK - 1, c)
+        for i in range(len(pieces)):
+            round_page(PACK - 1, i)
+        clip(0)
+        clip(1)
         for c in range(CHUNKS):
             if c + 1 < CHUNKS:
-                clip(c + 1)
+                clip(c + 2)
             quantize(c)
         for c in range(CHUNKS):
             scores(0, c)
 
-        for b in range(BLOCKS):
-            picked = tile([P, S], F32, "picked%d" % b, tag="bell%d" % b)
-            nc.vector.tensor_copy(picked[:], score[b][:].indirect(idx3[:]))
-            if b + 1 < BLOCKS:
-                for c in range(CHUNKS):
-                    scores(b + 1, c)
-            nc.vector.tensor_tensor(budget[b][:].indirect(idx4[:]), picked[:], wgo_sb[:], ALU.mult)
+        picked = [tile([P, S], F32, "picked%d" % b, tag=tag) for b, tag in enumerate(("bell0", "tab1", "bell2"))]
+
+        def pick(b):
+            nc.vector.tensor_copy(picked[b][:], score[b][:].indirect(idx3[:]))
+
+        def put(b, values, j0, j1):
+            nc.vector.tensor_copy(budget[b][:].indirect(entries(idx4, j0, j1)), values[:, j0:j1])
+
+        def store(b):
             nc.sync.dma_start(out[b * P : (b + 1) * P, :], budget[b][:])
+
+        scores(1, 0)
+        pick(0)
+        for j0, j1 in ((0, LEAD), (LEAD, S)):
+            nc.gpsimd.tensor_tensor(picked[0][:, j0:j1], picked[0][:, j0:j1], wgo_sb[:, j0:j1], ALU.mult)
+        for c in range(1, CHUNKS):
+            scores(1, c)
+        put(0, picked[0], 0, LEAD)
+        pick(1)
+        put(0, picked[0], LEAD, S)
+        store(0)
+
+        last = BLOCKS - 1
+        first_score = tile([P, T2], F32, "first_score", tag="page1")
+        second_score = [tile([P, T2], F32, "second_score%d" % u, tag="lim%d" % u) for u in range(2)]
+        for c in range(CHUNKS):
+            y2, y3 = second_products(last, c)
+            less_bias(first_score[:, chunks[c]], y2, last)
+            less_bias(second_score[c // 2][:, chunks[c]], y3, last)
+        excess = tile([P, T2], F32, "excess", tag="lim2")
+
+        wide = [slice(u * T2 // 2, (u + 1) * T2 // 2) for u in range(2)]
+
+        def make_excess(u):
+            cols = wide[u]
+            nc.gpsimd.tensor_tensor(excess[:, cols], second_score[u][:, cols], first_score[:, cols], ALU.subtract)
+            nc.scalar.activation(excess[:, cols], excess[:, cols], ACT.Relu)
+
+        make_excess(0)
+        weighted = tile([P, S], F32, "weighted", tag="lim0")
+        nc.gpsimd.tensor_tensor(weighted[:], picked[1][:], wgo_sb[:], ALU.mult)
+        make_excess(1)
+        score.append(tile([P, T2], F32, "score2", tag="tab1"))
+        for cols in wide:
+            nc.gpsimd.tensor_tensor(score[last][:, cols], first_score[:, cols], excess[:, cols], ALU.add)
+        put(1, weighted, 0, S)
+        store(1)
+
+        pick(last)
+        nc.vector.tensor_tensor(budget[last][:].indirect(idx4[:]), picked[last][:], wgo_sb[:], ALU.mult)
+        store(last)

@@ -30,7 +30,6 @@ CHUNKS = T2 // BANK
 BLOCKS = N // P
 LEAD = BANK // 2
 FIRST_BANKS = 4
-ON_SCALAR = 2
 
 
 def tile_list_propellant_gauge_fusion_kernel(
@@ -61,31 +60,35 @@ def tile_list_propellant_gauge_fusion_kernel(
         idx1 = load_list(offs, "idx1")
         tab = [tile([P, T], U32, "tab%d" % a) for a in range(PASSES)]
         w1_raw = [tile([P, PACK, H], F32, "w1_raw%d" % a) for a in range(PASSES)]
-        for a in range(PASSES):
+
+        def load_w1(a):
             nc.sync.dma_start(w1_raw[a][:], w1[K_PASS * a : K_PASS * (a + 1), :].rearrange("(p j) c -> p j c", j=PACK))
+
+        load_w1(0)
         for q in range(QUADS):
             nc.sync.dma_start(
                 tab_sc[QUAD * q : QUAD * q + SCALE_ROWS * PASSES, :].bitcast(I32),
                 tab_scales[:, SCALE_ROWS * q : SCALE_ROWS * (q + 1), :].bitcast(I32),
             )
+        load_w1(1)
         for a in range(PASSES):
             nc.sync.dma_start(tab[a][:].bitcast(I32), tab_words[a].rearrange("p t i -> p (t i)").bitcast(I32))
         idx2 = load_list(offs2, "idx2")
         wgs_rows = wgs.rearrange("(i t) j -> t i j", t=PACK)
-        wgs_sb = tile([P, PACK, S], F32, "wgs_sb")
+        wgs_sb = [tile([P, S], F32, "wgs%d" % t) for t in range(PACK)]
         limit_rows = limit.rearrange("(p t) c -> p t c", t=PACK)
         lim = [tile([P, PACK, BANK], F32, "lim%d" % c) for c in range(CHUNKS)]
 
         def load_wgs(t, j0=0, j1=S):
             for q in (0, 2, 1, 3):
-                nc.sync.dma_start(wgs_sb[QUAD * q : QUAD * (q + 1), t, j0:j1], wgs_rows[t, :, j0:j1])
+                nc.sync.dma_start(wgs_sb[t][QUAD * q : QUAD * (q + 1), j0:j1], wgs_rows[t, :, j0:j1])
 
         def load_limit(c):
             nc.sync.dma_start(lim[c][:], limit_rows[:, :, c * BANK : (c + 1) * BANK])
 
-        load_wgs(0, 0, LEAD)
-        load_wgs(0, LEAD, S)
-        load_wgs(1)
+        for u in range(HALVES):
+            for t in range(2):
+                load_wgs(t, u * BANK, (u + 1) * BANK)
         gain_sb = tile([P, PACK], F32, "gain_sb")
         nc.sync.dma_start(gain_sb[:], gain.rearrange("(p t) -> p t", t=PACK))
         bias_sb = tile([P, BLOCKS], F32, "bias_sb")
@@ -106,7 +109,7 @@ def tile_list_propellant_gauge_fusion_kernel(
             nc.vector.memset(pages[t][:], 0.0)
         budget = [tile([P, T2], F32, "budget%d" % b) for b in range(BLOCKS)]
         for b in range(BLOCKS):
-            nc.gpsimd.memset(budget[b][:], 0.0)
+            nc.vector.memset(budget[b][:], 0.0)
         w2_sc = tile([P, N], U8, "w2_sc")
         nc.vector.memset(w2_sc[:].bitcast(I32), 0)
 
@@ -167,7 +170,7 @@ def tile_list_propellant_gauge_fusion_kernel(
                 nc.scalar.activation(result, root, ACT.Square)
 
         def weigh(engine, t, j0, j1):
-            engine.tensor_tensor(bell[t][:, j0:j1], bell[t][:, j0:j1], wgs_sb[:, t, j0:j1], ALU.mult)
+            engine.tensor_tensor(bell[t][:, j0:j1], bell[t][:, j0:j1], wgs_sb[t][:, j0:j1], ALU.mult)
 
         def place(t, j0, j1):
             nc.vector.tensor_copy(pages[t][:].indirect(entries(idx2, j0, j1)), bell[t][:, j0:j1])
@@ -176,16 +179,18 @@ def tile_list_propellant_gauge_fusion_kernel(
         respond([(acc[:, j : j + P],) + (bell[0][:, j : j + P],) * 3 for j in range(0, LEAD, P)])
         weigh(nc.vector, 0, 0, LEAD)
         place(0, 0, LEAD)
-        acc = first_product(0, LEAD, BANK, FIRST_BANKS)
-        respond([(acc[:],) + (bell[0][:, LEAD:BANK],) * 3])
-        weigh(nc.gpsimd, 0, LEAD, BANK)
-        place(0, LEAD, BANK)
+        woven = [(1, 0, LEAD), (0, LEAD, BANK), (1, LEAD, BANK), (0, BANK, S), (1, BANK, S)]
+        for i, (t, j0, j1) in enumerate(woven):
+            acc = first_product(t, j0, j1, (i + 1) % FIRST_BANKS)
+            respond([(acc[:],) + (bell[t][:, j0:j1],) * 3])
+            weigh(nc.gpsimd, t, j0, j1)
+            place(t, j0, j1)
 
         held_tags = {2: "after_plane2_%d", 3: "after_plane3_%d"}
-        for t in range(PACK):
-            for u in range(1 if t == 0 else 0, HALVES):
+        for t in range(2, PACK):
+            for u in range(HALVES):
                 j0, j1 = u * BANK, (u + 1) * BANK
-                acc = first_product(t, j0, j1, (HALVES * t + u) % FIRST_BANKS)
+                acc = first_product(t, j0, j1, (HALVES * t + u + 2) % FIRST_BANKS)
                 result = bell[t][:, j0:j1]
                 if t in held_tags:
                     square = tile([P, BANK], F32, "square%d_%d" % (t, u), tag=held_tags[t] % (2 * u))[:]
@@ -194,17 +199,15 @@ def tile_list_propellant_gauge_fusion_kernel(
                     square, root = result, result
                 respond([(acc[:], square, root, result)])
                 weigh(nc.gpsimd, t, j0, j1)
-            place(t, BANK if t == 0 else 0, S)
+            place(t, 0, S)
 
         edges = [0, P] + [BANK * (c + 1) for c in range(CHUNKS)]
         pieces = list(zip(edges[:-1], edges[1:]))
         pair_tags = ["after_plane3_0", "after_plane2_2"] + ["after_plane3_%d" % c for c in range(1, CHUNKS)]
         pairs = [tile([P, 2, j1 - j0, 2], BF16, "pairs_at%d" % j0, tag=tag) for (j0, j1), tag in zip(pieces, pair_tags)]
-        lim_late = tile([P, CHUNKS - ON_SCALAR, 2, BANK, 2], BF16, "lim_late", tag="wgs_sb")
-        lim_pairs = [
-            tile([P, 2, BANK, 2], BF16, "lim_pairs%d" % c, tag="after_plane2_%d" % c)[:] for c in range(ON_SCALAR)
-        ]
-        lim_pairs.extend(lim_late[:, c] for c in range(CHUNKS - ON_SCALAR))
+        lim_late = tile([P, 2, 2, BANK, 2], BF16, "lim_late", tag="wgs3")
+        lim_pairs = [tile([P, 2, BANK, 2], BF16, "lim_pairs%d" % c, tag="wgs%d" % (c + 1))[:] for c in range(2)]
+        lim_pairs.extend(lim_late[:, c] for c in range(2))
 
         def round_page(t, i):
             j0, j1 = pieces[i]
@@ -212,10 +215,8 @@ def tile_list_propellant_gauge_fusion_kernel(
 
         def round_limit(c):
             src = lim[c][:].rearrange("p (u e) c -> p u c e", e=2)
-            if c < ON_SCALAR:
-                nc.scalar.copy(lim_pairs[c], src)
-            else:
-                nc.gpsimd.tensor_scalar(lim_pairs[c], src, 1.0, 0.0, ALU.mult, ALU.add)
+            for u in range(2):
+                nc.gpsimd.tensor_scalar(lim_pairs[c][:, u], src[:, u], 1.0, 0.0, ALU.mult, ALU.add)
 
         for t in range(PACK - 1):
             for i in range(len(pieces)):

@@ -104,12 +104,9 @@ def tile_list_propellant_gauge_fusion_kernel(
             load_limit(t - 1)
         load_limit(CHUNKS - 1)
 
-        pages = [tile([P, T2], F32, "page%d" % t) for t in range(PACK)]
-        for t in range(PACK):
-            nc.vector.memset(pages[t][:], 0.0)
-        budget = [tile([P, T2], F32, "budget%d" % b) for b in range(BLOCKS)]
-        for b in range(BLOCKS):
-            nc.vector.memset(budget[b][:], 0.0)
+        pages = [tile([P, T2], F32, "page%d" % t) for t in range(PACK - 1)]
+        for t in range(PACK - 1):
+            nc.vector.memset(pages[t][:].bitcast(I32), 0)
         w2_sc = tile([P, N], U8, "w2_sc")
         nc.vector.memset(w2_sc[:].bitcast(I32), 0)
 
@@ -137,6 +134,10 @@ def tile_list_propellant_gauge_fusion_kernel(
             nc.vector.quantize_mx(codes[:].bitcast(FP8X4), sc[:], grouped[:].rearrange("p t m j -> p (t m j)"))
             w1_codes.append(codes)
             w1_sc.append(sc)
+        budget = [tile([P, T2], F32, "budget%d" % b, tag="w1_grouped%d" % b) for b in range(2)]
+        pages.append(tile([P, T2], F32, "page3", tag="w1_raw1"))
+        for window in (budget[0], pages[3], budget[1]):
+            nc.gpsimd.memset(window[:], 0.0)
         got_sc = tile([P, S], U8, "got_sc")
         nc.vector.tensor_copy(got_sc[:], tab_sc[:].indirect(idx1[:]))
         got = [tile([P, S], U32, "got0", tag="tab_sc"), tile([P, S], U32, "got1", tag="tab0")]
@@ -227,13 +228,15 @@ def tile_list_propellant_gauge_fusion_kernel(
             w3_grouped[:].rearrange("p (c i) j -> p c j i", i=4), w3_raw[:].rearrange("p j (c i) -> p c j i", i=4)
         )
         round_limit(CHUNKS - 1)
+        budget.append(tile([P, T2], F32, "budget2", tag="lim3"))
+        nc.gpsimd.memset(budget[2][:], 0.0)
         w3_codes = tile([P, N], U32, "w3_codes", tag="bell%d" % (PACK - 1))
         w3_sc = tile([P, N], U8, "w3_sc")
         w3_flat = w3_grouped[:].rearrange("p c j -> p (c j)")
         for c0, c1 in ((0, 2 * P), (2 * P, N)):
             nc.vector.quantize_mx(w3_codes[:, c0:c1].bitcast(FP8X4), w3_sc[:, c0:c1], w3_flat[:, PACK * c0 : PACK * c1])
 
-        z_tags = ("tab0", "w1_raw0", "w1_grouped1", "w1_raw1")
+        z_tags = ("tab0", "w1_raw0", "wgs0", "z_grouped3")
         z_grouped = [tile([P, BANK, PACK], BF16, "z_grouped%d" % c, tag=z_tags[c]) for c in range(CHUNKS)]
         z_codes = tile([P, T2], U32, "z_codes")
         z_sc = [tile([P, BANK], U8, "z_sc%d" % c) for c in range(CHUNKS)]
@@ -270,7 +273,7 @@ def tile_list_propellant_gauge_fusion_kernel(
         def less_bias(dst, sums, b):
             nc.scalar.activation(dst, sums[:], ACT.Identity, bias=neg_bias[:, b : b + 1])
 
-        score = [tile([P, T2], F32, "score0", tag="page3"), tile([P, T2], F32, "score1", tag="page0")]
+        score = [tile([P, T2], F32, "score0", tag="w1_raw1"), tile([P, T2], F32, "score1", tag="page0")]
 
         def scores(b, c):
             y2, y3 = second_products(b, c)

@@ -57,22 +57,29 @@ def tile_list_propellant_gauge_fusion_kernel(
         warm = tile([P, 2], F32, "warm")
         nc.vector.memset(warm[:, 0:1], 1.0)
         nc.scalar.activation(warm[:, 1:2], warm[:, 0:1], ACT.Abs_reciprocal_sqrt)
-        idx1 = load_list(offs, "idx1")
         tab = [tile([P, T], U32, "tab%d" % a) for a in range(PASSES)]
         w1_raw = [tile([P, PACK, H], F32, "w1_raw%d" % a) for a in range(PASSES)]
 
         def load_w1(a):
             nc.sync.dma_start(w1_raw[a][:], w1[K_PASS * a : K_PASS * (a + 1), :].rearrange("(p j) c -> p j c", j=PACK))
 
-        load_w1(0)
-        for q in range(QUADS):
-            nc.sync.dma_start(
-                tab_sc[QUAD * q : QUAD * q + SCALE_ROWS * PASSES, :].bitcast(I32),
-                tab_scales[:, SCALE_ROWS * q : SCALE_ROWS * (q + 1), :].bitcast(I32),
-            )
-        load_w1(1)
-        for a in range(PASSES):
+        def load_tab(a):
             nc.sync.dma_start(tab[a][:].bitcast(I32), tab_words[a].rearrange("p t i -> p (t i)").bitcast(I32))
+
+        def load_scales(rows):
+            for r in rows:
+                for a in range(PASSES):
+                    nc.sync.dma_start(
+                        tab_sc[SCALE_ROWS * a + r : P : QUAD, :].bitcast(I32), tab_scales[a, r::SCALE_ROWS, :].bitcast(I32)
+                    )
+
+        load_w1(0)
+        idx1 = load_list(offs, "idx1")
+        load_scales((0, 1))
+        load_w1(1)
+        load_tab(0)
+        load_scales((2, 3))
+        load_tab(1)
         idx2 = load_list(offs2, "idx2")
         wgs_rows = wgs.rearrange("(i t) j -> t i j", t=PACK)
         wgs_sb = [tile([P, S], F32, "wgs%d" % t) for t in range(PACK)]
@@ -138,13 +145,15 @@ def tile_list_propellant_gauge_fusion_kernel(
         pages.append(tile([P, T2], F32, "page3", tag="w1_raw1"))
         for window in (budget[0], pages[3], budget[1]):
             nc.gpsimd.memset(window[:], 0.0)
-        got_sc = tile([P, S], U8, "got_sc")
-        nc.vector.tensor_copy(got_sc[:], tab_sc[:].indirect(idx1[:]))
-        got = [tile([P, S], U32, "got0", tag="tab_sc"), tile([P, S], U32, "got1", tag="tab0")]
+        got = [tile([P, S], U32, "got0"), tile([P, S], U32, "got1", tag="tab0")]
         nc.vector.tensor_copy(got[0][:], tab[0][:].indirect(idx1[:]))
+        got_sc = [tile([P, BANK], U8, "got_sc0")]
+        nc.vector.tensor_copy(got_sc[0][:], tab_sc[:].indirect(entries(idx1, 0, BANK)))
         for u in range(HALVES):
             j0, j1 = u * BANK, (u + 1) * BANK
             nc.vector.tensor_copy(got[1][:, j0:j1], tab[1][:].indirect(entries(idx1, j0, j1)))
+        got_sc.append(tile([P, BANK], U8, "got_sc1", tag="tab1"))
+        nc.vector.tensor_copy(got_sc[1][:], tab_sc[:].indirect(entries(idx1, BANK, S)))
 
         bell = [tile([P, S], F32, "bell%d" % t) for t in range(PACK)]
 
@@ -156,7 +165,7 @@ def tile_list_propellant_gauge_fusion_kernel(
                     lhsT=w1_codes[a][:, t * P : (t + 1) * P].bitcast(FP8X4),
                     lhsT_scale=w1_sc[a][:, t * P : (t + 1) * P],
                     rhs=got[a][:, j0:j1].bitcast(FP8X4),
-                    rhs_scale=got_sc[SCALE_ROWS * a : P, j0:j1],
+                    rhs_scale=got_sc[j0 // BANK][SCALE_ROWS * a : P, j0 % BANK : j0 % BANK + j1 - j0],
                     start=(a == 0),
                     stop=(a == PASSES - 1),
                 )
@@ -176,8 +185,8 @@ def tile_list_propellant_gauge_fusion_kernel(
         def place(t, j0, j1):
             nc.vector.tensor_copy(pages[t][:].indirect(entries(idx2, j0, j1)), bell[t][:, j0:j1])
 
-        acc = first_product(0, 0, LEAD, 0)
-        respond([(acc[:, j : j + P],) + (bell[0][:, j : j + P],) * 3 for j in range(0, LEAD, P)])
+        accs = [first_product(0, j, j + P, FIRST_BANKS * (j // P)) for j in range(0, LEAD, P)]
+        respond([(accs[j // P][:],) + (bell[0][:, j : j + P],) * 3 for j in range(0, LEAD, P)])
         weigh(nc.vector, 0, 0, LEAD)
         place(0, 0, LEAD)
         woven = [(1, 0, LEAD), (0, LEAD, BANK), (1, LEAD, BANK), (0, BANK, S), (1, BANK, S)]

@@ -63,23 +63,32 @@ def tile_list_propellant_gauge_fusion_kernel(
         def load_w1(a):
             nc.sync.dma_start(w1_raw[a][:], w1[K_PASS * a : K_PASS * (a + 1), :].rearrange("(p j) c -> p j c", j=PACK))
 
-        def load_tab(a):
-            nc.sync.dma_start(tab[a][:].bitcast(I32), tab_words[a].rearrange("p t i -> p (t i)").bitcast(I32))
-
-        def load_scales(rows):
-            for r in rows:
-                for a in range(PASSES):
-                    nc.sync.dma_start(
-                        tab_sc[SCALE_ROWS * a + r : P : QUAD, :].bitcast(I32), tab_scales[a, r::SCALE_ROWS, :].bitcast(I32)
-                    )
+        def load_tab(a, t0=0, t1=T):
+            words = tab_words[a].rearrange("p t i -> p (t i)").bitcast(I32)
+            nc.sync.dma_start(tab[a][:, t0:t1].bitcast(I32), words[:, t0:t1])
 
         load_w1(0)
+        nc.sync.dma_start(tab_sc[0:P:SCALE_ROWS, :].bitcast(I32), tab_scales.rearrange("a i t -> (a i) t").bitcast(I32))
         idx1 = load_list(offs, "idx1")
-        load_scales((0, 1))
+        spread_sc = tile([P, S], U8, "spread_sc")
+        nc.vector.tensor_copy(spread_sc[:], tab_sc[:].indirect(idx1[:]))
+        got_sc = [tile([P, S], U8, "got_sc%d" % a) for a in range(PASSES)]
+
+        def move_scales(a):
+            nc.vector.memset(got_sc[a][:].bitcast(I32), 0)
+            for r in range(SCALE_ROWS):
+                first = SCALE_ROWS * (QUADS * SCALE_ROWS * a + r)
+                step = SCALE_ROWS * SCALE_ROWS
+                nc.sync.dma_start(
+                    got_sc[a][r:P:QUAD, :].bitcast(I32), spread_sc[first : first + step * (QUADS - 1) + 1 : step, :].bitcast(I32)
+                )
+
         load_w1(1)
         load_tab(0)
-        load_scales((2, 3))
-        load_tab(1)
+        load_tab(1, 0, T // 2)
+        move_scales(0)
+        load_tab(1, T // 2, T)
+        move_scales(1)
         idx2 = load_list(offs2, "idx2")
         wgs_rows = wgs.rearrange("(i t) j -> t i j", t=PACK)
         wgs_sb = [tile([P, S], F32, "wgs%d" % t) for t in range(PACK)]
@@ -147,13 +156,9 @@ def tile_list_propellant_gauge_fusion_kernel(
             nc.gpsimd.memset(window[:], 0.0)
         got = [tile([P, S], U32, "got0"), tile([P, S], U32, "got1", tag="tab0")]
         nc.vector.tensor_copy(got[0][:], tab[0][:].indirect(idx1[:]))
-        got_sc = [tile([P, BANK], U8, "got_sc0")]
-        nc.vector.tensor_copy(got_sc[0][:], tab_sc[:].indirect(entries(idx1, 0, BANK)))
         for u in range(HALVES):
             j0, j1 = u * BANK, (u + 1) * BANK
             nc.vector.tensor_copy(got[1][:, j0:j1], tab[1][:].indirect(entries(idx1, j0, j1)))
-        got_sc.append(tile([P, BANK], U8, "got_sc1", tag="tab1"))
-        nc.vector.tensor_copy(got_sc[1][:], tab_sc[:].indirect(entries(idx1, BANK, S)))
 
         bell = [tile([P, S], F32, "bell%d" % t) for t in range(PACK)]
 
@@ -165,7 +170,7 @@ def tile_list_propellant_gauge_fusion_kernel(
                     lhsT=w1_codes[a][:, t * P : (t + 1) * P].bitcast(FP8X4),
                     lhsT_scale=w1_sc[a][:, t * P : (t + 1) * P],
                     rhs=got[a][:, j0:j1].bitcast(FP8X4),
-                    rhs_scale=got_sc[j0 // BANK][SCALE_ROWS * a : P, j0 % BANK : j0 % BANK + j1 - j0],
+                    rhs_scale=got_sc[a][:, j0:j1],
                     start=(a == 0),
                     stop=(a == PASSES - 1),
                 )
@@ -198,17 +203,15 @@ def tile_list_propellant_gauge_fusion_kernel(
 
         held_tags = {2: "after_plane2_%d", 3: "after_plane3_%d"}
         for t in range(2, PACK):
+            steps = []
             for u in range(HALVES):
-                j0, j1 = u * BANK, (u + 1) * BANK
-                acc = first_product(t, j0, j1, (HALVES * t + u + 2) % FIRST_BANKS)
-                result = bell[t][:, j0:j1]
-                if t in held_tags:
-                    square = tile([P, BANK], F32, "square%d_%d" % (t, u), tag=held_tags[t] % (2 * u))[:]
-                    root = tile([P, BANK], F32, "root%d_%d" % (t, u), tag=held_tags[t] % (2 * u + 1))[:]
-                else:
-                    square, root = result, result
-                respond([(acc[:], square, root, result)])
-                weigh(nc.gpsimd, t, j0, j1)
+                acc = first_product(t, u * BANK, (u + 1) * BANK, (HALVES * t + u + 2) % FIRST_BANKS)
+                square = tile([P, BANK], F32, "square%d_%d" % (t, u), tag=held_tags[t] % (2 * u))
+                root = tile([P, BANK], F32, "root%d_%d" % (t, u), tag=held_tags[t] % (2 * u + 1))
+                steps.append((acc[:], square[:], root[:], bell[t][:, u * BANK : (u + 1) * BANK]))
+            respond(steps)
+            for u in range(HALVES):
+                weigh(nc.gpsimd, t, u * BANK, (u + 1) * BANK)
             place(t, 0, S)
 
         edges = [0, P] + [BANK * (c + 1) for c in range(CHUNKS)]

@@ -70,6 +70,7 @@ def tile_list_propellant_gauge_fusion_kernel(
         load_w1(0)
         nc.sync.dma_start(tab_sc[0:P:SCALE_ROWS, :].bitcast(I32), tab_scales.rearrange("a i t -> (a i) t").bitcast(I32))
         idx1 = load_list(offs, "idx1")
+        idx2 = load_list(offs2, "idx2")
         spread_sc = tile([P, S], U8, "spread_sc")
         nc.vector.tensor_copy(spread_sc[:], tab_sc[:].indirect(idx1[:]))
         got_sc = [tile([P, S], U8, "got_sc%d" % a) for a in range(PASSES)]
@@ -89,9 +90,9 @@ def tile_list_propellant_gauge_fusion_kernel(
         move_scales(0)
         load_tab(1, T // 2, T)
         move_scales(1)
-        idx2 = load_list(offs2, "idx2")
         wgs_rows = wgs.rearrange("(i t) j -> t i j", t=PACK)
-        wgs_sb = [tile([P, S], F32, "wgs%d" % t) for t in range(PACK)]
+        wgs_first = tile([P, 2, S], F32, "wgs1")
+        wgs_sb = [wgs_first[:, 0, :], wgs_first[:, 1, :]] + [tile([P, S], F32, "wgs%d" % t)[:] for t in range(2, PACK)]
         limit_rows = limit.rearrange("(p t) c -> p t c", t=PACK)
         lim = [tile([P, PACK, BANK], F32, "lim%d" % c) for c in range(CHUNKS)]
 
@@ -102,16 +103,14 @@ def tile_list_propellant_gauge_fusion_kernel(
         def load_limit(c):
             nc.sync.dma_start(lim[c][:], limit_rows[:, :, c * BANK : (c + 1) * BANK])
 
-        for u in range(HALVES):
-            for t in range(2):
-                load_wgs(t, u * BANK, (u + 1) * BANK)
+        for j0, j1 in ((0, LEAD), (LEAD, BANK), (BANK, S)):
+            for q in (0, 2, 1, 3):
+                nc.sync.dma_start(wgs_first[QUAD * q : QUAD * (q + 1), :, j0:j1], wgs_rows.rearrange("t i j -> i t j")[:, 0:2, j0:j1])
         gain_sb = tile([P, PACK], F32, "gain_sb")
         nc.sync.dma_start(gain_sb[:], gain.rearrange("(p t) -> p t", t=PACK))
         bias_sb = tile([P, BLOCKS], F32, "bias_sb")
         with nc.allow_non_contiguous_dma(reason="one bias value for each partition and block"):
             nc.sync.dma_start(bias_sb[:], bias.rearrange("(b p) -> p b", p=P))
-        neg_bias = tile([P, BLOCKS], F32, "neg_bias")
-        nc.gpsimd.tensor_scalar(neg_bias[:], bias_sb[:], -1.0, None, ALU.mult)
         load_limit(0)
         w3_raw = tile([P, PACK, N], F32, "w3_raw")
         nc.sync.dma_start(w3_raw[:], w3.rearrange("(p j) c -> p j c", j=PACK))
@@ -191,21 +190,28 @@ def tile_list_propellant_gauge_fusion_kernel(
             nc.vector.tensor_copy(pages[t][:].indirect(entries(idx2, j0, j1)), bell[t][:, j0:j1])
 
         accs = [first_product(0, j, j + P, FIRST_BANKS * (j // P)) for j in range(0, LEAD, P)]
-        respond([(accs[j // P][:],) + (bell[0][:, j : j + P],) * 3 for j in range(0, LEAD, P)])
-        weigh(nc.vector, 0, 0, LEAD)
-        place(0, 0, LEAD)
+        work = tile([P, LEAD], F32, "work")
+        respond([(accs[j // P][:], work[:, j : j + P], work[:, j : j + P], bell[0][:, j : j + P]) for j in range(0, LEAD, P)])
+        nc.vector.tensor_tensor(pages[0][:].indirect(entries(idx2, 0, LEAD)), bell[0][:, :LEAD], wgs_sb[0][:, :LEAD], ALU.mult)
         woven = [(1, 0, LEAD), (0, LEAD, BANK), (1, LEAD, BANK), (0, BANK, S), (1, BANK, S)]
         for i, (t, j0, j1) in enumerate(woven):
             acc = first_product(t, j0, j1, (i + 1) % FIRST_BANKS)
-            respond([(acc[:],) + (bell[t][:, j0:j1],) * 3])
-            weigh(nc.gpsimd, t, j0, j1)
+            half = (j1 - j0) // 2
+            square = tile([P, j1 - j0], F32, "square_at%d" % i, tag="work")
+            cuts = [slice(h, h + half) for h in (0, half)]
+            respond([(acc[:, c], square[:, c]) + (bell[t][:, j0 + c.start : j0 + c.stop],) * 2 for c in cuts])
+            for j in range(j0, j1, LEAD):
+                weigh(nc.gpsimd if i else nc.vector, t, j, j + LEAD)
             place(t, j0, j1)
+
+        neg_bias = tile([P, BLOCKS], F32, "neg_bias", tag="work")
+        nc.gpsimd.tensor_scalar(neg_bias[:], bias_sb[:], -1.0, None, ALU.mult)
 
         held_tags = {2: "after_plane2_%d", 3: "after_plane3_%d"}
         for t in range(2, PACK):
             steps = []
             for u in range(HALVES):
-                acc = first_product(t, u * BANK, (u + 1) * BANK, (HALVES * t + u + 2) % FIRST_BANKS)
+                acc = first_product(t, u * BANK, (u + 1) * BANK, u)
                 square = tile([P, BANK], F32, "square%d_%d" % (t, u), tag=held_tags[t] % (2 * u))
                 root = tile([P, BANK], F32, "root%d_%d" % (t, u), tag=held_tags[t] % (2 * u + 1))
                 steps.append((acc[:], square[:], root[:], bell[t][:, u * BANK : (u + 1) * BANK]))
@@ -248,7 +254,7 @@ def tile_list_propellant_gauge_fusion_kernel(
         for c0, c1 in ((0, 2 * P), (2 * P, N)):
             nc.vector.quantize_mx(w3_codes[:, c0:c1].bitcast(FP8X4), w3_sc[:, c0:c1], w3_flat[:, PACK * c0 : PACK * c1])
 
-        z_tags = ("tab0", "w1_raw0", "wgs0", "z_grouped3")
+        z_tags = ("tab0", "w1_raw0", "z_grouped2", "z_grouped3")
         z_grouped = [tile([P, BANK, PACK], BF16, "z_grouped%d" % c, tag=z_tags[c]) for c in range(CHUNKS)]
         z_codes = tile([P, T2], U32, "z_codes")
         z_sc = [tile([P, BANK], U8, "z_sc%d" % c) for c in range(CHUNKS)]

@@ -207,22 +207,22 @@ def tile_list_propellant_gauge_fusion_kernel(
         neg_bias = tile([P, BLOCKS], F32, "neg_bias", tag="work")
         nc.gpsimd.tensor_scalar(neg_bias[:], bias_sb[:], -1.0, None, ALU.mult)
 
-        held_tags = {2: "after_plane2_%d", 3: "after_plane3_%d"}
         for t in range(2, PACK):
             steps = []
-            for u in range(HALVES):
-                acc = first_product(t, u * BANK, (u + 1) * BANK, u)
-                square = tile([P, BANK], F32, "square%d_%d" % (t, u), tag=held_tags[t] % (2 * u))
-                root = tile([P, BANK], F32, "root%d_%d" % (t, u), tag=held_tags[t] % (2 * u + 1))
-                steps.append((acc[:], square[:], root[:], bell[t][:, u * BANK : (u + 1) * BANK]))
+            width = BANK if t < PACK - 1 else LEAD
+            accs = [first_product(t, u * BANK, (u + 1) * BANK, u) for u in range(HALVES)]
+            for i, j in enumerate(range(0, S, width)):
+                square = tile([P, width], F32, "square%d_%d" % (t, i), tag="after_plane%d_%d" % (t, 2 * i))
+                root = tile([P, width], F32, "root%d_%d" % (t, i), tag="after_plane%d_%d" % (t, 2 * i + 1))
+                steps.append((accs[j // BANK][:, j % BANK : j % BANK + width], square[:], root[:], bell[t][:, j : j + width]))
             respond(steps)
             for u in range(HALVES):
                 weigh(nc.gpsimd, t, u * BANK, (u + 1) * BANK)
             place(t, 0, S)
 
-        edges = [0, P] + [BANK * (c + 1) for c in range(CHUNKS)]
+        edges = [0, P, 2 * P, 4 * P, 6 * P] + [BANK * c for c in range(2, CHUNKS + 1)]
         pieces = list(zip(edges[:-1], edges[1:]))
-        pair_tags = ["after_plane3_0", "after_plane2_2"] + ["after_plane3_%d" % c for c in range(1, CHUNKS)]
+        pair_tags = ["after_plane3_%d" % i for i in range(len(pieces))]
         pairs = [tile([P, 2, j1 - j0, 2], BF16, "pairs_at%d" % j0, tag=tag) for (j0, j1), tag in zip(pieces, pair_tags)]
         lim_late = tile([P, 2, 2, BANK, 2], BF16, "lim_late", tag="wgs3")
         lim_pairs = [tile([P, 2, BANK, 2], BF16, "lim_pairs%d" % c, tag="wgs%d" % (c + 1))[:] for c in range(2)]
@@ -302,12 +302,11 @@ def tile_list_propellant_gauge_fusion_kernel(
 
         for i in range(len(pieces)):
             round_page(PACK - 1, i)
-        clip(0)
-        clip(1)
-        for c in range(CHUNKS):
-            if c + 1 < CHUNKS:
-                clip(c + 2)
-            quantize(c)
+        for i, (j0, j1) in enumerate(pieces):
+            clip(i)
+            if j1 % BANK == 0 and j1 > BANK:
+                quantize(j1 // BANK - 2)
+        quantize(CHUNKS - 1)
         for c in range(CHUNKS):
             scores(0, c)
 

@@ -275,13 +275,13 @@ def tile_list_propellant_gauge_fusion_kernel(
                 z_codes[:, chunks[c]].bitcast(FP8X4), z_sc[c][:], z_grouped[c][:].rearrange("p c t -> p (c t)")
             )
 
-        def second_products(b, c):
-            y2 = psum.tile([P, BANK], F32, name="y2", tag="bank%d" % c)
+        def second_products(b, c, banks):
+            y2 = psum.tile([P, BANK], F32, name="y2", tag="bank%d" % banks[0])
             nc.tensor.matmul_mx(
                 y2[:], lhsT=w2_codes[:, 2 * P * b : 2 * P * (b + 1)].bitcast(FP4X4), lhsT_scale=w2_sc[:, P * b : P * (b + 1)],
                 rhs=z_codes[:, chunks[c]].bitcast(FP8X4), rhs_scale=z_sc[c][:], start=True, stop=True,
             )
-            y3 = psum.tile([P, BANK], F32, name="y3", tag="bank%d" % (CHUNKS + c))
+            y3 = psum.tile([P, BANK], F32, name="y3", tag="bank%d" % banks[1])
             nc.tensor.matmul_mx(
                 y3[:], lhsT=w3_codes[:, P * b : P * (b + 1)].bitcast(FP8X4), lhsT_scale=w3_sc[:, P * b : P * (b + 1)],
                 rhs=z_codes[:, chunks[c]].bitcast(FP8X4), rhs_scale=z_sc[c][:], start=True, stop=True,
@@ -291,10 +291,10 @@ def tile_list_propellant_gauge_fusion_kernel(
         def less_bias(dst, sums, b):
             nc.scalar.activation(dst, sums[:], ACT.Identity, bias=neg_bias[:, b : b + 1])
 
-        score = [tile([P, T2], F32, "score0", tag="w1_raw1"), tile([P, T2], F32, "score1", tag="page0")]
+        score = [tile([P, T2], F32, "score0", tag="w1_raw1")[:], tile([P, T2], F32, "score1", tag="page0")[:]]
 
         def scores(b, c):
-            y2, y3 = second_products(b, c)
+            y2, y3 = second_products(b, c, (c, CHUNKS + c))
             less_bias(score[b][:, chunks[c]], y2, b)
             nc.vector.scalar_tensor_tensor(
                 score[b][:, chunks[c]], y3[:], bias_sb[:, b : b + 1], score[b][:, chunks[c]], ALU.subtract, ALU.max
@@ -310,10 +310,11 @@ def tile_list_propellant_gauge_fusion_kernel(
         for c in range(CHUNKS):
             scores(0, c)
 
-        picked = [tile([P, S], F32, "picked%d" % b, tag=tag) for b, tag in enumerate(("bell0", "tab1", "bell2"))]
+        shared = tile([P, LEAD + T2], F32, "shared", tag="tab1")
+        picked = [tile([P, S], F32, "picked0", tag="bell0")[:], shared[:, :S], tile([P, S], F32, "picked2", tag="bell2")[:]]
 
         def pick(b):
-            nc.vector.tensor_copy(picked[b][:], score[b][:].indirect(idx3[:]))
+            nc.vector.tensor_copy(picked[b], score[b].indirect(idx3[:]))
 
         def put(b, values, j0, j1):
             nc.vector.tensor_copy(budget[b][:].indirect(entries(idx4, j0, j1)), values[:, j0:j1])
@@ -336,7 +337,7 @@ def tile_list_propellant_gauge_fusion_kernel(
         first_score = tile([P, T2], F32, "first_score", tag="page1")
         second_score = [tile([P, T2], F32, "second_score%d" % u, tag="lim%d" % u) for u in range(2)]
         for c in range(CHUNKS):
-            y2, y3 = second_products(last, c)
+            y2, y3 = second_products(last, c, (2 * c % CHUNKS, (2 * c + 1) % CHUNKS))
             less_bias(first_score[:, chunks[c]], y2, last)
             less_bias(second_score[c // 2][:, chunks[c]], y3, last)
         excess = tile([P, T2], F32, "excess", tag="lim2")
@@ -349,15 +350,18 @@ def tile_list_propellant_gauge_fusion_kernel(
             nc.scalar.activation(excess[:, cols], excess[:, cols], ACT.Relu)
 
         make_excess(0)
-        weighted = tile([P, S], F32, "weighted", tag="lim0")
-        nc.gpsimd.tensor_tensor(weighted[:], picked[1][:], wgo_sb[:], ALU.mult)
         make_excess(1)
-        score.append(tile([P, T2], F32, "score2", tag="tab1"))
+        weighted = tile([P, S], F32, "weighted", tag="lim1")
+        nc.gpsimd.tensor_tensor(weighted[:, LEAD:], picked[1][:, LEAD:], wgo_sb[:, LEAD:], ALU.mult)
+        score.append(shared[:, LEAD:])
         for cols in wide:
             nc.gpsimd.tensor_tensor(score[last][:, cols], first_score[:, cols], excess[:, cols], ALU.add)
-        put(1, weighted, 0, S)
+        put(1, weighted, LEAD, S)
+        pick(last)
+        rest = tile([P, LEAD], F32, "rest", tag="lim2")
+        nc.gpsimd.tensor_tensor(rest[:], picked[1][:, :LEAD], wgo_sb[:, :LEAD], ALU.mult)
+        put(1, rest, 0, LEAD)
         store(1)
 
-        pick(last)
-        nc.vector.tensor_tensor(budget[last][:].indirect(idx4[:]), picked[last][:], wgo_sb[:], ALU.mult)
+        nc.vector.tensor_tensor(budget[last][:].indirect(idx4[:]), picked[last], wgo_sb[:], ALU.mult)
         store(last)

@@ -1,6 +1,7 @@
 from contextlib import ExitStack
 
 import concourse.mybir as mybir
+from concourse.masks import make_identity
 
 K, T, H, N, S, T2 = 1024, 4096, 512, 384, 1024, 2048
 FLOPS = 2 * K * H * S + 2 * 2 * H * N * T2
@@ -29,6 +30,9 @@ HALVES = S // BANK
 CHUNKS = T2 // BANK
 BLOCKS = N // P
 LEAD = BANK // 2
+TAB_CUT = 5 * T // 8
+LENT = 2
+LENT_CHUNKS = (0, CHUNKS - 1)
 FIRST_BANKS = 4
 
 
@@ -39,10 +43,14 @@ def tile_list_propellant_gauge_fusion_kernel(
     with ExitStack() as ctx:
         lists = ctx.enter_context(tc.tile_pool(name="lists", bufs=1))
         sb = ctx.enter_context(tc.tile_pool(name="sb", bufs=1))
+        last_page = ctx.enter_context(tc.tile_pool(name="last_page", bufs=1))
         psum = ctx.enter_context(tc.psum_pool(name="psum", bufs=1))
 
         def tile(shape, dtype, name, tag=None):
             return sb.tile(shape, dtype, name=name, tag=tag or name, align_bytes=64)
+
+        def on_last_page(shape, dtype, name, offset):
+            return last_page.tile(shape, dtype, name=name, align_bytes=64, offset=offset)
 
         def load_list(src, name):
             held = lists.tile([P, S // PER_COLUMN], U16, name=name)
@@ -57,8 +65,10 @@ def tile_list_propellant_gauge_fusion_kernel(
         warm = tile([P, 2], F32, "warm")
         nc.vector.memset(warm[:, 0:1], 1.0)
         nc.scalar.activation(warm[:, 1:2], warm[:, 0:1], ACT.Abs_reciprocal_sqrt)
+        ident = tile([P, P], F32, "ident")
+        make_identity(nc, ident[:])
         tab = [tile([P, T], U32, "tab%d" % a) for a in range(PASSES)]
-        w1_raw = [tile([P, PACK, H], F32, "w1_raw%d" % a) for a in range(PASSES)]
+        w1_raw = [tile([P, PACK, H], F32, "w1_raw0"), on_last_page([P, PACK, H], F32, "w1_raw1", 0)]
 
         def load_w1(a):
             nc.sync.dma_start(w1_raw[a][:], w1[K_PASS * a : K_PASS * (a + 1), :].rearrange("(p j) c -> p j c", j=PACK))
@@ -70,7 +80,6 @@ def tile_list_propellant_gauge_fusion_kernel(
         load_w1(0)
         nc.sync.dma_start(tab_sc[0:P:SCALE_ROWS, :].bitcast(I32), tab_scales.rearrange("a i t -> (a i) t").bitcast(I32))
         idx1 = load_list(offs, "idx1")
-        idx2 = load_list(offs2, "idx2")
         spread_sc = tile([P, S], U8, "spread_sc")
         nc.vector.tensor_copy(spread_sc[:], tab_sc[:].indirect(idx1[:]))
         got_sc = [tile([P, S], U8, "got_sc%d" % a) for a in range(PASSES)]
@@ -86,10 +95,11 @@ def tile_list_propellant_gauge_fusion_kernel(
 
         load_w1(1)
         load_tab(0)
-        load_tab(1, 0, T // 2)
         move_scales(0)
-        load_tab(1, T // 2, T)
+        load_tab(1, 0, TAB_CUT)
         move_scales(1)
+        load_tab(1, TAB_CUT, T)
+        idx2 = load_list(offs2, "idx2")
         wgs_rows = wgs.rearrange("(i t) j -> t i j", t=PACK)
         wgs_first = tile([P, 2, S], F32, "wgs1")
         wgs_sb = [wgs_first[:, 0, :], wgs_first[:, 1, :]] + [tile([P, S], F32, "wgs%d" % t)[:] for t in range(2, PACK)]
@@ -119,7 +129,7 @@ def tile_list_propellant_gauge_fusion_kernel(
             load_limit(t - 1)
         load_limit(CHUNKS - 1)
 
-        pages = [tile([P, T2], F32, "page%d" % t) for t in range(PACK - 1)]
+        pages = [tile([P, T2], F32, "page%d" % t, tag="tab_sc" if t == 1 else None) for t in range(PACK - 1)]
         for t in range(PACK - 1):
             nc.vector.memset(pages[t][:].bitcast(I32), 0)
         w2_sc = tile([P, N], U8, "w2_sc")
@@ -150,13 +160,12 @@ def tile_list_propellant_gauge_fusion_kernel(
             w1_codes.append(codes)
             w1_sc.append(sc)
         budget = [tile([P, T2], F32, "budget%d" % b, tag="w1_grouped%d" % b) for b in range(2)]
-        pages.append(tile([P, T2], F32, "page3", tag="w1_raw1"))
+        pages.append(on_last_page([P, T2], F32, "page3", 0))
         for window in (budget[0], pages[3], budget[1]):
             nc.gpsimd.memset(window[:], 0.0)
         got = [tile([P, S], U32, "got0"), tile([P, S], U32, "got1", tag="tab0")]
         nc.vector.tensor_copy(got[0][:], tab[0][:].indirect(idx1[:]))
-        for u in range(HALVES):
-            j0, j1 = u * BANK, (u + 1) * BANK
+        for j0, j1 in ((0, LEAD), (LEAD, S)):
             nc.vector.tensor_copy(got[1][:, j0:j1], tab[1][:].indirect(entries(idx1, j0, j1)))
 
         bell = [tile([P, S], F32, "bell%d" % t) for t in range(PACK)]
@@ -203,9 +212,6 @@ def tile_list_propellant_gauge_fusion_kernel(
             for j in range(j0, j1, LEAD):
                 weigh(nc.gpsimd if i else nc.vector, t, j, j + LEAD)
             place(t, j0, j1)
-
-        neg_bias = tile([P, BLOCKS], F32, "neg_bias", tag="work")
-        nc.gpsimd.tensor_scalar(neg_bias[:], bias_sb[:], -1.0, None, ALU.mult)
 
         for t in range(2, PACK):
             steps = []
@@ -257,7 +263,7 @@ def tile_list_propellant_gauge_fusion_kernel(
         z_tags = ("tab0", "w1_raw0", "z_grouped2", "z_grouped3")
         z_grouped = [tile([P, BANK, PACK], BF16, "z_grouped%d" % c, tag=z_tags[c]) for c in range(CHUNKS)]
         z_codes = tile([P, T2], U32, "z_codes")
-        z_sc = [tile([P, BANK], U8, "z_sc%d" % c) for c in range(CHUNKS)]
+        z_sc = [on_last_page([P, BANK], U8, "z_sc2", 0) if c == 2 else tile([P, BANK], U8, "z_sc%d" % c) for c in range(CHUNKS)]
         chunks = [slice(c * BANK, (c + 1) * BANK) for c in range(CHUNKS)]
 
         def clip(i):
@@ -275,93 +281,145 @@ def tile_list_propellant_gauge_fusion_kernel(
                 z_codes[:, chunks[c]].bitcast(FP8X4), z_sc[c][:], z_grouped[c][:].rearrange("p c t -> p (c t)")
             )
 
-        def second_products(b, c, banks):
-            y2 = psum.tile([P, BANK], F32, name="y2", tag="bank%d" % banks[0])
+        def product(b, c, codes, sc, dtype, width, bank):
+            y = psum.tile([P, BANK], F32, name="y", tag="bank%d" % bank)
             nc.tensor.matmul_mx(
-                y2[:], lhsT=w2_codes[:, 2 * P * b : 2 * P * (b + 1)].bitcast(FP4X4), lhsT_scale=w2_sc[:, P * b : P * (b + 1)],
+                y[:], lhsT=codes[:, width * P * b : width * P * (b + 1)].bitcast(dtype), lhsT_scale=sc[:, P * b : P * (b + 1)],
                 rhs=z_codes[:, chunks[c]].bitcast(FP8X4), rhs_scale=z_sc[c][:], start=True, stop=True,
             )
-            y3 = psum.tile([P, BANK], F32, name="y3", tag="bank%d" % banks[1])
-            nc.tensor.matmul_mx(
-                y3[:], lhsT=w3_codes[:, P * b : P * (b + 1)].bitcast(FP8X4), lhsT_scale=w3_sc[:, P * b : P * (b + 1)],
-                rhs=z_codes[:, chunks[c]].bitcast(FP8X4), rhs_scale=z_sc[c][:], start=True, stop=True,
-            )
-            return y2, y3
+            return y
+
+        def first(b, c, bank):
+            return product(b, c, w2_codes, w2_sc, FP4X4, 2, bank)
+
+        def second(b, c, bank):
+            return product(b, c, w3_codes, w3_sc, FP8X4, 1, bank)
 
         def less_bias(dst, sums, b):
-            nc.scalar.activation(dst, sums[:], ACT.Identity, bias=neg_bias[:, b : b + 1])
+            nc.scalar.activation(dst, sums[:], ACT.Identity, bias=neg_bias[b])
 
-        score = [tile([P, T2], F32, "score0", tag="w1_raw1")[:], tile([P, T2], F32, "score1", tag="page0")[:]]
-
-        def scores(b, c):
-            y2, y3 = second_products(b, c, (c, CHUNKS + c))
-            less_bias(score[b][:, chunks[c]], y2, b)
+        def larger(b, c, y3):
             nc.vector.scalar_tensor_tensor(
-                score[b][:, chunks[c]], y3[:], bias_sb[:, b : b + 1], score[b][:, chunks[c]], ALU.subtract, ALU.max
+                score[b][:, chunks[c]], y3[:], bias_sb[:, b : b + 1], lead[b][:, chunks[c]], ALU.subtract, ALU.max
             )
+
+        score = [tile([P, T2], F32, "score0", tag="z_grouped2"), tile([P, T2], F32, "score1", tag="page0")]
+        lead = [tile([P, T2], F32, "lead0", tag="page2"), score[1]]
+        other = tile([P, LENT * BANK], F32, "other", tag="bell1")
+        held = []
 
         for i in range(len(pieces)):
             round_page(PACK - 1, i)
+        neg_first = on_last_page([P, 1], F32, "neg_first", 2 * BANK)
+        nc.scalar.activation(neg_first[:], bias_sb[:, :1], ACT.Copy, scale=-1.0)
+        neg_rest = on_last_page([P, BLOCKS - 1], F32, "neg_rest", BANK)
+        nc.scalar.activation(neg_rest[:], bias_sb[:, 1:], ACT.Copy, scale=-1.0)
+        neg_bias = [neg_first[:]] + [neg_rest[:, b : b + 1] for b in range(BLOCKS - 1)]
         for i, (j0, j1) in enumerate(pieces):
             clip(i)
-            if j1 % BANK == 0 and j1 > BANK:
-                quantize(j1 // BANK - 2)
+            if j0 % BANK == 0 and j0 >= BANK:
+                quantize(j0 // BANK - 1)
         quantize(CHUNKS - 1)
+        less_bias(lead[0][:, chunks[0]], first(0, 0, 0), 0)
+        less_bias(score[1][:, chunks[0]], first(1, 0, 1), 1)
+        less_bias(other[:, chunks[0]], second(1, 0, 2), 1)
+        held.append(second(0, 0, 7))
+        less_bias(lead[0][:, chunks[1]], first(0, 1, 3), 0)
+        less_bias(score[1][:, chunks[1]], first(1, 1, 4), 1)
+        held.append(second(0, 1, 5))
+        less_bias(lead[0][:, chunks[2]], first(0, 2, 6), 0)
+        less_bias(lead[0][:, chunks[3]], first(0, 3, 0), 0)
+        held.append(second(0, 2, 3))
+        held.append(second(0, 3, 4))
         for c in range(CHUNKS):
-            scores(0, c)
+            larger(0, c, held[c])
 
-        shared = tile([P, LEAD + T2], F32, "shared", tag="tab1")
-        picked = [tile([P, S], F32, "picked0", tag="bell0")[:], shared[:, :S], tile([P, S], F32, "picked2", tag="bell2")[:]]
+        excess1 = [tile([P, BANK], F32, "excess1_%d" % c, tag=tag) for c, tag in enumerate(("z_grouped3", "bell0"))]
+
+        above = [on_last_page([P, BANK], F32, "above0", 2 * BANK), excess1[1]]
+
+        def lent_difference(c):
+            nc.gpsimd.tensor_tensor(excess1[c][:], other[:, chunks[c]], score[1][:, chunks[LENT_CHUNKS[c]]], ALU.subtract)
+
+        def lent_relu(c):
+            nc.scalar.activation(above[c][:], excess1[c][:], ACT.Relu)
+
+        def lent_sum(c):
+            cols = score[1][:, chunks[LENT_CHUNKS[c]]]
+            nc.gpsimd.tensor_tensor(cols, cols, above[c][:], ALU.add)
+
+        halves = [tile([P, BANK], F32, "picked0_%d" % u, tag=tag) for u, tag in enumerate(("bell0", "picked0_1"))]
+        picked = [None, tile([P, S], F32, "picked1", tag="tab0"), tile([P, S], F32, "picked2", tag="bell2")]
 
         def pick(b):
-            nc.vector.tensor_copy(picked[b], score[b].indirect(idx3[:]))
+            nc.vector.tensor_copy(picked[b][:], score[b][:].indirect(idx3[:]))
+
+        def pick_half(u):
+            nc.vector.tensor_copy(halves[u][:], score[0][:].indirect(entries(idx3, u * BANK, (u + 1) * BANK)))
 
         def put(b, values, j0, j1):
-            nc.vector.tensor_copy(budget[b][:].indirect(entries(idx4, j0, j1)), values[:, j0:j1])
+            nc.vector.tensor_copy(budget[b][:].indirect(entries(idx4, j0, j1)), values)
 
         def store(b):
             nc.sync.dma_start(out[b * P : (b + 1) * P, :], budget[b][:])
 
-        scores(1, 0)
-        pick(0)
-        for j0, j1 in ((0, LEAD), (LEAD, S)):
-            nc.gpsimd.tensor_tensor(picked[0][:, j0:j1], picked[0][:, j0:j1], wgo_sb[:, j0:j1], ALU.mult)
-        for c in range(1, CHUNKS):
-            scores(1, c)
-        put(0, picked[0], 0, LEAD)
+        weighted0 = [tile([P, BANK], F32, "weighted0_%d" % u, tag=tag) for u, tag in enumerate(("page2", "bell0"))]
+
+        def weigh_picked(u):
+            nc.gpsimd.tensor_tensor(weighted0[u][:], halves[u][:], wgo_sb[:, chunks[u]], ALU.mult)
+
+        lent_difference(0)
+        lent_relu(0)
+        lent_sum(0)
+        larger(1, 1, second(1, 1, 7))
+        pick_half(0)
+        less_bias(score[1][:, chunks[2]], first(1, 2, 0), 1)
+        larger(1, 2, second(1, 2, 5))
+        pick_half(1)
+        less_bias(score[1][:, chunks[3]], first(1, 3, 3), 1)
+        less_bias(other[:, chunks[1]], second(1, 3, 4), 1)
+        weigh_picked(0)
+        put(0, weighted0[0][:], 0, BANK)
+        lent_difference(1)
+        lent_relu(1)
+        lent_sum(1)
+        weigh_picked(1)
         pick(1)
-        put(0, picked[0], LEAD, S)
+        put(0, weighted0[1][:], BANK, S)
         store(0)
+        weighted1 = tile([P, S], F32, "weighted1", tag="w1_raw0")
+        nc.gpsimd.tensor_tensor(weighted1[:, LEAD:], picked[1][:, LEAD:], wgo_sb[:, LEAD:], ALU.mult)
 
         last = BLOCKS - 1
-        first_score = tile([P, T2], F32, "first_score", tag="page1")
-        second_score = [tile([P, T2], F32, "second_score%d" % u, tag="lim%d" % u) for u in range(2)]
-        for c in range(CHUNKS):
-            y2, y3 = second_products(last, c, (2 * c % CHUNKS, (2 * c + 1) % CHUNKS))
-            less_bias(first_score[:, chunks[c]], y2, last)
-            less_bias(second_score[c // 2][:, chunks[c]], y3, last)
+        first_score = tile([P, T2], F32, "first_score", tag="tab_sc")
+        minus_second = tile([P, T2], F32, "minus_second", tag="lim0")
+        turned = tile([P, T2], F32, "turned", tag="lim1")
         excess = tile([P, T2], F32, "excess", tag="lim2")
-
-        wide = [slice(u * T2 // 2, (u + 1) * T2 // 2) for u in range(2)]
-
-        def make_excess(u):
-            cols = wide[u]
-            nc.gpsimd.tensor_tensor(excess[:, cols], second_score[u][:, cols], first_score[:, cols], ALU.subtract)
-            nc.scalar.activation(excess[:, cols], excess[:, cols], ACT.Relu)
-
-        make_excess(0)
-        make_excess(1)
-        weighted = tile([P, S], F32, "weighted", tag="lim1")
-        nc.gpsimd.tensor_tensor(weighted[:, LEAD:], picked[1][:, LEAD:], wgo_sb[:, LEAD:], ALU.mult)
-        score.append(shared[:, LEAD:])
-        for cols in wide:
+        score.append(tile([P, T2], F32, "score2", tag="tab1"))
+        for c in range(CHUNKS):
+            less_bias(first_score[:, chunks[c]], first(last, c, (0, 3)[c % 2]), last)
+            nc.scalar.activation(
+                minus_second[:, chunks[c]], second(last, c, (7, 4)[c % 2])[:], ACT.Identity, bias=bias_sb[:, last : last + 1], scale=-1.0
+            )
+        for c in range(CHUNKS):
+            gap = psum.tile([P, BANK], F32, name="gap", tag="bank%d" % (1 + c % 2))
+            for j in range(0, BANK, P):
+                cols = slice(c * BANK + j, c * BANK + j + P)
+                nc.tensor.matmul(gap[:, j : j + P], first_score[:, cols], ident[:], start=True, stop=False, is_transpose=True)
+                nc.tensor.matmul(gap[:, j : j + P], minus_second[:, cols], ident[:], start=False, stop=True, is_transpose=True)
+            nc.scalar.activation(turned[:, chunks[c]], gap[:], ACT.Relu, scale=-1.0)
+            back = psum.tile([P, BANK], F32, name="back", tag="bank%d" % (5 + c % 2))
+            for j in range(0, BANK, P):
+                nc.tensor.transpose(back[:, j : j + P], turned[:, c * BANK + j : c * BANK + j + P], ident[:])
+            nc.scalar.copy(excess[:, chunks[c]], back[:])
+        for cols in chunks:
             nc.gpsimd.tensor_tensor(score[last][:, cols], first_score[:, cols], excess[:, cols], ALU.add)
-        put(1, weighted, LEAD, S)
+        put(1, weighted1[:, LEAD:], LEAD, S)
         pick(last)
         rest = tile([P, LEAD], F32, "rest", tag="lim2")
         nc.gpsimd.tensor_tensor(rest[:], picked[1][:, :LEAD], wgo_sb[:, :LEAD], ALU.mult)
-        put(1, rest, 0, LEAD)
+        put(1, rest[:], 0, LEAD)
         store(1)
 
-        nc.vector.tensor_tensor(budget[last][:].indirect(idx4[:]), picked[last], wgo_sb[:], ALU.mult)
+        nc.vector.tensor_tensor(budget[last][:].indirect(idx4[:]), picked[last][:], wgo_sb[:], ALU.mult)
         store(last)

@@ -305,7 +305,7 @@ def tile_list_propellant_gauge_fusion_kernel(
 
         score = [tile([P, T2], F32, "score0", tag="z_grouped2"), tile([P, T2], F32, "score1", tag="page0")]
         lead = [tile([P, T2], F32, "lead0", tag="page2"), score[1]]
-        other = tile([P, LENT * BANK], F32, "other", tag="bell1")
+        other = [tile([P, BANK], F32, "other%d" % c, tag=tag) for c, tag in enumerate(("bell1", "w1_codes0"))]
         held = []
 
         for i in range(len(pieces)):
@@ -322,7 +322,7 @@ def tile_list_propellant_gauge_fusion_kernel(
         quantize(CHUNKS - 1)
         less_bias(lead[0][:, chunks[0]], first(0, 0, 0), 0)
         less_bias(score[1][:, chunks[0]], first(1, 0, 1), 1)
-        less_bias(other[:, chunks[0]], second(1, 0, 2), 1)
+        less_bias(other[0][:], second(1, 0, 2), 1)
         held.append(second(0, 0, 7))
         less_bias(lead[0][:, chunks[1]], first(0, 1, 3), 0)
         less_bias(score[1][:, chunks[1]], first(1, 1, 4), 1)
@@ -334,19 +334,18 @@ def tile_list_propellant_gauge_fusion_kernel(
         for c in range(CHUNKS):
             larger(0, c, held[c])
 
-        excess1 = [tile([P, BANK], F32, "excess1_%d" % c, tag=tag) for c, tag in enumerate(("z_grouped3", "bell0"))]
+        excess1 = [tile([P, BANK], F32, "excess1_%d" % c, tag=tag) for c, tag in enumerate(("z_grouped3", "w1_codes1"))]
 
-        above = [on_last_page([P, BANK], F32, "above0", 2 * BANK), excess1[1]]
 
         def lent_difference(c):
-            nc.gpsimd.tensor_tensor(excess1[c][:], other[:, chunks[c]], score[1][:, chunks[LENT_CHUNKS[c]]], ALU.subtract)
+            nc.gpsimd.tensor_tensor(excess1[c][:], other[c][:], score[1][:, chunks[LENT_CHUNKS[c]]], ALU.subtract)
 
         def lent_relu(c):
-            nc.scalar.activation(above[c][:], excess1[c][:], ACT.Relu)
+            nc.gpsimd.tensor_scalar(excess1[c][:], excess1[c][:], float("inf"), 0.0, ALU.min, ALU.max)
 
         def lent_sum(c):
             cols = score[1][:, chunks[LENT_CHUNKS[c]]]
-            nc.gpsimd.tensor_tensor(cols, cols, above[c][:], ALU.add)
+            nc.gpsimd.tensor_tensor(cols, cols, excess1[c][:], ALU.add)
 
         halves = [tile([P, BANK], F32, "picked0_%d" % u, tag=tag) for u, tag in enumerate(("bell0", "picked0_1"))]
         picked = [None, tile([P, S], F32, "picked1", tag="tab0"), tile([P, S], F32, "picked2", tag="bell2")]
@@ -363,7 +362,7 @@ def tile_list_propellant_gauge_fusion_kernel(
         def store(b):
             nc.sync.dma_start(out[b * P : (b + 1) * P, :], budget[b][:])
 
-        weighted0 = [tile([P, BANK], F32, "weighted0_%d" % u, tag=tag) for u, tag in enumerate(("page2", "bell0"))]
+        weighted0 = [tile([P, BANK], F32, "weighted0_%d" % u, tag=tag) for u, tag in enumerate(("page2", "w1_codes1"))]
 
         def weigh_picked(u):
             nc.gpsimd.tensor_tensor(weighted0[u][:], halves[u][:], wgo_sb[:, chunks[u]], ALU.mult)
@@ -377,7 +376,7 @@ def tile_list_propellant_gauge_fusion_kernel(
         larger(1, 2, second(1, 2, 5))
         pick_half(1)
         less_bias(score[1][:, chunks[3]], first(1, 3, 3), 1)
-        less_bias(other[:, chunks[1]], second(1, 3, 4), 1)
+        less_bias(other[1][:], second(1, 3, 4), 1)
         weigh_picked(0)
         put(0, weighted0[0][:], 0, BANK)
         lent_difference(1)
@@ -388,35 +387,44 @@ def tile_list_propellant_gauge_fusion_kernel(
         put(0, weighted0[1][:], BANK, S)
         store(0)
         weighted1 = tile([P, S], F32, "weighted1", tag="w1_raw0")
-        nc.gpsimd.tensor_tensor(weighted1[:, LEAD:], picked[1][:, LEAD:], wgo_sb[:, LEAD:], ALU.mult)
 
         last = BLOCKS - 1
         first_score = tile([P, T2], F32, "first_score", tag="tab_sc")
         minus_second = tile([P, T2], F32, "minus_second", tag="lim0")
         turned = tile([P, T2], F32, "turned", tag="lim1")
-        excess = tile([P, T2], F32, "excess", tag="lim2")
+        excess = [tile([P, BANK], F32, "excess%d" % c, tag=tag) for c, tag in enumerate(("w1_raw0", "lim2", "got0", "wgs2"))]
         score.append(tile([P, T2], F32, "score2", tag="tab1"))
-        for c in range(CHUNKS):
+
+        def copy_out(c):
             less_bias(first_score[:, chunks[c]], first(last, c, (0, 3)[c % 2]), last)
             nc.scalar.activation(
                 minus_second[:, chunks[c]], second(last, c, (7, 4)[c % 2])[:], ACT.Identity, bias=bias_sb[:, last : last + 1], scale=-1.0
             )
-        for c in range(CHUNKS):
+
+        def turn(c):
             gap = psum.tile([P, BANK], F32, name="gap", tag="bank%d" % (1 + c % 2))
             for j in range(0, BANK, P):
                 cols = slice(c * BANK + j, c * BANK + j + P)
                 nc.tensor.matmul(gap[:, j : j + P], first_score[:, cols], ident[:], start=True, stop=False, is_transpose=True)
                 nc.tensor.matmul(gap[:, j : j + P], minus_second[:, cols], ident[:], start=False, stop=True, is_transpose=True)
             nc.scalar.activation(turned[:, chunks[c]], gap[:], ACT.Relu, scale=-1.0)
+
+        def turn_back(c):
             back = psum.tile([P, BANK], F32, name="back", tag="bank%d" % (5 + c % 2))
             for j in range(0, BANK, P):
                 nc.tensor.transpose(back[:, j : j + P], turned[:, c * BANK + j : c * BANK + j + P], ident[:])
-            nc.scalar.copy(excess[:, chunks[c]], back[:])
-        for cols in chunks:
-            nc.gpsimd.tensor_tensor(score[last][:, cols], first_score[:, cols], excess[:, cols], ALU.add)
+            nc.scalar.copy(excess[c][:], back[:])
+            nc.gpsimd.tensor_tensor(score[last][:, chunks[c]], first_score[:, chunks[c]], excess[c][:], ALU.add)
+            if c == 0:
+                nc.gpsimd.tensor_tensor(weighted1[:, LEAD:], picked[1][:, LEAD:], wgo_sb[:, LEAD:], ALU.mult)
+
+        for step in range(CHUNKS + 2):
+            for stage, c in ((turn_back, step - 2), (turn, step - 1), (copy_out, step)):
+                if 0 <= c < CHUNKS:
+                    stage(c)
         put(1, weighted1[:, LEAD:], LEAD, S)
         pick(last)
-        rest = tile([P, LEAD], F32, "rest", tag="lim2")
+        rest = tile([P, LEAD], F32, "rest", tag="wgs2")
         nc.gpsimd.tensor_tensor(rest[:], picked[1][:, :LEAD], wgo_sb[:, :LEAD], ALU.mult)
         put(1, rest[:], 0, LEAD)
         store(1)

@@ -33,6 +33,8 @@ LEAD = BANK // 2
 TAB_CUT = 5 * T // 8
 LENT = 2
 LENT_CHUNKS = (0, CHUNKS - 1)
+EARLY = 256
+MIDDLE = 640
 FIRST_BANKS = 4
 
 
@@ -347,14 +349,16 @@ def tile_list_propellant_gauge_fusion_kernel(
             cols = score[1][:, chunks[LENT_CHUNKS[c]]]
             nc.gpsimd.tensor_tensor(cols, cols, excess1[c][:], ALU.add)
 
-        halves = [tile([P, BANK], F32, "picked0_%d" % u, tag=tag) for u, tag in enumerate(("bell0", "picked0_1"))]
+        parts = [slice(0, EARLY), slice(EARLY, MIDDLE), slice(MIDDLE, S)]
+        halves = tile([P, S], F32, "picked0", tag="bell0")
         picked = [None, tile([P, S], F32, "picked1", tag="tab0"), tile([P, S], F32, "picked2", tag="bell2")]
 
         def pick(b):
             nc.vector.tensor_copy(picked[b][:], score[b][:].indirect(idx3[:]))
 
         def pick_half(u):
-            nc.vector.tensor_copy(halves[u][:], score[0][:].indirect(entries(idx3, u * BANK, (u + 1) * BANK)))
+            cut = (parts[0], slice(EARLY, S))[u]
+            nc.vector.tensor_copy(halves[:, cut], score[0][:].indirect(entries(idx3, cut.start, cut.stop)))
 
         def put(b, values, j0, j1):
             nc.vector.tensor_copy(budget[b][:].indirect(entries(idx4, j0, j1)), values)
@@ -362,29 +366,34 @@ def tile_list_propellant_gauge_fusion_kernel(
         def store(b):
             nc.sync.dma_start(out[b * P : (b + 1) * P, :], budget[b][:])
 
-        weighted0 = [tile([P, BANK], F32, "weighted0_%d" % u, tag=tag) for u, tag in enumerate(("page2", "w1_codes1"))]
+        weighted0 = [
+            tile([P, cut.stop - cut.start], F32, "weighted0_%d" % cut.start, tag=tag)
+            for cut, tag in zip(parts, ("page2", "w1_codes0", "w1_codes1"))
+        ]
 
         def weigh_picked(u):
-            nc.gpsimd.tensor_tensor(weighted0[u][:], halves[u][:], wgo_sb[:, chunks[u]], ALU.mult)
+            nc.gpsimd.tensor_tensor(weighted0[u][:], halves[:, parts[u]], wgo_sb[:, parts[u]], ALU.mult)
 
         lent_difference(0)
         lent_relu(0)
         lent_sum(0)
         larger(1, 1, second(1, 1, 7))
-        pick_half(0)
         less_bias(score[1][:, chunks[2]], first(1, 2, 0), 1)
         larger(1, 2, second(1, 2, 5))
+        pick_half(0)
         pick_half(1)
         less_bias(score[1][:, chunks[3]], first(1, 3, 3), 1)
         less_bias(other[1][:], second(1, 3, 4), 1)
         weigh_picked(0)
-        put(0, weighted0[0][:], 0, BANK)
+        put(0, weighted0[0][:], 0, EARLY)
         lent_difference(1)
+        weigh_picked(1)
+        put(0, weighted0[1][:], EARLY, MIDDLE)
         lent_relu(1)
         lent_sum(1)
-        weigh_picked(1)
+        weigh_picked(2)
         pick(1)
-        put(0, weighted0[1][:], BANK, S)
+        put(0, weighted0[2][:], MIDDLE, S)
         store(0)
         weighted1 = tile([P, S], F32, "weighted1", tag="w1_raw0")
 

@@ -30,7 +30,7 @@ HALVES = S // BANK
 CHUNKS = T2 // BANK
 BLOCKS = N // P
 LEAD = BANK // 2
-TAB_CUT = 5 * T // 8
+TAB_CUT = 3 * T // 4
 LENT = 2
 LENT_CHUNKS = (0, CHUNKS - 1)
 EARLY = 256
@@ -259,8 +259,7 @@ def tile_list_propellant_gauge_fusion_kernel(
         w3_codes = tile([P, N], U32, "w3_codes", tag="bell%d" % (PACK - 1))
         w3_sc = tile([P, N], U8, "w3_sc")
         w3_flat = w3_grouped[:].rearrange("p c j -> p (c j)")
-        for c0, c1 in ((0, 2 * P), (2 * P, N)):
-            nc.vector.quantize_mx(w3_codes[:, c0:c1].bitcast(FP8X4), w3_sc[:, c0:c1], w3_flat[:, PACK * c0 : PACK * c1])
+        nc.vector.quantize_mx(w3_codes[:].bitcast(FP8X4), w3_sc[:], w3_flat)
 
         z_tags = ("tab0", "w1_raw0", "z_grouped2", "z_grouped3")
         z_grouped = [tile([P, BANK, PACK], BF16, "z_grouped%d" % c, tag=z_tags[c]) for c in range(CHUNKS)]
@@ -439,4 +438,5 @@ def tile_list_propellant_gauge_fusion_kernel(
         store(1)
 
         nc.vector.tensor_tensor(budget[last][:].indirect(idx4[:]), picked[last][:], wgo_sb[:], ALU.mult)
-        store(last)
+        for queue, cols in zip((nc.sync, nc.scalar), (slice(0, T2 // 2), slice(T2 // 2, T2))):
+            queue.dma_start(out[last * P :, cols], budget[last][:, cols])

@@ -23,6 +23,7 @@ BANK = 512
 QUAD = 32
 QUADS = P // QUAD
 SCALE_ROWS = 4
+ROW = 4 * T2
 PER_COLUMN = 16
 K_PASS = P * PACK
 PASSES = K // K_PASS
@@ -46,6 +47,7 @@ def tile_list_propellant_gauge_fusion_kernel(
         lists = ctx.enter_context(tc.tile_pool(name="lists", bufs=1))
         sb = ctx.enter_context(tc.tile_pool(name="sb", bufs=1))
         last_page = ctx.enter_context(tc.tile_pool(name="last_page", bufs=1))
+        reused = ctx.enter_context(tc.tile_pool(name="reused", bufs=1))
         psum = ctx.enter_context(tc.psum_pool(name="psum", bufs=1))
 
         def tile(shape, dtype, name, tag=None):
@@ -53,6 +55,9 @@ def tile_list_propellant_gauge_fusion_kernel(
 
         def on_last_page(shape, dtype, name, offset):
             return last_page.tile(shape, dtype, name=name, align_bytes=64, offset=offset)
+
+        def on_reused(shape, dtype, name, offset):
+            return reused.tile(shape, dtype, name=name, align_bytes=64, offset=offset)
 
         def load_list(src, name):
             held = lists.tile([P, S // PER_COLUMN], U16, name=name)
@@ -70,7 +75,7 @@ def tile_list_propellant_gauge_fusion_kernel(
         ident = tile([P, P], F32, "ident")
         make_identity(nc, ident[:])
         tab = [tile([P, T], U32, "tab%d" % a) for a in range(PASSES)]
-        w1_raw = [tile([P, PACK, H], F32, "w1_raw0"), on_last_page([P, PACK, H], F32, "w1_raw1", 0)]
+        w1_raw = [tile([P, PACK, H], F32, "w1_raw0"), on_reused([P, PACK, H], F32, "w1_raw1", 0)]
 
         def load_w1(a):
             nc.sync.dma_start(w1_raw[a][:], w1[K_PASS * a : K_PASS * (a + 1), :].rearrange("(p j) c -> p j c", j=PACK))
@@ -132,7 +137,8 @@ def tile_list_propellant_gauge_fusion_kernel(
         load_limit(CHUNKS - 1)
 
         pages = [tile([P, T2], F32, "page%d" % t, tag="tab_sc" if t == 1 else None) for t in range(PACK - 1)]
-        for t in range(PACK - 1):
+        pages.append(on_last_page([P, T2], F32, "page3", 0))
+        for t in range(PACK):
             nc.vector.memset(pages[t][:].bitcast(I32), 0)
         w2_sc = tile([P, N], U8, "w2_sc")
         nc.vector.memset(w2_sc[:].bitcast(I32), 0)
@@ -152,7 +158,7 @@ def tile_list_propellant_gauge_fusion_kernel(
         w1_codes = []
         w1_sc = []
         for a in range(PASSES):
-            grouped = tile([P, PACK, P, PACK], BF16, "w1_grouped%d" % a)
+            grouped = on_reused([P, PACK, P, PACK], BF16, "w1_grouped1", ROW) if a else tile([P, PACK, P, PACK], BF16, "w1_grouped0")
             nc.scalar.copy(
                 grouped[:].rearrange("p t m j -> p m j t"), w1_raw[a][:].rearrange("p j (m t) -> p m j t", t=PACK)
             )
@@ -161,9 +167,9 @@ def tile_list_propellant_gauge_fusion_kernel(
             nc.vector.quantize_mx(codes[:].bitcast(FP8X4), sc[:], grouped[:].rearrange("p t m j -> p (t m j)"))
             w1_codes.append(codes)
             w1_sc.append(sc)
-        budget = [tile([P, T2], F32, "budget%d" % b, tag="w1_grouped%d" % b) for b in range(2)]
-        pages.append(on_last_page([P, T2], F32, "page3", 0))
-        for window in (budget[0], pages[3], budget[1]):
+        budget = [tile([P, T2], F32, "budget0", tag="w1_grouped0")]
+        budget.extend(on_reused([P, T2], F32, "budget%d" % b, ROW // 4 + ROW * (b - 1)) for b in (1, 2))
+        for window in budget:
             nc.gpsimd.memset(window[:], 0.0)
         got = [tile([P, S], U32, "got0"), tile([P, S], U32, "got1", tag="tab0")]
         nc.vector.tensor_copy(got[0][:], tab[0][:].indirect(idx1[:]))
@@ -254,14 +260,12 @@ def tile_list_propellant_gauge_fusion_kernel(
             w3_grouped[:].rearrange("p (c i) j -> p c j i", i=4), w3_raw[:].rearrange("p j (c i) -> p c j i", i=4)
         )
         round_limit(CHUNKS - 1)
-        budget.append(tile([P, T2], F32, "budget2", tag="lim3"))
-        nc.gpsimd.memset(budget[2][:], 0.0)
         w3_codes = tile([P, N], U32, "w3_codes", tag="bell%d" % (PACK - 1))
         w3_sc = tile([P, N], U8, "w3_sc")
         w3_flat = w3_grouped[:].rearrange("p c j -> p (c j)")
         nc.vector.quantize_mx(w3_codes[:].bitcast(FP8X4), w3_sc[:], w3_flat)
 
-        z_tags = ("tab0", "w1_raw0", "z_grouped2", "z_grouped3")
+        z_tags = ("tab0", "w1_raw0", "z_grouped2", "w3_raw")
         z_grouped = [tile([P, BANK, PACK], BF16, "z_grouped%d" % c, tag=z_tags[c]) for c in range(CHUNKS)]
         z_codes = tile([P, T2], U32, "z_codes")
         z_sc = [on_last_page([P, BANK], U8, "z_sc2", 0) if c == 2 else tile([P, BANK], U8, "z_sc%d" % c) for c in range(CHUNKS)]
@@ -335,7 +339,7 @@ def tile_list_propellant_gauge_fusion_kernel(
         for c in range(CHUNKS):
             larger(0, c, held[c])
 
-        excess1 = [tile([P, BANK], F32, "excess1_%d" % c, tag=tag) for c, tag in enumerate(("z_grouped3", "w1_codes1"))]
+        excess1 = [tile([P, BANK], F32, "excess1_%d" % c, tag=tag) for c, tag in enumerate(("w3_raw", "w1_codes1"))]
 
 
         def lent_difference(c):

@@ -303,9 +303,9 @@ def tile_list_propellant_gauge_fusion_kernel(
         def less_bias(dst, sums, b):
             nc.scalar.activation(dst, sums[:], ACT.Identity, bias=neg_bias[b])
 
-        def larger(b, c, y3):
+        def larger(b, c, y3, minus_bias):
             nc.vector.scalar_tensor_tensor(
-                score[b][:, chunks[c]], y3[:], bias_sb[:, b : b + 1], lead[b][:, chunks[c]], ALU.subtract, ALU.max
+                score[b][:, chunks[c]], y3[:], minus_bias, lead[b][:, chunks[c]], ALU.add, ALU.max
             )
 
         score = [tile([P, T2], F32, "score0", tag="z_grouped2"), tile([P, T2], F32, "score1", tag="page0")]
@@ -329,15 +329,15 @@ def tile_list_propellant_gauge_fusion_kernel(
         less_bias(score[1][:, chunks[0]], first(1, 0, 1), 1)
         less_bias(other[0][:], second(1, 0, 2), 1)
         held.append(second(0, 0, 7))
-        less_bias(lead[0][:, chunks[1]], first(0, 1, 3), 0)
-        less_bias(score[1][:, chunks[1]], first(1, 1, 4), 1)
+        less_bias(lead[0][:, chunks[1]], first(0, 1, 2), 0)
         held.append(second(0, 1, 5))
         less_bias(lead[0][:, chunks[2]], first(0, 2, 6), 0)
         less_bias(lead[0][:, chunks[3]], first(0, 3, 0), 0)
-        held.append(second(0, 2, 3))
-        held.append(second(0, 3, 4))
+        held.append(second(0, 2, 6))
+        held.append(second(0, 3, 1))
+        less_bias(score[1][:, chunks[1]], first(1, 1, 2), 1)
         for c in range(CHUNKS):
-            larger(0, c, held[c])
+            larger(0, c, held[c], neg_bias[0])
 
         excess1 = [tile([P, BANK], F32, "excess1_%d" % c, tag=tag) for c, tag in enumerate(("w3_raw", "w1_codes1"))]
 
@@ -353,7 +353,8 @@ def tile_list_propellant_gauge_fusion_kernel(
             nc.gpsimd.tensor_tensor(cols, cols, excess1[c][:], ALU.add)
 
         parts = [slice(0, EARLY), slice(EARLY, MIDDLE), slice(MIDDLE, S)]
-        halves = tile([P, S], F32, "picked0", tag="bell0")
+        halves = [tile([P, EARLY], F32, "early_pick", tag="work"), tile([P, S - EARLY], F32, "late_pick", tag="bell0")]
+        picked0 = [halves[0][:], halves[1][:, : MIDDLE - EARLY], halves[1][:, MIDDLE - EARLY :]]
         picked = [None, tile([P, S], F32, "picked1", tag="tab0"), tile([P, S], F32, "picked2", tag="bell2")]
 
         def pick(b):
@@ -361,7 +362,7 @@ def tile_list_propellant_gauge_fusion_kernel(
 
         def pick_half(u):
             cut = (parts[0], slice(EARLY, S))[u]
-            nc.vector.tensor_copy(halves[:, cut], score[0][:].indirect(entries(idx3, cut.start, cut.stop)))
+            nc.vector.tensor_copy(halves[u][:], score[0][:].indirect(entries(idx3, cut.start, cut.stop)))
 
         def put(b, values, j0, j1):
             nc.vector.tensor_copy(budget[b][:].indirect(entries(idx4, j0, j1)), values)
@@ -375,20 +376,23 @@ def tile_list_propellant_gauge_fusion_kernel(
         ]
 
         def weigh_picked(u):
-            nc.gpsimd.tensor_tensor(weighted0[u][:], halves[:, parts[u]], wgo_sb[:, parts[u]], ALU.mult)
+            nc.gpsimd.tensor_tensor(weighted0[u][:], picked0[u], wgo_sb[:, parts[u]], ALU.mult)
 
         lent_difference(0)
         lent_relu(0)
         lent_sum(0)
-        larger(1, 1, second(1, 1, 7))
-        less_bias(score[1][:, chunks[2]], first(1, 2, 0), 1)
-        larger(1, 2, second(1, 2, 5))
+        larger(1, 1, second(1, 1, 5), neg_bias[1])
+        less_bias(score[1][:, chunks[2]], first(1, 2, 6), 1)
+        late_sums = second(1, 2, 7)
         pick_half(0)
         pick_half(1)
-        less_bias(score[1][:, chunks[3]], first(1, 3, 3), 1)
-        less_bias(other[1][:], second(1, 3, 4), 1)
+        less_bias(score[1][:, chunks[3]], first(1, 3, 0), 1)
+        less_bias(other[1][:], second(1, 3, 2), 1)
         weigh_picked(0)
         put(0, weighted0[0][:], 0, EARLY)
+        late_bias = tile([P, 1], F32, "late_bias", tag="work")
+        nc.gpsimd.tensor_scalar(late_bias[:], bias_sb[:, 1:2], -1.0, 0.0, ALU.mult, ALU.add)
+        larger(1, 2, late_sums, late_bias[:])
         lent_difference(1)
         weigh_picked(1)
         put(0, weighted0[1][:], EARLY, MIDDLE)
@@ -408,13 +412,13 @@ def tile_list_propellant_gauge_fusion_kernel(
         score.append(tile([P, T2], F32, "score2", tag="tab1"))
 
         def copy_out(c):
-            less_bias(first_score[:, chunks[c]], first(last, c, (0, 3)[c % 2]), last)
+            less_bias(first_score[:, chunks[c]], first(last, c, (0, 2)[c % 2]), last)
             nc.scalar.activation(
-                minus_second[:, chunks[c]], second(last, c, (7, 4)[c % 2])[:], ACT.Identity, bias=bias_sb[:, last : last + 1], scale=-1.0
+                minus_second[:, chunks[c]], second(last, c, (5, 1)[c % 2])[:], ACT.Identity, bias=bias_sb[:, last : last + 1], scale=-1.0
             )
 
         def turn(c):
-            gap = psum.tile([P, BANK], F32, name="gap", tag="bank%d" % (1 + c % 2))
+            gap = psum.tile([P, BANK], F32, name="gap", tag="bank%d" % (3, 4)[c % 2])
             for j in range(0, BANK, P):
                 cols = slice(c * BANK + j, c * BANK + j + P)
                 nc.tensor.matmul(gap[:, j : j + P], first_score[:, cols], ident[:], start=True, stop=False, is_transpose=True)
@@ -422,7 +426,7 @@ def tile_list_propellant_gauge_fusion_kernel(
             nc.scalar.activation(turned[:, chunks[c]], gap[:], ACT.Relu, scale=-1.0)
 
         def turn_back(c):
-            back = psum.tile([P, BANK], F32, name="back", tag="bank%d" % (5 + c % 2))
+            back = psum.tile([P, BANK], F32, name="back", tag="bank%d" % (6, 7)[c % 2])
             for j in range(0, BANK, P):
                 nc.tensor.transpose(back[:, j : j + P], turned[:, c * BANK + j : c * BANK + j + P], ident[:])
             nc.scalar.copy(excess[c][:], back[:])

@@ -281,32 +281,32 @@ def tile_list_propellant_gauge_fusion_kernel(
                 ALU.min,
             )
 
-        def quantize(c):
+        def quantize(c, j0=0, j1=BANK):
             nc.vector.quantize_mx(
-                z_codes[:, chunks[c]].bitcast(FP8X4), z_sc[c][:], z_grouped[c][:].rearrange("p c t -> p (c t)")
+                z_codes[:, c * BANK + j0 : c * BANK + j1].bitcast(FP8X4),
+                z_sc[c][:, j0:j1],
+                z_grouped[c][:, j0:j1, :].rearrange("p c t -> p (c t)"),
             )
 
-        def product(b, c, codes, sc, dtype, width, bank):
-            y = psum.tile([P, BANK], F32, name="y", tag="bank%d" % bank)
+        def product(b, c, j0, j1, codes, sc, dtype, width, bank):
+            y = psum.tile([P, j1 - j0], F32, name="y", tag="bank%d" % bank)
             nc.tensor.matmul_mx(
                 y[:], lhsT=codes[:, width * P * b : width * P * (b + 1)].bitcast(dtype), lhsT_scale=sc[:, P * b : P * (b + 1)],
-                rhs=z_codes[:, chunks[c]].bitcast(FP8X4), rhs_scale=z_sc[c][:], start=True, stop=True,
+                rhs=z_codes[:, c * BANK + j0 : c * BANK + j1].bitcast(FP8X4), rhs_scale=z_sc[c][:, j0:j1], start=True, stop=True,
             )
             return y
 
-        def first(b, c, bank):
-            return product(b, c, w2_codes, w2_sc, FP4X4, 2, bank)
+        def first(b, c, bank, j0=0, j1=BANK):
+            return product(b, c, j0, j1, w2_codes, w2_sc, FP4X4, 2, bank)
 
-        def second(b, c, bank):
-            return product(b, c, w3_codes, w3_sc, FP8X4, 1, bank)
+        def second(b, c, bank, j0=0, j1=BANK):
+            return product(b, c, j0, j1, w3_codes, w3_sc, FP8X4, 1, bank)
 
         def less_bias(dst, sums, b):
             nc.scalar.activation(dst, sums[:], ACT.Identity, bias=neg_bias[b])
 
-        def larger(b, c, y3, minus_bias):
-            nc.vector.scalar_tensor_tensor(
-                score[b][:, chunks[c]], y3[:], minus_bias, lead[b][:, chunks[c]], ALU.add, ALU.max
-            )
+        def larger(b, cols, y3, minus_bias):
+            nc.vector.scalar_tensor_tensor(score[b][:, cols], y3[:], minus_bias, lead[b][:, cols], ALU.add, ALU.max)
 
         score = [tile([P, T2], F32, "score0", tag="z_grouped2"), tile([P, T2], F32, "score1", tag="page0")]
         lead = [tile([P, T2], F32, "lead0", tag="page2"), score[1]]
@@ -324,7 +324,9 @@ def tile_list_propellant_gauge_fusion_kernel(
             clip(i)
             if j0 % BANK == 0 and j0 >= BANK:
                 quantize(j0 // BANK - 1)
-        quantize(CHUNKS - 1)
+        tail = [(0, BANK // 2), (BANK // 2, BANK)]
+        for j0, j1 in tail:
+            quantize(CHUNKS - 1, j0, j1)
         less_bias(lead[0][:, chunks[0]], first(0, 0, 0), 0)
         less_bias(score[1][:, chunks[0]], first(1, 0, 1), 1)
         less_bias(other[0][:], second(1, 0, 2), 1)
@@ -332,12 +334,14 @@ def tile_list_propellant_gauge_fusion_kernel(
         less_bias(lead[0][:, chunks[1]], first(0, 1, 2), 0)
         held.append(second(0, 1, 5))
         less_bias(lead[0][:, chunks[2]], first(0, 2, 6), 0)
-        less_bias(lead[0][:, chunks[3]], first(0, 3, 0), 0)
         held.append(second(0, 2, 6))
-        held.append(second(0, 3, 1))
+        spans = chunks[:-1] + [slice(T2 - BANK + j0, T2 - BANK + j1) for j0, j1 in tail]
+        for (j0, j1), cols, banks in zip(tail, spans[-2:], ((0, 1), (3, 4))):
+            less_bias(lead[0][:, cols], first(0, 3, banks[0], j0, j1), 0)
+            held.append(second(0, 3, banks[1], j0, j1))
         less_bias(score[1][:, chunks[1]], first(1, 1, 2), 1)
-        for c in range(CHUNKS):
-            larger(0, c, held[c], neg_bias[0])
+        for cols, sums in zip(spans, held):
+            larger(0, cols, sums, neg_bias[0])
 
         excess1 = [tile([P, BANK], F32, "excess1_%d" % c, tag=tag) for c, tag in enumerate(("w3_raw", "w1_codes1"))]
 
@@ -381,7 +385,7 @@ def tile_list_propellant_gauge_fusion_kernel(
         lent_difference(0)
         lent_relu(0)
         lent_sum(0)
-        larger(1, 1, second(1, 1, 5), neg_bias[1])
+        larger(1, chunks[1], second(1, 1, 5), neg_bias[1])
         less_bias(score[1][:, chunks[2]], first(1, 2, 6), 1)
         late_sums = second(1, 2, 7)
         pick_half(0)
@@ -392,7 +396,7 @@ def tile_list_propellant_gauge_fusion_kernel(
         put(0, weighted0[0][:], 0, EARLY)
         late_bias = tile([P, 1], F32, "late_bias", tag="work")
         nc.gpsimd.tensor_scalar(late_bias[:], bias_sb[:, 1:2], -1.0, 0.0, ALU.mult, ALU.add)
-        larger(1, 2, late_sums, late_bias[:])
+        larger(1, chunks[2], late_sums, late_bias[:])
         lent_difference(1)
         weigh_picked(1)
         put(0, weighted0[1][:], EARLY, MIDDLE)

@@ -35,7 +35,7 @@ TAB_CUT = 3 * T // 4
 LENT = 2
 LENT_CHUNKS = (0, CHUNKS - 1)
 EARLY = 256
-MIDDLE = 640
+MIDDLE = 512
 FIRST_BANKS = 4
 
 
@@ -302,8 +302,8 @@ def tile_list_propellant_gauge_fusion_kernel(
         def second(b, c, bank, j0=0, j1=BANK):
             return product(b, c, j0, j1, w3_codes, w3_sc, FP8X4, 1, bank)
 
-        def less_bias(dst, sums, b):
-            nc.scalar.activation(dst, sums[:], ACT.Identity, bias=neg_bias[b])
+        def less_bias(dst, sums, b, early=False):
+            nc.scalar.activation(dst, sums[:], ACT.Identity, bias=neg_early[:] if early else neg_bias[b])
 
         def larger(b, cols, y3, minus_bias):
             nc.vector.scalar_tensor_tensor(score[b][:, cols], y3[:], minus_bias, lead[b][:, cols], ALU.add, ALU.max)
@@ -319,6 +319,8 @@ def tile_list_propellant_gauge_fusion_kernel(
         nc.scalar.activation(neg_first[:], bias_sb[:, :1], ACT.Copy, scale=-1.0)
         neg_rest = on_last_page([P, BLOCKS - 1], F32, "neg_rest", BANK)
         nc.scalar.activation(neg_rest[:], bias_sb[:, 1:], ACT.Copy, scale=-1.0)
+        neg_early = on_last_page([P, 1], F32, "neg_early", 4 * BANK)
+        nc.scalar.activation(neg_early[:], bias_sb[:, BLOCKS - 1 :], ACT.Copy, scale=-1.0)
         neg_bias = [neg_first[:]] + [neg_rest[:, b : b + 1] for b in range(BLOCKS - 1)]
         for i, (j0, j1) in enumerate(pieces):
             clip(i)
@@ -346,23 +348,29 @@ def tile_list_propellant_gauge_fusion_kernel(
         excess1 = [tile([P, BANK], F32, "excess1_%d" % c, tag=tag) for c, tag in enumerate(("w3_raw", "w1_codes1"))]
 
 
+        kept = [excess1[0], on_last_page([P, BANK], F32, "kept1", 4 * BANK)]
+
         def lent_difference(c):
             nc.gpsimd.tensor_tensor(excess1[c][:], other[c][:], score[1][:, chunks[LENT_CHUNKS[c]]], ALU.subtract)
 
         def lent_relu(c):
-            nc.gpsimd.tensor_scalar(excess1[c][:], excess1[c][:], float("inf"), 0.0, ALU.min, ALU.max)
+            if c:
+                nc.scalar.activation(kept[c][:], excess1[c][:], ACT.Relu)
+            else:
+                nc.gpsimd.tensor_scalar(excess1[c][:], excess1[c][:], float("inf"), 0.0, ALU.min, ALU.max)
 
         def lent_sum(c):
             cols = score[1][:, chunks[LENT_CHUNKS[c]]]
-            nc.gpsimd.tensor_tensor(cols, cols, excess1[c][:], ALU.add)
+            nc.gpsimd.tensor_tensor(cols, cols, kept[c][:], ALU.add)
 
         parts = [slice(0, EARLY), slice(EARLY, MIDDLE), slice(MIDDLE, S)]
         halves = [tile([P, EARLY], F32, "early_pick", tag="work"), tile([P, S - EARLY], F32, "late_pick", tag="bell0")]
         picked0 = [halves[0][:], halves[1][:, : MIDDLE - EARLY], halves[1][:, MIDDLE - EARLY :]]
-        picked = [None, tile([P, S], F32, "picked1", tag="tab0"), tile([P, S], F32, "picked2", tag="bell2")]
+        shared = tile([P, LEAD + T2], F32, "shared", tag="tab1")
+        picked = [None, shared[:, :S], tile([P, S], F32, "picked2", tag="bell2")[:]]
 
         def pick(b):
-            nc.vector.tensor_copy(picked[b][:], score[b][:].indirect(idx3[:]))
+            nc.vector.tensor_copy(picked[b], score[b][:, :].indirect(idx3[:]))
 
         def pick_half(u):
             cut = (parts[0], slice(EARLY, S))[u]
@@ -376,8 +384,9 @@ def tile_list_propellant_gauge_fusion_kernel(
 
         weighted0 = [
             tile([P, cut.stop - cut.start], F32, "weighted0_%d" % cut.start, tag=tag)
-            for cut, tag in zip(parts, ("page2", "w1_codes0", "w1_codes1"))
+            for cut, tag in zip(parts, ("page2", "w1_codes0"))
         ]
+        weighted0.append(on_last_page([P, S - MIDDLE], F32, "weighted0_late", 4 * BANK))
 
         def weigh_picked(u):
             nc.gpsimd.tensor_tensor(weighted0[u][:], picked0[u], wgo_sb[:, parts[u]], ALU.mult)
@@ -400,26 +409,30 @@ def tile_list_propellant_gauge_fusion_kernel(
         lent_difference(1)
         weigh_picked(1)
         put(0, weighted0[1][:], EARLY, MIDDLE)
+        last = BLOCKS - 1
+        first_score = tile([P, T2], F32, "first_score", tag="tab_sc")
+        minus_second = tile([P, T2], F32, "minus_second", tag="lim0")
+        turned = tile([P, T2], F32, "turned", tag="lim1")
+        excess = [tile([P, 2 * BANK], F32, "excess0", tag="tab0"), tile([P, BANK], F32, "excess2", tag="got0"), tile([P, BANK], F32, "excess3", tag="wgs2")]
+        returned = [excess[0][:, :BANK], excess[0][:, BANK:], excess[1][:], excess[2][:]]
+        score.append(shared[:, LEAD:])
+
+        def copy_out(c):
+            less_bias(first_score[:, chunks[c]], first(last, c, (0, 2)[c % 2]), last, c < 2)
+            nc.scalar.activation(
+                minus_second[:, chunks[c]], second(last, c, (5, 1)[c % 2])[:], ACT.Identity, bias=bias_sb[:, last : last + 1], scale=-1.0
+            )
+
+        copy_out(0)
+        copy_out(1)
         lent_relu(1)
         lent_sum(1)
         weigh_picked(2)
         pick(1)
         put(0, weighted0[2][:], MIDDLE, S)
         store(0)
-        weighted1 = tile([P, S], F32, "weighted1", tag="w1_raw0")
-
-        last = BLOCKS - 1
-        first_score = tile([P, T2], F32, "first_score", tag="tab_sc")
-        minus_second = tile([P, T2], F32, "minus_second", tag="lim0")
-        turned = tile([P, T2], F32, "turned", tag="lim1")
-        excess = [tile([P, BANK], F32, "excess%d" % c, tag=tag) for c, tag in enumerate(("w1_raw0", "lim2", "got0", "wgs2"))]
-        score.append(tile([P, T2], F32, "score2", tag="tab1"))
-
-        def copy_out(c):
-            less_bias(first_score[:, chunks[c]], first(last, c, (0, 2)[c % 2]), last)
-            nc.scalar.activation(
-                minus_second[:, chunks[c]], second(last, c, (5, 1)[c % 2])[:], ACT.Identity, bias=bias_sb[:, last : last + 1], scale=-1.0
-            )
+        weighted1 = tile([P, S - LEAD], F32, "weighted1", tag="w1_raw0")
+        nc.gpsimd.tensor_tensor(weighted1[:], picked[1][:, LEAD:], wgo_sb[:, LEAD:], ALU.mult)
 
         def turn(c):
             gap = psum.tile([P, BANK], F32, name="gap", tag="bank%d" % (3, 4)[c % 2])
@@ -433,22 +446,22 @@ def tile_list_propellant_gauge_fusion_kernel(
             back = psum.tile([P, BANK], F32, name="back", tag="bank%d" % (6, 7)[c % 2])
             for j in range(0, BANK, P):
                 nc.tensor.transpose(back[:, j : j + P], turned[:, c * BANK + j : c * BANK + j + P], ident[:])
-            nc.scalar.copy(excess[c][:], back[:])
-            nc.gpsimd.tensor_tensor(score[last][:, chunks[c]], first_score[:, chunks[c]], excess[c][:], ALU.add)
-            if c == 0:
-                nc.gpsimd.tensor_tensor(weighted1[:, LEAD:], picked[1][:, LEAD:], wgo_sb[:, LEAD:], ALU.mult)
+            nc.scalar.copy(returned[c], back[:])
+            if c:
+                cols = chunks[c] if c > 1 else slice(0, 2 * BANK)
+                nc.gpsimd.tensor_tensor(score[last][:, cols], first_score[:, cols], excess[c - 1][:], ALU.add)
 
         for step in range(CHUNKS + 2):
             for stage, c in ((turn_back, step - 2), (turn, step - 1), (copy_out, step)):
-                if 0 <= c < CHUNKS:
+                if (2 if stage == copy_out else 0) <= c < CHUNKS:
                     stage(c)
-        put(1, weighted1[:, LEAD:], LEAD, S)
+        put(1, weighted1[:], LEAD, S)
         pick(last)
         rest = tile([P, LEAD], F32, "rest", tag="wgs2")
         nc.gpsimd.tensor_tensor(rest[:], picked[1][:, :LEAD], wgo_sb[:, :LEAD], ALU.mult)
         put(1, rest[:], 0, LEAD)
         store(1)
 
-        nc.vector.tensor_tensor(budget[last][:].indirect(idx4[:]), picked[last][:], wgo_sb[:], ALU.mult)
+        nc.vector.tensor_tensor(budget[last][:].indirect(idx4[:]), picked[last], wgo_sb[:], ALU.mult)
         for queue, cols in zip((nc.sync, nc.scalar), (slice(0, T2 // 2), slice(T2 // 2, T2))):
             queue.dma_start(out[last * P :, cols], budget[last][:, cols])

@@ -159,7 +159,7 @@ def tile_list_propellant_gauge_fusion_kernel(
         w1_sc = []
         for a in range(PASSES):
             grouped = on_reused([P, PACK, P, PACK], BF16, "w1_grouped1", ROW) if a else tile([P, PACK, P, PACK], BF16, "w1_grouped0")
-            nc.scalar.copy(
+            (nc.vector.tensor_copy if a else nc.scalar.copy)(
                 grouped[:].rearrange("p t m j -> p m j t"), w1_raw[a][:].rearrange("p j (m t) -> p m j t", t=PACK)
             )
             codes = tile([P, H], U32, "w1_codes%d" % a)

from contextlib import ExitStack

import concourse.mybir as mybir
from concourse.masks import make_identity

K, T, H, N, S, T2 = 1024, 4096, 512, 384, 1024, 2048
FLOPS = 2 * K * H * S + 2 * 2 * H * N * T2

F32 = mybir.dt.float32
BF16 = mybir.dt.bfloat16
I32 = mybir.dt.int32
U32 = mybir.dt.uint32
U16 = mybir.dt.uint16
U8 = mybir.dt.uint8
FP8X4 = mybir.dt.float8_e4m3fn_x4
FP4X4 = mybir.dt.float4_e2m1fn_x4
ALU = mybir.AluOpType
ACT = mybir.ActivationFunctionType

P = 128
PACK = 4
BANK = 512
QUAD = 32
QUADS = P // QUAD
SCALE_ROWS = 4
ROW = 4 * T2
PER_COLUMN = 16
K_PASS = P * PACK
PASSES = K // K_PASS
HALVES = S // BANK
CHUNKS = T2 // BANK
BLOCKS = N // P
LEAD = BANK // 2
TAB_CUT = 3 * T // 4
LENT = 2
LENT_CHUNKS = (0, CHUNKS - 1)
EARLY = 256
MIDDLE = 512
FIRST_BANKS = 4


def tile_list_propellant_gauge_fusion_kernel(
    tc, tab_words, tab_scales, offs, w1, gain, wgs, offs2, limit, w2_words, w2_scales, w3, offs3, bias, wgo, offs4, out
):
    nc = tc.nc
    with ExitStack() as ctx:
        lists = ctx.enter_context(tc.tile_pool(name="lists", bufs=1))
        sb = ctx.enter_context(tc.tile_pool(name="sb", bufs=1))
        last_page = ctx.enter_context(tc.tile_pool(name="last_page", bufs=1))
        reused = ctx.enter_context(tc.tile_pool(name="reused", bufs=1))
        psum = ctx.enter_context(tc.psum_pool(name="psum", bufs=1))

        def tile(shape, dtype, name, tag=None):
            return sb.tile(shape, dtype, name=name, tag=tag or name, align_bytes=64)

        def on_last_page(shape, dtype, name, offset):
            return last_page.tile(shape, dtype, name=name, align_bytes=64, offset=offset)

        def on_reused(shape, dtype, name, offset):
            return reused.tile(shape, dtype, name=name, align_bytes=64, offset=offset)

        def load_list(src, name):
            held = lists.tile([P, S // PER_COLUMN], U16, name=name)
            nc.sync.dma_start(held[:], src)
            return held

        def entries(held, j0, j1):
            return held[:, j0 // PER_COLUMN : j1 // PER_COLUMN]

        tab_sc = tile([P, T], U8, "tab_sc")
        nc.vector.memset(tab_sc[:].bitcast(I32), 0)
        warm = tile([P, 2], F32, "warm")
        nc.vector.memset(warm[:, 0:1], 1.0)
        nc.scalar.activation(warm[:, 1:2], warm[:, 0:1], ACT.Abs_reciprocal_sqrt)
        ident = tile([P, P], F32, "ident")
        make_identity(nc, ident[:])
        tab = [tile([P, T], U32, "tab%d" % a) for a in range(PASSES)]
        w1_raw = [tile([P, PACK, H], F32, "w1_raw0"), on_reused([P, PACK, H], F32, "w1_raw1", 0)]

        def load_w1(a):
            nc.sync.dma_start(w1_raw[a][:], w1[K_PASS * a : K_PASS * (a + 1), :].rearrange("(p j) c -> p j c", j=PACK))

        def load_tab(a, t0=0, t1=T):
            words = tab_words[a].rearrange("p t i -> p (t i)").bitcast(I32)
            nc.sync.dma_start(tab[a][:, t0:t1].bitcast(I32), words[:, t0:t1])

        load_w1(0)
        nc.sync.dma_start(tab_sc[0:P:SCALE_ROWS, :].bitcast(I32), tab_scales.rearrange("a i t -> (a i) t").bitcast(I32))
        idx1 = load_list(offs, "idx1")
        spread_sc = tile([P, S], U8, "spread_sc")
        nc.vector.tensor_copy(spread_sc[:], tab_sc[:].indirect(idx1[:]))
        got_sc = [tile([P, S], U8, "got_sc%d" % a) for a in range(PASSES)]

        def move_scales(a):
            nc.vector.memset(got_sc[a][:].bitcast(I32), 0)
            for r in range(SCALE_ROWS):
                first = SCALE_ROWS * (QUADS * SCALE_ROWS * a + r)
                step = SCALE_ROWS * SCALE_ROWS
                nc.sync.dma_start(
                    got_sc[a][r:P:QUAD, :].bitcast(I32), spread_sc[first : first + step * (QUADS - 1) + 1 : step, :].bitcast(I32)
                )

        load_w1(1)
        load_tab(0)
        move_scales(0)
        load_tab(1, 0, TAB_CUT)
        move_scales(1)
        load_tab(1, TAB_CUT, T)
        idx2 = load_list(offs2, "idx2")
        wgs_rows = wgs.rearrange("(i t) j -> t i j", t=PACK)
        wgs_first = tile([P, 2, S], F32, "wgs1")
        wgs_sb = [wgs_first[:, 0, :], wgs_first[:, 1, :]] + [tile([P, S], F32, "wgs%d" % t)[:] for t in range(2, PACK)]
        limit_rows = limit.rearrange("(p t) c -> p t c", t=PACK)
        lim = [tile([P, PACK, BANK], F32, "lim%d" % c) for c in range(CHUNKS)]

        def load_wgs(t, j0=0, j1=S):
            for q in (0, 2, 1, 3):
                nc.sync.dma_start(wgs_sb[t][QUAD * q : QUAD * (q + 1), j0:j1], wgs_rows[t, :, j0:j1])

        def load_limit(c):
            nc.sync.dma_start(lim[c][:], limit_rows[:, :, c * BANK : (c + 1) * BANK])

        for j0, j1 in ((0, LEAD), (LEAD, BANK), (BANK, S)):
            for q in (0, 2, 1, 3):
                nc.sync.dma_start(wgs_first[QUAD * q : QUAD * (q + 1), :, j0:j1], wgs_rows.rearrange("t i j -> i t j")[:, 0:2, j0:j1])
        gain_sb = tile([P, PACK], F32, "gain_sb")
        nc.sync.dma_start(gain_sb[:], gain.rearrange("(p t) -> p t", t=PACK))
        bias_sb = tile([P, BLOCKS], F32, "bias_sb")
        with nc.allow_non_contiguous_dma(reason="one bias value for each partition and block"):
            nc.sync.dma_start(bias_sb[:], bias.rearrange("(b p) -> p b", p=P))
        load_limit(0)
        w3_raw = tile([P, PACK, N], F32, "w3_raw")
        nc.sync.dma_start(w3_raw[:], w3.rearrange("(p j) c -> p j c", j=PACK))
        for t in range(2, PACK):
            load_wgs(t)
            load_limit(t - 1)
        load_limit(CHUNKS - 1)

        pages = [tile([P, T2], F32, "page%d" % t, tag="tab_sc" if t == 1 else None) for t in range(PACK - 1)]
        pages.append(on_last_page([P, T2], F32, "page3", 0))
        for t in range(PACK):
            nc.vector.memset(pages[t][:].bitcast(I32), 0)
        w2_sc = tile([P, N], U8, "w2_sc")
        nc.vector.memset(w2_sc[:].bitcast(I32), 0)

        w2_codes = tile([P, 2 * N], U8, "w2_codes")
        nc.sync.dma_start(w2_codes[:].bitcast(I32), w2_words[0].bitcast(I32))
        for q in range(QUADS):
            nc.sync.dma_start(
                w2_sc[QUAD * q : QUAD * q + SCALE_ROWS, :].bitcast(I32),
                w2_scales[0, SCALE_ROWS * q : SCALE_ROWS * (q + 1), :].bitcast(I32),
            )
        idx3 = load_list(offs3, "idx3")
        idx4 = load_list(offs4, "idx4")
        wgo_sb = tile([P, S], F32, "wgo_sb")
        nc.sync.dma_start(wgo_sb[:], wgo)

        w1_codes = []
        w1_sc = []
        for a in range(PASSES):
            grouped = on_reused([P, PACK, P, PACK], BF16, "w1_grouped1", ROW) if a else tile([P, PACK, P, PACK], BF16, "w1_grouped0")
            (nc.vector.tensor_copy if a else nc.scalar.copy)(
                grouped[:].rearrange("p t m j -> p m j t"), w1_raw[a][:].rearrange("p j (m t) -> p m j t", t=PACK)
            )
            codes = tile([P, H], U32, "w1_codes%d" % a)
            sc = tile([P, H], U8, "w1_sc%d" % a)
            nc.vector.quantize_mx(codes[:].bitcast(FP8X4), sc[:], grouped[:].rearrange("p t m j -> p (t m j)"))
            w1_codes.append(codes)
            w1_sc.append(sc)
        budget = [tile([P, T2], F32, "budget0", tag="w1_grouped0")]
        budget.extend(on_reused([P, T2], F32, "budget%d" % b, ROW // 4 + ROW * (b - 1)) for b in (1, 2))
        for window in budget:
            nc.gpsimd.memset(window[:], 0.0)
        got = [tile([P, S], U32, "got0"), tile([P, S], U32, "got1", tag="tab0")]
        nc.vector.tensor_copy(got[0][:], tab[0][:].indirect(idx1[:]))
        for j0, j1 in ((0, LEAD), (LEAD, S)):
            nc.vector.tensor_copy(got[1][:, j0:j1], tab[1][:].indirect(entries(idx1, j0, j1)))

        bell = [tile([P, S], F32, "bell%d" % t) for t in range(PACK)]

        def first_product(t, j0, j1, bank):
            acc = psum.tile([P, j1 - j0], F32, name="acc", tag="bank%d" % bank)
            for a in range(PASSES):
                nc.tensor.matmul_mx(
                    acc[:],
                    lhsT=w1_codes[a][:, t * P : (t + 1) * P].bitcast(FP8X4),
                    lhsT_scale=w1_sc[a][:, t * P : (t + 1) * P],
                    rhs=got[a][:, j0:j1].bitcast(FP8X4),
                    rhs_scale=got_sc[a][:, j0:j1],
                    start=(a == 0),
                    stop=(a == PASSES - 1),
                )
            return acc

        def respond(steps):
            for sums, square, root, result in steps:
                nc.scalar.activation(square, sums, ACT.Square)
            for sums, square, root, result in steps:
                nc.scalar.activation(root, square, ACT.Abs_reciprocal_sqrt, bias=1.0)
            for sums, square, root, result in steps:
                nc.scalar.activation(result, root, ACT.Square)

        def weigh(engine, t, j0, j1):
            engine.tensor_tensor(bell[t][:, j0:j1], bell[t][:, j0:j1], wgs_sb[t][:, j0:j1], ALU.mult)

        def place(t, j0, j1):
            nc.vector.tensor_copy(pages[t][:].indirect(entries(idx2, j0, j1)), bell[t][:, j0:j1])

        accs = [first_product(0, j, j + P, FIRST_BANKS * (j // P)) for j in range(0, LEAD, P)]
        work = tile([P, LEAD], F32, "work")
        respond([(accs[j // P][:], work[:, j : j + P], work[:, j : j + P], bell[0][:, j : j + P]) for j in range(0, LEAD, P)])
        nc.vector.tensor_tensor(pages[0][:].indirect(entries(idx2, 0, LEAD)), bell[0][:, :LEAD], wgs_sb[0][:, :LEAD], ALU.mult)
        woven = [(1, 0, LEAD), (0, LEAD, BANK), (1, LEAD, BANK), (0, BANK, S), (1, BANK, S)]
        for i, (t, j0, j1) in enumerate(woven):
            acc = first_product(t, j0, j1, (i + 1) % FIRST_BANKS)
            half = (j1 - j0) // 2
            square = tile([P, j1 - j0], F32, "square_at%d" % i, tag="work")
            cuts = [slice(h, h + half) for h in (0, half)]
            respond([(acc[:, c], square[:, c]) + (bell[t][:, j0 + c.start : j0 + c.stop],) * 2 for c in cuts])
            for j in range(j0, j1, LEAD):
                weigh(nc.gpsimd if i else nc.vector, t, j, j + LEAD)
            place(t, j0, j1)

        for t in range(2, PACK):
            steps = []
            width = BANK if t < PACK - 1 else LEAD
            accs = [first_product(t, u * BANK, (u + 1) * BANK, u) for u in range(HALVES)]
            for i, j in enumerate(range(0, S, width)):
                square = tile([P, width], F32, "square%d_%d" % (t, i), tag="after_plane%d_%d" % (t, 2 * i))
                root = tile([P, width], F32, "root%d_%d" % (t, i), tag="after_plane%d_%d" % (t, 2 * i + 1))
                steps.append((accs[j // BANK][:, j % BANK : j % BANK + width], square[:], root[:], bell[t][:, j : j + width]))
            respond(steps)
            for u in range(HALVES):
                weigh(nc.gpsimd, t, u * BANK, (u + 1) * BANK)
            place(t, 0, S)

        edges = [0, P, 2 * P, 4 * P, 6 * P] + [BANK * c for c in range(2, CHUNKS + 1)]
        pieces = list(zip(edges[:-1], edges[1:]))
        pair_tags = ["after_plane3_%d" % i for i in range(len(pieces))]
        pairs = [tile([P, 2, j1 - j0, 2], BF16, "pairs_at%d" % j0, tag=tag) for (j0, j1), tag in zip(pieces, pair_tags)]
        lim_late = tile([P, 2, 2, BANK, 2], BF16, "lim_late", tag="wgs3")
        lim_pairs = [tile([P, 2, BANK, 2], BF16, "lim_pairs%d" % c, tag="wgs%d" % (c + 1))[:] for c in range(2)]
        lim_pairs.extend(lim_late[:, c] for c in range(2))

        def round_page(t, i):
            j0, j1 = pieces[i]
            nc.scalar.activation(pairs[i][:, t // 2, :, t % 2], pages[t][:, j0:j1], ACT.Copy, scale=gain_sb[:, t : t + 1])

        def round_limit(c):
            src = lim[c][:].rearrange("p (u e) c -> p u c e", e=2)
            for u in range(2):
                nc.gpsimd.tensor_scalar(lim_pairs[c][:, u], src[:, u], 1.0, 0.0, ALU.mult, ALU.add)

        for t in range(PACK - 1):
            for i in range(len(pieces)):
                round_page(t, i)
            round_limit(t)
        w3_grouped = tile([P, N, PACK], BF16, "w3_grouped", tag="after_plane2_3")
        nc.scalar.copy(
            w3_grouped[:].rearrange("p (c i) j -> p c j i", i=4), w3_raw[:].rearrange("p j (c i) -> p c j i", i=4)
        )
        round_limit(CHUNKS - 1)
        w3_codes = tile([P, N], U32, "w3_codes", tag="bell%d" % (PACK - 1))
        w3_sc = tile([P, N], U8, "w3_sc")
        w3_flat = w3_grouped[:].rearrange("p c j -> p (c j)")
        nc.vector.quantize_mx(w3_codes[:].bitcast(FP8X4), w3_sc[:], w3_flat)

        z_tags = ("tab0", "w1_raw0", "z_grouped2", "w3_raw")
        z_grouped = [tile([P, BANK, PACK], BF16, "z_grouped%d" % c, tag=z_tags[c]) for c in range(CHUNKS)]
        z_codes = tile([P, T2], U32, "z_codes")
        z_sc = [on_last_page([P, BANK], U8, "z_sc2", 0) if c == 2 else tile([P, BANK], U8, "z_sc%d" % c) for c in range(CHUNKS)]
        chunks = [slice(c * BANK, (c + 1) * BANK) for c in range(CHUNKS)]

        def clip(i):
            c = pieces[i][0] // BANK
            j0, j1 = pieces[i][0] - c * BANK, pieces[i][1] - c * BANK
            nc.vector.tensor_tensor(
                z_grouped[c][:, j0:j1, :].rearrange("p c (u e) -> p c u e", e=2),
                pairs[i][:].rearrange("p u c e -> p c u e"),
                lim_pairs[c][:, :, j0:j1, :].rearrange("p u c e -> p c u e"),
                ALU.min,
            )

        def quantize(c, j0=0, j1=BANK):
            nc.vector.quantize_mx(
                z_codes[:, c * BANK + j0 : c * BANK + j1].bitcast(FP8X4),
                z_sc[c][:, j0:j1],
                z_grouped[c][:, j0:j1, :].rearrange("p c t -> p (c t)"),
            )

        def product(b, c, j0, j1, codes, sc, dtype, width, bank):
            y = psum.tile([P, j1 - j0], F32, name="y", tag="bank%d" % bank)
            nc.tensor.matmul_mx(
                y[:], lhsT=codes[:, width * P * b : width * P * (b + 1)].bitcast(dtype), lhsT_scale=sc[:, P * b : P * (b + 1)],
                rhs=z_codes[:, c * BANK + j0 : c * BANK + j1].bitcast(FP8X4), rhs_scale=z_sc[c][:, j0:j1], start=True, stop=True,
            )
            return y

        def first(b, c, bank, j0=0, j1=BANK):
            return product(b, c, j0, j1, w2_codes, w2_sc, FP4X4, 2, bank)

        def second(b, c, bank, j0=0, j1=BANK):
            return product(b, c, j0, j1, w3_codes, w3_sc, FP8X4, 1, bank)

        def less_bias(dst, sums, b, early=False):
            nc.scalar.activation(dst, sums[:], ACT.Identity, bias=neg_early[:] if early else neg_bias[b])

        def larger(b, cols, y3, minus_bias):
            nc.vector.scalar_tensor_tensor(score[b][:, cols], y3[:], minus_bias, lead[b][:, cols], ALU.add, ALU.max)

        score = [tile([P, T2], F32, "score0", tag="z_grouped2"), tile([P, T2], F32, "score1", tag="page0")]
        lead = [tile([P, T2], F32, "lead0", tag="page2"), score[1]]
        other = [tile([P, BANK], F32, "other%d" % c, tag=tag) for c, tag in enumerate(("bell1", "w1_codes0"))]
        held = []

        for i in range(len(pieces)):
            round_page(PACK - 1, i)
        neg_first = on_last_page([P, 1], F32, "neg_first", 2 * BANK)
        nc.scalar.activation(neg_first[:], bias_sb[:, :1], ACT.Copy, scale=-1.0)
        neg_rest = on_last_page([P, BLOCKS - 1], F32, "neg_rest", BANK)
        nc.scalar.activation(neg_rest[:], bias_sb[:, 1:], ACT.Copy, scale=-1.0)
        neg_early = on_last_page([P, 1], F32, "neg_early", 4 * BANK)
        nc.scalar.activation(neg_early[:], bias_sb[:, BLOCKS - 1 :], ACT.Copy, scale=-1.0)
        neg_bias = [neg_first[:]] + [neg_rest[:, b : b + 1] for b in range(BLOCKS - 1)]
        for i, (j0, j1) in enumerate(pieces):
            clip(i)
            if j0 % BANK == 0 and j0 >= BANK:
                quantize(j0 // BANK - 1)
        tail = [(0, BANK // 2), (BANK // 2, BANK)]
        for j0, j1 in tail:
            quantize(CHUNKS - 1, j0, j1)
        less_bias(lead[0][:, chunks[0]], first(0, 0, 0), 0)
        less_bias(score[1][:, chunks[0]], first(1, 0, 1), 1)
        less_bias(other[0][:], second(1, 0, 2), 1)
        held.append(second(0, 0, 7))
        less_bias(lead[0][:, chunks[1]], first(0, 1, 2), 0)
        held.append(second(0, 1, 5))
        less_bias(lead[0][:, chunks[2]], first(0, 2, 6), 0)
        held.append(second(0, 2, 6))
        spans = chunks[:-1] + [slice(T2 - BANK + j0, T2 - BANK + j1) for j0, j1 in tail]
        for (j0, j1), cols, banks in zip(tail, spans[-2:], ((0, 1), (3, 4))):
            less_bias(lead[0][:, cols], first(0, 3, banks[0], j0, j1), 0)
            held.append(second(0, 3, banks[1], j0, j1))
        less_bias(score[1][:, chunks[1]], first(1, 1, 2), 1)
        for cols, sums in zip(spans, held):
            larger(0, cols, sums, neg_bias[0])

        excess1 = [tile([P, BANK], F32, "excess1_%d" % c, tag=tag) for c, tag in enumerate(("w3_raw", "w1_codes1"))]


        kept = [excess1[0], on_last_page([P, BANK], F32, "kept1", 4 * BANK)]

        def lent_difference(c):
            nc.gpsimd.tensor_tensor(excess1[c][:], other[c][:], score[1][:, chunks[LENT_CHUNKS[c]]], ALU.subtract)

        def lent_relu(c):
            if c:
                nc.scalar.activation(kept[c][:], excess1[c][:], ACT.Relu)
            else:
                nc.gpsimd.tensor_scalar(excess1[c][:], excess1[c][:], float("inf"), 0.0, ALU.min, ALU.max)

        def lent_sum(c):
            cols = score[1][:, chunks[LENT_CHUNKS[c]]]
            nc.gpsimd.tensor_tensor(cols, cols, kept[c][:], ALU.add)

        parts = [slice(0, EARLY), slice(EARLY, MIDDLE), slice(MIDDLE, S)]
        halves = [tile([P, EARLY], F32, "early_pick", tag="work"), tile([P, S - EARLY], F32, "late_pick", tag="bell0")]
        picked0 = [halves[0][:], halves[1][:, : MIDDLE - EARLY], halves[1][:, MIDDLE - EARLY :]]
        shared = tile([P, LEAD + T2], F32, "shared", tag="tab1")
        picked = [None, shared[:, :S], tile([P, S], F32, "picked2", tag="bell2")[:]]

        def pick(b):
            nc.vector.tensor_copy(picked[b], score[b][:, :].indirect(idx3[:]))

        def pick_half(u):
            cut = (parts[0], slice(EARLY, S))[u]
            nc.vector.tensor_copy(halves[u][:], score[0][:].indirect(entries(idx3, cut.start, cut.stop)))

        def put(b, values, j0, j1):
            nc.vector.tensor_copy(budget[b][:].indirect(entries(idx4, j0, j1)), values)

        def store(b):
            nc.sync.dma_start(out[b * P : (b + 1) * P, :], budget[b][:])

        weighted0 = [
            tile([P, cut.stop - cut.start], F32, "weighted0_%d" % cut.start, tag=tag)
            for cut, tag in zip(parts, ("page2", "w1_codes0"))
        ]
        weighted0.append(on_last_page([P, S - MIDDLE], F32, "weighted0_late", 4 * BANK))

        def weigh_picked(u):
            nc.gpsimd.tensor_tensor(weighted0[u][:], picked0[u], wgo_sb[:, parts[u]], ALU.mult)

        lent_difference(0)
        lent_relu(0)
        lent_sum(0)
        larger(1, chunks[1], second(1, 1, 5), neg_bias[1])
        less_bias(score[1][:, chunks[2]], first(1, 2, 6), 1)
        late_sums = second(1, 2, 7)
        pick_half(0)
        pick_half(1)
        less_bias(score[1][:, chunks[3]], first(1, 3, 0), 1)
        less_bias(other[1][:], second(1, 3, 2), 1)
        weigh_picked(0)
        put(0, weighted0[0][:], 0, EARLY)
        late_bias = tile([P, 1], F32, "late_bias", tag="work")
        nc.gpsimd.tensor_scalar(late_bias[:], bias_sb[:, 1:2], -1.0, 0.0, ALU.mult, ALU.add)
        larger(1, chunks[2], late_sums, late_bias[:])
        lent_difference(1)
        weigh_picked(1)
        put(0, weighted0[1][:], EARLY, MIDDLE)
        last = BLOCKS - 1
        first_score = tile([P, T2], F32, "first_score", tag="tab_sc")
        minus_second = tile([P, T2], F32, "minus_second", tag="lim0")
        turned = tile([P, T2], F32, "turned", tag="lim1")
        excess = [tile([P, 2 * BANK], F32, "excess0", tag="tab0"), tile([P, BANK], F32, "excess2", tag="got0"), tile([P, BANK], F32, "excess3", tag="wgs2")]
        returned = [excess[0][:, :BANK], excess[0][:, BANK:], excess[1][:], excess[2][:]]
        score.append(shared[:, LEAD:])

        def copy_out(c):
            less_bias(first_score[:, chunks[c]], first(last, c, (0, 2)[c % 2]), last, c < 2)
            nc.scalar.activation(
                minus_second[:, chunks[c]], second(last, c, (5, 1)[c % 2])[:], ACT.Identity, bias=bias_sb[:, last : last + 1], scale=-1.0
            )

        copy_out(0)
        copy_out(1)
        lent_relu(1)
        lent_sum(1)
        weigh_picked(2)
        pick(1)
        put(0, weighted0[2][:], MIDDLE, S)
        store(0)
        weighted1 = tile([P, S - LEAD], F32, "weighted1", tag="w1_raw0")
        nc.gpsimd.tensor_tensor(weighted1[:], picked[1][:, LEAD:], wgo_sb[:, LEAD:], ALU.mult)

        def turn(c):
            gap = psum.tile([P, BANK], F32, name="gap", tag="bank%d" % (3, 4)[c % 2])
            for j in range(0, BANK, P):
                cols = slice(c * BANK + j, c * BANK + j + P)
                nc.tensor.matmul(gap[:, j : j + P], first_score[:, cols], ident[:], start=True, stop=False, is_transpose=True)
                nc.tensor.matmul(gap[:, j : j + P], minus_second[:, cols], ident[:], start=False, stop=True, is_transpose=True)
            nc.scalar.activation(turned[:, chunks[c]], gap[:], ACT.Relu, scale=-1.0)

        def turn_back(c):
            back = psum.tile([P, BANK], F32, name="back", tag="bank%d" % (6, 7)[c % 2])
            for j in range(0, BANK, P):
                nc.tensor.transpose(back[:, j : j + P], turned[:, c * BANK + j : c * BANK + j + P], ident[:])
            nc.scalar.copy(returned[c], back[:])
            if c:
                cols = chunks[c] if c > 1 else slice(0, 2 * BANK)
                nc.gpsimd.tensor_tensor(score[last][:, cols], first_score[:, cols], excess[c - 1][:], ALU.add)

        for step in range(CHUNKS + 2):
            for stage, c in ((turn_back, step - 2), (turn, step - 1), (copy_out, step)):
                if (2 if stage == copy_out else 0) <= c < CHUNKS:
                    stage(c)
        put(1, weighted1[:], LEAD, S)
        pick(last)
        rest = tile([P, LEAD], F32, "rest", tag="wgs2")
        nc.gpsimd.tensor_tensor(rest[:], picked[1][:, :LEAD], wgo_sb[:, :LEAD], ALU.mult)
        put(1, rest[:], 0, LEAD)
        store(1)

        nc.vector.tensor_tensor(budget[last][:].indirect(idx4[:]), picked[last], wgo_sb[:], ALU.mult)
        for queue, cols in zip((nc.sync, nc.scalar), (slice(0, T2 // 2), slice(T2 // 2, T2))):
            queue.dma_start(out[last * P :, cols], budget[last][:, cols])
